import numpy as np, ml_dtypes
CORES = [1,5,17,21,33,37,49,53]
N = 8
BF = ml_dtypes.bfloat16
def gentries(a):
    return np.ascontiguousarray(a.reshape(8, 16, -1).transpose(0, 2, 1)).reshape(8, -1)
def gtable(e):
    e = np.asarray(e); return np.ascontiguousarray(e.reshape(8, -1, 16).transpose(0, 2, 1)).reshape(128, -1).astype(np.int32)
S, M, NA, RO = 128, 1024, 2048, 4
W0 = M + (N - 1) * S; W = W0 + RO * S
def parts(rng):
    amp = rng.choice(np.array([255, 160, 96]), (1, 8, 1, 1))
    y = (rng.random((N, 8, 16, W0)) * (amp + 1)).astype(np.int64)
    l = rng.integers(0, W0, (N, 8, 16, NA)); c = rng.integers(0, NA, (N, 8, 16, M))
    f = np.where(rng.random((N, 8, W0)) < 0.3, rng.integers(0, W0, (N, 8, W0)), np.arange(W0))
    th = (amp[..., 0] * (4.6 + 2.2 * rng.random((N, 8, S)))).astype(np.int64)
    return y, l, c, f, th
def pack(y, l, c, f, th):
    return {"y0": np.ascontiguousarray(y.reshape(N, 128, W0)).astype(np.float32).astype(BF), "lk": np.ascontiguousarray(l.reshape(N, 128, NA)).astype(np.int32),
            "cl": np.ascontiguousarray(c.reshape(N, 128, M)).astype(np.int32), "fw0": np.stack([gtable(z) for z in f]), "th": np.ascontiguousarray(th).astype(np.int32)}
def uneven(rng, hi, *shape):
    z = rng.random(shape) ** 3; side = rng.random(shape[:2] + (1,) * (len(shape) - 2)) < 0.5
    return np.minimum((hi * np.where(side, z, 1 - z)).astype(np.int64), hi - 1)
def far(y, l, c, f):
    r4 = np.arange(N)[:, None, None, None]; g4 = np.arange(8)[None, :, None, None]; k4 = np.arange(16)[None, None, :, None]
    a = c[..., :S]; b = f[r4, g4, l[r4, g4, k4, a]].reshape(N, 8, 1, 16 * S); e = f[r4, g4, l[r4, g4, (k4 + 5) % 16, a]].reshape(N, 8, 1, 16 * S)
    z = ((np.take_along_axis(y, b, 3) + np.take_along_axis(y, e, 3)) >> 1).reshape(N, 8, 16, 16, S)
    return np.max(np.add.reduce(np.abs(z - y[..., :S][:, :, :, None, :]), axis=2), axis=2)
def setup_inputs(rng):
    return pack(*parts(rng))
def setup_inputs_spread(rng):
    y, l, c, f, th = parts(rng)
    y = np.minimum((np.exp2(8 * rng.random((N, 8, 1, W0))) * rng.random((N, 8, 16, W0))).astype(np.int64), 255)
    l = uneven(rng, W0, N, 8, 16, NA); c = uneven(rng, NA, N, 8, 16, M)
    f = np.where(rng.random((N, 8, W0)) < 0.5, uneven(rng, W0, N, 8, W0), f)
    th = np.minimum((4081 * rng.random((N, 8, S)) ** 3).astype(np.int64), 4080)
    return pack(y, l, c, f, th)
def setup_inputs_ends(rng):
    y, l, c, f, th = parts(rng)
    y = np.where(rng.random((N, 8, 1, W0)) < 0.6, 255 * rng.integers(0, 2, (N, 8, 1, W0)), 255 * rng.integers(0, 2, (N, 8, 16, W0)))
    y[..., 0] = 0; y[..., W0 - 1] = 255; y[..., S - 1] = 0
    l = np.where(rng.random(l.shape) < 0.72, (W0 - 1) * rng.integers(0, 2, l.shape), l)
    c = np.where(rng.random(c.shape) < 0.72, (NA - 1) * rng.integers(0, 2, c.shape), c)
    f = np.where(rng.random(f.shape) < 0.7, (W0 - 1) * rng.integers(0, 2, f.shape), rng.integers(0, W0, f.shape))
    f[..., 0] = 0; f[..., W0 - 1] = W0 - 1
    l[:, 1::2, :, 0] = 0; l[:, 1::2, :, NA - 1] = W0 - 1
    c[:, :, 0, S - 1] = 0; c[:, :, 14, S - 1] = 0; c[:, :, 2, S - 1] = NA - 1; c[:, :, 15, S - 1] = NA - 1
    th = 4080 * rng.integers(0, 2, (N, 8, S))
    near = np.maximum(far(y, l, c, f) - rng.choice(np.array([0, 0, 1, 1, 1, 2, 9, 15, 16]), th.shape), 0)
    th = np.where(rng.random(th.shape) < 0.28, near, th)
    th[..., S - 1] = 0; th[:, 1::4, S - 1] = 4079
    th[np.arange(N), 2 * rng.integers(0, 4, N)] = 4080
    return pack(y, l, c, f, th)
def setup_inputs_corners(rng):
    y, l, c, f, th = parts(rng); x = np.arange(W0)
    th = np.where(rng.random(th.shape) < 0.25, 4080 * rng.integers(0, 2, th.shape), th)
    for r in range(N):
        o = rng.permutation(8)
        for g in range(8):
            f[r, g] = (x, np.maximum(x - 1, 0), (x + 1) % W0, x ^ 1, x * 0, x * 0 + W0 - 1, rng.choice(np.array([0, M - 1, M, W0 - 1]), W0), W0 - 1 - x)[int(o[g])]
            j = int(rng.integers(0, 6)); h = int(rng.integers(0, 6))
            if o[g] == 0: j = 5; h = 1; th[r, g] = 0
            if o[g] == 2: th[r, g] = 4080
            if j == 0: l[r, g] = np.arange(NA) % M
            if j == 1: l[r, g] = rng.choice(np.array([0, M - 1, M, W0 - 1]), (16, NA))
            if j == 2: l[r, g] = rng.integers(M, W0, (16, NA))
            if j == 3: l[r, g] = rng.integers(0, M, (16, NA))
            if j == 4: l[r, g, 1::2] = W0 - 1
            if h == 0: c[r, g] = c[r, g, :1]
            if h == 1: c[r, g] = np.arange(M) % NA
            if h == 2: c[r, g] = rng.choice(np.array([0, NA - 1]), (16, M))
            if h == 3: c[r, g] = (np.arange(M)[None, :] * 7 + np.arange(16)[:, None]) % NA
    return pack(y, l, c, f, th)
def setup_inputs_crowd(rng):
    y, l, c, f, th = parts(rng); y = rng.integers(0, 8, y.shape); th = rng.integers(25, 60, th.shape); i = np.arange(S)
    for r in range(N):
        for g in range(8):
            m = (1, 1, 2, 2, 16, 16, 1, 1)[g]; o = rng.permutation(NA); a = o[:m]
            x = int(rng.integers(M - S, M)) if g % 4 < 2 else int(rng.integers(M, W0))
            if r == N - 1 and g > 5: x = W0 - 1
            y[r, g, :, x] = 255; f[r, g, x] = x; l[r, g][:, a] = x
            c[r, g][rng.integers(0, 16, S), i] = a[i % m]
            if g in (1, 3, 4, 6):
                e = int(rng.integers(0, S)); f[r, g, e] = e; l[r, g, :, o[m]] = e; c[r, g, :, e] = o[m]
    return pack(y, l, c, f, th)
def setup_inputs_ties(rng):
    y, l, c, f, th = parts(rng)
    step = rng.choice(np.array([1, 3]), (1, 8, 1)); low = np.array([0, 127, 200, 252, 0, 127, 200, 252])[rng.permutation(8)].reshape(1, 8, 1)
    o = rng.permutation(8); step[0, o[:2]] = 1
    y = low[..., None] + step[..., None] * rng.integers(0, 2, y.shape)
    th = step * rng.integers(0, 11, th.shape)
    for g in o[:2]:
        y[:, g, 0] = low[0, g, 0]; th[:, g] = 0
        for r in range(N):
            e = int(rng.integers(0, S)); b = int(rng.integers(0, NA))
            f[r, g, e] = e; l[r, g, :, b] = e; c[r, g, :, e] = b
    B = NA // RO
    for r in range(N):
        for j in (2, 3):
            g = int(o[j]); e = int(rng.integers(0, S)); h = int(rng.integers(0, 16)); x = int(rng.integers(40, 175)); d = int(rng.integers(4, 41))
            s = np.array([x, x, x + d, x - d, x + 2 * d]) if j == 2 else np.array([x, x + 1, x + 1 + d, x + 1, x + 1 + d])
            y[r, g, :, :RO * S] = rng.integers(0, 256, (16, 1)); y[r, g, h, :RO * S] = np.repeat(s[:RO], S); y[r, g, h, (RO - 1) * S + e] = s[RO]
            f[r, g, :RO * S] = np.arange(RO * S)
            for t in range(RO):
                c[r, g, :, t * S:(t + 1) * S] = rng.integers(t * B, (t + 1) * B, (16, S))
                l[r, g, :, t * B:(t + 1) * B] = (t + 1) * S + (e + rng.integers(1, S, (16, B))) % S if t < RO - 1 else t * S + e
            if j == 2: th[r, g] = (1 + r % (RO - 1)) * d - 1
            else:
                k = 1 + r % 3; th[r, g] = d - rng.integers(1, k + 1, S); th[r, g, rng.permutation(S)[:k]] = 0
    w = far(y, l, c, f); th[:, o[4:6]] = w[:, o[4:6]]; g = int(o[5])
    for r in range(N): th[r, g, np.argsort(-w[r, g])[:1 + r % 3]] -= 1
    return pack(y, l, c, f, np.maximum(th, 0))
def check_inputs(d):
    bad = []
    for k, lo, hi in (("y0", 0, 255), ("lk", 0, W0 - 1), ("cl", 0, NA - 1), ("fw0", 0, W0 - 1), ("th", 0, 4080)):
        z = np.asarray(d[k]).astype(np.float64)
        if not np.all((z >= lo) & (z <= hi)): bad.append("range of " + k)
        elif not np.all(z == np.floor(z)): bad.append("whole numbers in " + k)
    return bad
def at(z, k):
    return np.take_along_axis(z, k[:, :, None, :], 2)[:, :, 0]
def reference(y0, lk, cl, fw0, th):
    Y = np.zeros((N, 8, 16, W), np.int64); Y[..., :W0] = y0.astype(np.float32).astype(np.int64).reshape(N, 8, 16, W0)
    L = lk.astype(np.int64).reshape(N, 8, 16, NA)
    C = np.zeros((N, 8, 16, W), np.int64); C[..., :M] = cl.astype(np.int64).reshape(N, 8, 16, M)
    F = np.tile(np.arange(W), (N, 8, 1)); F[:, :, :W0] = np.stack([gentries(z) for z in fw0])
    lane = np.arange(S); v = np.tile(lane, (N, 8, 1)); A = np.zeros((N, 8), np.int64); lim = th.astype(np.int64).reshape(N, 8, S)
    rk = np.arange(N)[:, None, None]; gr = np.arange(8)[None, :, None]; row = np.arange(16)[None, None, :, None]
    rk4 = rk[..., None]; gr4 = gr[..., None]
    for t in range(RO):
        a = np.take_along_axis(C, v[:, :, None, :], 3)
        b = np.take_along_axis(L, a, 3); c = L[rk4, gr4, (row + 5) % 16, a]
        fb = F[rk4, gr4, b].reshape(N, 8, 1, 16 * S); fc = F[rk4, gr4, c].reshape(N, 8, 1, 16 * S)
        y = ((np.take_along_axis(Y, fb, 3) + np.take_along_axis(Y, fc, 3)) >> 1).reshape(N, 8, 16, 16, S)
        own = np.take_along_axis(Y, v[:, :, None, :], 3)
        D = np.add.reduce(np.abs(y - own[:, :, :, None, :]), axis=2)
        p = np.argmax(D, axis=2); q = np.argmin(D, axis=2)
        big = at(D, p) > lim + (A % 16)[:, :, None]
        ap = at(a, p); bp = at(b, p); bq = at(b, q)
        yp = np.take_along_axis(y, p[:, :, None, None, :], 3)[:, :, :, 0]; yq = np.take_along_axis(y, q[:, :, None, None, :], 3)[:, :, :, 0]
        n = W0 + t * S + lane; new = own + np.sign(yq - own); u = np.add.reduce(own, axis=2)
        Y[..., W0 + t * S:W0 + (t + 1) * S] = yp
        C[..., W0 + t * S:W0 + (t + 1) * S] = a
        C[rk, gr, p, v] = (ap + u + t + 1) % NA
        Y[rk4, gr4, row, v[:, :, None, :]] = new
        for r in range(N):
            for s in range(N - 1): Y[r, :, :, M + s * S:M + (s + 1) * S] = new[(r + 1 + s) % N]
        for i in range(S - 1, -1, -1):
            i0, i1 = np.nonzero(big[:, :, i])
            L[i0, i1, 1::2, ap[i0, i1, i]] = n[i]
        F[rk, gr, v] = np.where(big, F[rk, gr, v], F[rk, gr, bq])
        F = np.take_along_axis(F, F, 2)
        w = F[rk, gr, bp]
        v = np.where((w < M) | (w >= W0), w - w % S + lane, np.where(big, n, (v + S) % M))
        A = np.add.reduce(big.astype(np.int64), axis=2)
    return {"yo": Y.reshape(N, 128, W).astype(np.float32).astype(BF), "lo": L.reshape(N, 128, NA).astype(np.float32), "fo": np.stack([gtable(z) for z in F]).astype(np.float32)}

@@ -1,0 +1,829 @@
+import numpy as np
+from concourse.bass import DstId, RemoteDMATransfer
+from concourse.mybir import AluOpType, ActivationFunctionType
+
+OP = AluOpType
+AF = ActivationFunctionType
+N, S, RO = 8, 128, 4
+W0, WA, WD = 1920, 2432, 2560
+GA, RM, BS, GB, YW = 0, 896, 1408, 2432, 3328
+OFF = 1216
+BIG = 1.0e6
+PK = 8192.0
+
+
+def sb(n, d):
+    return ("sbuf", [128, n], d)
+
+
+SCRATCH = {
+    "Y": sb(YW, "bfloat16"), "YF": sb(WA, "bfloat16"), "F0": sb(WD, "bfloat16"), "F1": sb(WD, "bfloat16"),
+    "FI": sb(WD, "bfloat16"), "Li": sb(2048, "int32"), "L": sb(2064, "float32"), "Ci": sb(1024, "int32"),
+    "C": sb(1536, "float32"), "fwi": sb(120, "int32"), "fwf": sb(160, "float32"), "thi": sb(128, "int32"),
+    "thf": sb(128, "float32"), "th16": sb(128, "float32"),
+    "DD": sb(4096, "bfloat16"), "J": sb(144, "float32"), "JG": sb(128, "float32"),
+    "pi": sb(8, "int32"), "pf": sb(8, "float32"), "RH": sb(16, "float32"), "col": sb(40, "float32"),
+    "Id": sb(128, "bfloat16"), "Idf": sb(128, "float32"), "R5": sb(128, "bfloat16"), "Go": sb(128, "bfloat16"), "Gb": sb(128, "bfloat16"),
+    "G1r": sb(128, "bfloat16"), "Gn": sb(128, "bfloat16"), "Gv": sb(128, "bfloat16"), "Jb": sb(128, "bfloat16"),
+    "m16": sb(128, "bfloat16"), "nId": sb(128, "bfloat16"), "one": sb(512, "bfloat16"), "onf": sb(128, "float32"),
+    "Bw": sb(5 * 144, "bfloat16"), "E32": sb(512, "bfloat16"),
+    "MS": sb(512, "float32"), "T16": sb(128, "float32"), "ks": sb(16, "bfloat16"), "tie": sb(256, "float32"),
+    "rs": sb(256, "float32"), "keep": sb(128, "float32"), "tri": sb(128, "bfloat16"), "trt": sb(128, "float32"), "pick": sb(128, "float32"),
+    "cw": sb(64, "float16"), "lw": sb(8, "bfloat16"), "lwf": sb(8, "float32"), "xi": sb(32, "int32"), "xl": sb(32, "uint16"),
+    "t1": sb(160, "bfloat16"), "t2": sb(160, "float32"), "t3": sb(160, "float32"), "t4": sb(160, "float32"), "t5": sb(160, "float32"),
+    "Fl": sb(160, "uint16"), "Yl": sb(160, "uint16"), "vl": sb(8, "uint16"), "al": sb(128, "uint16"),
+    "G": sb(2048, "float16"), "bc": sb(256, "uint16"),
+    "pay": sb(768, "float32"), "Z1": sb(512, "float16"), "Z2": sb(512, "float16"),
+    "A": sb(2048, "float32"), "B": sb(2048, "float16"), "ab": sb(2048, "bfloat16"),
+    "own": sb(128, "bfloat16"), "oT": sb(128, "bfloat16"),
+    "key": sb(384, "float32"), "mx": sb(256, "float32"), "OH": sb(384, "bfloat16"),
+    "l1": sb(24, "uint16"), "l2": sb(24, "uint16"), "fq": sb(128, "bfloat16"),
+    "x1": sb(128, "bfloat16"), "x1l": sb(8, "uint16"), "x2": sb(128, "bfloat16"), "sx": sb(128, "float32"), "sv2": sb(128, "float32"),
+    "A2": sb(256, "float32"), "B2": sb(128, "float16"), "B3": sb(128, "float16"), "n1": sb(128, "bfloat16"), "new": sb(512, "bfloat16"),
+    "cn": sb(128, "float32"), "f1": sb(128, "bfloat16"), "f2": sb(128, "bfloat16"), "f3": sb(128, "bfloat16"),
+    "aw": sb(8, "float32"), "ar": sb(128, "float32"), "eq": sb(128, "float32"), "kl": sb(128, "float32"), "kt": sb(8, "float32"),
+    "sl": sb(16, "uint16"), "lv": sb(128, "float32"), "nod": sb(512, "float32"), "fof": sb(152, "float32"),
+}
+for k_ in range(8):
+    SCRATCH["P%d" % k_] = ("psum", [128, 512], "float32")
+NDMA = 16
+SEMAPHORES = ["sv", "sa", "sp", "sg", "sent"] + ["arr%d" % t for t in range(RO)] + ["d%d" % k for k in range(NDMA)]
+DSZ = {"bfloat16": 2, "float16": 2, "uint16": 2, "float32": 4, "int32": 4}
+
+TM = {"CY": 1.0, "GAT": 1.56, "SCA": 3.8, "FIX": 60.0, "PCY": 0.55, "PFIX": 0.0, "HOP": 110.0, "HOPS": 70.0, "BW": 200.0, "ARR": 3000.0,
+      "SCAN": 0, "C1": 512, "DS": ((0, 64), (64, 96), (96, 128)), "IT": 4000, "SEED": 1, "LEAN": 300.0,
+      "WIN": (1500, 3000, 8000), "AMP": (100, 300, 800), "FLIP": (0.0, 0.03, 0.1), "BOTH": 0.5, "HEAT": 40.0, "AIM": 0.9, "ITA": 0, "HEATA": 150.0}
+VARIANTS = [{"PCY": 0.45, "GAT": 1.2, "SCA": 2.5, "BW": 350.0}, {"PCY": 0.9, "GAT": 1.9, "SCA": 5.0, "ARR": 4500.0}]
+
+
+LETTERS = "abcdefghijklmnopqrstuvwxyzABCDEFGHIJKLMNOPQRSTUVWXYZ"
+START = "aiaaacamakdQbOaeeYagaoaqasauaEaObcbybKbWceckcqcAcQdadgdodydIdUeacucycMcYbYcoayaAaCawaIaGbsbCdcaWaMbebMbgbuaUbEbabJchbGbqbAcbcdbxbkbVbocwcIdCcmcUdPhohufihCcEfehihIfchYcGcOcCcKdYemeMicieikbQhMighAhWhqhQdqdidwaQbSdmcWdGdKcsekfEdkaSdebmhEeceQbidAdNeieqeseUeWciaKaYdWeoeweCeEeGeOfufQfkgegOgUhahcgnhwhSiyiqiiiwcSdudsdEeeeSeufCfyfwdSegeyeKeIeAfgfqfafGjAjugSgMjggIiIgAjWkmjKjQhOfmfpfAfKfSfsfMfUfYfOfWgcgsgogugCgKgggqgwgyfIgEgbglgWhghmhsgigGgQgYhehkhyhGhKiahUioimiCiEiMisiAiGiSiYjejmjCjqiKiUjcjwiWjskakejEjSkqjijIiuiOiQjajojGjYjMkckikokukwkAkIkOkUkkkykEkGkCjkjykgjUjOkMlilqkskSkYlykKkQlelclklalmkWlglwlolulslAlKlClSlPlJlFlUmcmglGmemqmwlYmomAmIlWmamimkmzmGmMmSlMlQmLmPmmmsmumCmQmXnanmnqninonwnCncnsmEmUmYnengnknunAnynGnEnKnInUnOoanMnSnYoeokoqowoUoyogosoCoIouoEoWpaoQpcpmomoKpopEnQnWocoioooGoMoAoSoYpepkpqpwpApCpgpspypUpQoOpGpMpipupSqiqxqqpKpYqkqeqoqAqGqQqMqSrcpIpOqmqcqgqaqsquqyqIpWqEqDqOqYreqKqWrirIrmrErMrUqUrgrqrCrarkrurGrQrWrxrBrortryrOsgsksosqsysisssAsGsasurSrYrKscsesmswsEsCsKsIsOsMsYsStcsQsUtatgtmtstytQtItitAtGtOtwtKucuktYumustqtWuguysWtetltotutEtMtCtSuaueuiuquwuAuGuuuEuIwJuOuKtUuCuUuouQuYvovgvevqvtvwuWvavQvUvKvWvIuMuSvcvkvivmvAvuvyvOvEvHvSwcwqvMwawkwGwgwswEwMvYwmwuwAwewiwowwvDwWwDwUwywQwYxgxkxmxcxowOwSwKxaxexixqxsxuxwxyxCxAxMxGxWxFxIxOxUyayeymyCzaxYzgzmzoyqyMygyExKydxSykyoysywxRyyyAyGyKyOyQyUyYzczizszuyuyiyIySzeyWzlzqzxzy"
+
+
+def R(name, a, b, step=1, p0=0, p1=128, ps=1):
+    return ("r", name, a, b, step, p0, p1, ps)
+
+
+def IND(win, off):
+    return ("i", win, off)
+
+
+def cnt(x):
+    if x[0] == "i":
+        return 16 * cnt(x[2])
+    return (x[3] - x[2] + x[4] - 1) // x[4]
+
+
+def isap(x):
+    return isinstance(x, tuple)
+
+
+def ap(T, x):
+    if not isap(x):
+        return x
+    if x[0] == "i":
+        return ap(T, x[1]).indirect(ap(T, x[2]))
+    cs = slice(x[2], x[3]) if x[4] == 1 else slice(x[2], x[3], x[4])
+    ps = slice(x[5], x[6]) if x[7] == 1 else slice(x[5], x[6], x[7])
+    return T[x[1]][ps, cs]
+
+
+def regs(x):
+    if x[0] == "i":
+        return [x[1], x[2]]
+    return [x]
+
+
+def narrow(*xs):
+    return all(DSZ[SCRATCH[x[1]][2]] == 2 for x in xs if isap(x))
+
+
+def build():
+    ops = []
+    rnd = [-1]
+    CY, GAT, SCA, FIX, PCY, PFIX = TM["CY"], TM["GAT"], TM["SCA"], TM["FIX"], TM["PCY"], TM["PFIX"]
+
+    def add(eng, calls, rd, wr, dur, kind="c", lat=0.0, name=""):
+        r2 = []
+        w2 = []
+        for x in rd:
+            if isap(x):
+                r2 += regs(x)
+        for x in wr:
+            if x[0] == "i":
+                w2.append(x[1])
+                r2.append(x[2])
+            else:
+                w2.append(x)
+        ops.append({"eng": eng, "calls": calls, "rd": r2, "wr": w2, "dur": dur, "kind": kind, "lat": lat, "name": name, "t": rnd[0]})
+
+    def vdur(out, a, per):
+        if a[0] == "i":
+            return FIX + cnt(a) * GAT * CY
+        if out[0] == "i":
+            return FIX + cnt(out) * SCA * CY
+        return FIX + max(64, cnt(a) * per) * CY
+
+    def cp(out, a, name=""):
+        add("v", [("tensor_copy", (out, a), {})], [a], [out], vdur(out, a, 0.5 if a[0] == "r" and out[0] == "r" and narrow(a, out) else 1), name=name)
+
+    def tt(out, a, b, op, name=""):
+        per = 1 if (a[0] == "r" and a[1][0] == "P") or b[1][0] == "P" else 2
+        add("v", [("tensor_tensor", (out, a, b, op), {})], [a, b], [out], vdur(out, a, per), name=name)
+
+    def ts(out, a, s1, o1, s2=None, o2=None, name=""):
+        args = (out, a, s1, None, o1) if o2 is None else (out, a, s1, s2, o1, o2)
+        add("v", [("tensor_scalar", args, {})], [a, s1, s2], [out], vdur(out, a, 0.5 if a[0] == "r" and narrow(a, out) else 1), name=name)
+
+    def scan(out, d0, d1, o0, o1, name=""):
+        add("v", [("tensor_tensor_scan", (out, d0, d1, 0.0, o0, o1), {})], [d0, d1], [out], vdur(out, d0, 1), name=name)
+
+    def ms(out, val):
+        add("v", [("memset", (out, val), {})], [], [out], vdur(out, out, 0.5 if narrow(out) else 1), name="ms")
+
+    def act(out, a, f=AF.Identity, bias=0.0, scale=1.0, name=""):
+        add("a", [("activation", (out, a, f), {"bias": bias, "scale": scale})], [a, bias, scale], [out], vdur(out, a, 1), name=name)
+        if f in (AF.Copy, AF.Identity):
+            if scale == 0.0 and not isap(bias):
+                c = ("memset", (out, bias), {})
+            elif scale == 1.0 and bias == 0.0:
+                c = ("tensor_copy", (out, a), {})
+            else:
+                c = ("tensor_scalar", (out, a, scale, bias, OP.mult, OP.add), {})
+            ops[-1]["alt"] = ([c], vdur(out, a, 0.5 if a[0] == "r" and narrow(a, out) else 1))
+
+    def mm(items, name=""):
+        calls = []
+        rd = []
+        wr = []
+        dur = 0.0
+        for (o, l, r, st, sp) in items:
+            calls.append(("matmul", (o, l, r, st, sp), {}))
+            rd += [l, r]
+            wr.append(o)
+            dur += PFIX + max(min(64, cnt(l)), cnt(r)) * PCY * (4 if SCRATCH[l[1]][2] == "float32" else 1)
+        add("p", calls, rd, wr, dur + 60, name=name)
+
+    def acc(out, pairs, name=""):
+        mm([(out, l, r, j == 0, j == len(pairs) - 1) for j, (l, r) in enumerate(pairs)], name)
+
+    def iota(out, pat, base, cm):
+        kw = {} if SCRATCH[out[1]][2] == "int32" else {"allow_small_or_imprecise_dtypes": True}
+        add("g", [("iota", (out, pat, base, cm), kw)], [], [out, R("@g", 0, 1)], 130 + 2 * cnt(out) * CY, name="io")
+
+    def sel(out, a, pat, op, fill, base, cm):
+        add("g", [("affine_select", (out, a, pat, op, fill, base, cm), {})], [a], [out, R("@g", 0, 1)], 170 + 2 * cnt(out) * CY, name="sel")
+
+    def dma(q, out, a, nbytes, name="", after=()):
+        add(q, [("dma_start", (out, a), {})], ([a] if a[1] in SCRATCH else []) + list(after), [out] if out[1] in SCRATCH else [], 60, kind="d",
+            lat=2000 + nbytes / TM["BW"], name=name)
+
+    def col(k):
+        return R("col", k, k + 1)
+
+    def rh(k):
+        return R("RH", k, k + 1)
+
+    def X(name):
+        return R(name, 0, 128)
+    Id, one = X("Id"), X("one")
+
+    def wstage(out, w, src, a, b, first=None, name=""):
+        it = [] if first is None else [(Id, first)]
+        for r in range(16):
+            it.append((R("Bw", 144 * w + 15 - r, 144 * w + 143 - r), R(src, a + r, b, 16)))
+        acc(out, it, name)
+
+    dma("s", R("Ci", 0, 128), R("cl", 0, 128), 65536, "ld_c0")
+    dma("a", R("fwi", 0, 120), R("fw0", 0, 120), 61440, "ld_f")
+    dma("s", R("Li", 0, 2048), R("lk", 0, 2048), 1600000, "ld_l")
+    dma("a", R("Y", BS, YW), R("y0", 0, W0), 1000000, "ld_y")
+    dma("a", R("thi", 0, 128, 1, 0, 8), R("th", 0, 128, 1, 0, 8), 4096, "ld_t")
+    dma("s", R("Ci", 128, 1024), R("cl", 128, 1024), 460000, "ld_c", [R("Li", 0, 2048)])
+    ms(R("one", 0, 512), 1.0)
+    ms(R("DD", 0, 4096), 0.0)
+    ms(R("Y", RM, BS), 0.0)
+    iota(R("pi", 0, 1), [[0, 1]], 0, 1)
+    iota(R("pi", 6, 7), [[0, 1]], 11, 1)
+    iota(R("J", 0, 144), [[1, 144]], 0, 0)
+    iota(X("JG"), [[1, 8], [0, 16]], 0, 0)
+    iota(R("E32", 0, 512), [[1, 32], [0, 16]], 0, 0)
+    iota(X("onf"), [[0, 128]], 1, 0)
+    iota(X("trt"), [[0, 8], [1, 16]], 0, 0)
+    iota(R("tie", 0, 256), [[0, 16], [-1, 16]], 15, 0)
+    iota(X("Jb"), [[1, 128]], 0, 0)
+    iota(X("m16"), [[0, 128]], -16, 0)
+    iota(R("xi", 0, 16), [[16, 16]], 15, 0)
+    iota(R("xi", 16, 24), [[16, 8]], 15, 0)
+    iota(R("xi", 24, 32), [[1, 8]], 0, 0)
+    iota(R("rs", 0, 256), [[0, 256]], 0, 0)
+    sel(R("rs", 0, 256), R("rs", 0, 256), [[0, 16], [1, 16]], OP.is_gt, -BIG, 0, 0)
+    sel(X("keep"), X("onf"), [[0, 8], [1, 16]], OP.is_gt, 0.0, 0, 0)
+    sel(X("Idf"), X("onf"), [[1, 128]], OP.is_equal, 0.0, 0, -1)
+    iota(X("T16"), [[0, 128]], 16, 0)
+    sel(X("T16"), X("T16"), [[1, 8], [0, 16]], OP.is_equal, 0.0, 0, -1)
+    for j in range(4):
+        sel(R("MS", 128 * j, 128 * j + 128), X("onf"), [[32, 4], [1000, 2], [1, 16]], OP.is_equal, 0.0, 16 * (j // 2) - 1000 * (j % 2), -1)
+    for h in range(0, WD, 640):
+        ms(R("FI", h, h + 640), 0.0)
+    act(R("C", 0, 512), R("one", 0, 512), AF.Copy, 0.0, 0.0, "zc")
+    act(R("L", 2048, 2064), R("one", 0, 16), AF.Copy, 0.0, 0.0)
+    ts(R("pi", 1, 2), R("pi", 0, 1), 15, OP.bitwise_and)
+    ts(R("pi", 2, 3), R("pi", 0, 1), 4, OP.arith_shift_right)
+    ts(R("pi", 3, 4), R("pi", 6, 7), 15, OP.bitwise_and)
+    ts(R("pi", 4, 5), R("pi", 0, 1), 1, OP.bitwise_and)
+    ts(R("pi", 7, 8), R("pi", 0, 1), 31, OP.bitwise_and)
+    cp(R("pf", 0, 5), R("pi", 0, 5))
+    cp(R("pf", 7, 8), R("pi", 7, 8))
+    ts(R("E32", 0, 512), R("E32", 0, 512), R("pf", 7, 8), OP.is_equal)
+    ts(R("pf", 5, 6), R("pf", 2, 3), 16.0, OP.mult, 15.0, OP.add)
+    ts(R("pf", 6, 7), R("pf", 2, 3), 16.0, OP.mult, R("pf", 3, 4), OP.add)
+    pP, pR, pG, p5, pO, pW = [R("pf", k, k + 1) for k in (0, 1, 2, 6, 4, 5)]
+    ts(Id, X("J"), pP, OP.is_equal)
+    ts(X("R5"), X("J"), p5, OP.is_equal)
+    act(X("nId"), Id, AF.Copy, 0.0, -1.0)
+    for j, m in enumerate(("Id", "R5")):
+        for h in range(8):
+            act(R("DD", 2048 * j + 256 * h, 2048 * j + 256 * h + 256, 17), R(m, 16 * h, 16 * h + 16), AF.Copy, name="DD")
+    ts(R("RH", 0, 16), R("J", 0, 16), pR, OP.is_equal)
+    ts(X("Go"), X("JG"), pG, OP.is_equal)
+    ts(R("Bw", 0, 144), R("J", 0, 144), pW, OP.is_equal)
+    ts(R("ks", 0, 8), R("J", 0, 8), pG, OP.is_equal, 16.0, OP.mult)
+    ts(R("ks", 8, 16), R("J", 0, 8), pG, OP.is_equal, -16.0, OP.mult)
+    act(col(0), rh(1), AF.Identity, rh(0), 128.0)
+    act(col(1), rh(3), AF.Identity, col(0), -2432.0)
+    act(col(2), rh(2), AF.Identity, col(1), -2432.0)
+    act(col(3), rh(2), AF.Identity, rh(4), 1.0)
+    act(col(4), rh(6), AF.Identity, col(3), 1.0)
+    act(col(5), rh(3), AF.Identity, rh(7), 1.0)
+    act(col(6), rh(5), AF.Identity, col(5), -1.0)
+    act(col(7), col(6), AF.Copy, 0.0, -2432.0)
+    act(col(8), col(4), AF.Identity, col(7), 128.0)
+    act(col(9), rh(1), AF.Copy, 0.0, -32.0)
+    act(col(10), rh(0), AF.Copy, 0.0, 128.0)
+    act(col(11), rh(1), AF.Copy, 0.0, 128.0)
+    act(col(12), rh(0), AF.Identity, col(11), -2560.0)
+    act(col(13), rh(4), AF.Identity, rh(5), 1.0)
+    act(col(14), col(5), AF.Identity, col(13), 1.0)
+    act(col(15), rh(2), AF.Identity, rh(6), -1.0)
+    act(col(16), col(15), AF.Identity, col(14), 15.0)
+    act(col(22), rh(2), AF.Identity, col(16), 1.0)
+    act(col(19), rh(2), AF.Identity, col(14), 1537.0)
+    for t in (1, 2):
+        act(col(16 + t), col(15), AF.Identity, col(19), 15.0 + t)
+    act(col(21), pR, AF.Identity, 2048.0, 1.0)
+    for w, c in ((1, 0), (2, 1), (3, 2)):
+        act(R("Bw", 144 * w, 144 * w + 144), R("Bw", 0, 144), AF.Identity, 0.0, col(c))
+    act(X("Gb"), X("Go"), AF.Identity, 0.0, col(4))
+    act(X("G1r"), X("Go"), AF.Identity, 0.0, col(9))
+    if TM["SCAN"]:
+        act(X("Gn"), X("Go"), AF.Identity, 0.0, col(0))
+        act(X("Gv"), X("Go"), AF.Identity, 0.0, col(8))
+        act(col(23), rh(15), AF.Identity, -PK, PK)
+        act(col(24), rh(15), AF.Identity, 512.0 - PK, PK)
+        ts(X("sx"), X("trt"), pR, OP.is_equal, -3 * PK, OP.mult)
+        ts(X("sv2"), X("trt"), -1.0, OP.add, pR, OP.is_equal)
+        act(X("sv2"), X("sv2"), AF.Copy, 0.0, PK)
+        tt(X("pick"), X("sx"), X("sv2"), OP.add)
+    else:
+        act(R("Bw", 144 * 4, 144 * 5), R("Bw", 0, 144), AF.Identity, 0.0, col(8))
+    ts(X("eq"), X("trt"), pR, OP.is_gt, -8192.0, OP.mult)
+    ts(X("kl"), X("trt"), pR, OP.is_equal, 4096.0, OP.mult)
+    tt(X("tri"), X("eq"), X("kl"), OP.add)
+    act(R("lwf", 0, 8), R("J", 0, 8), AF.Identity, pR, 16.0)
+    act(R("lw", 0, 8), R("lwf", 0, 8), AF.Copy)
+    ts(R("vl", 0, 8), R("lwf", 0, 8), 512.0, OP.add)
+    ts(R("cw", 0, 8), R("lwf", 0, 8), float(WA - OFF), OP.add)
+    ts(R("cw", 8, 40), R("J", 0, 32), 0.0, OP.mult)
+    ts(R("cw", 40, 48), R("J", 0, 8), 0.0, OP.mult, -float(OFF), OP.add)
+    cp(R("xl", 0, 32), R("xi", 0, 32))
+    iota(R("nod", 0, 512), [[1, 512]], W0, 0)
+    act(R("nod", 0, 512), R("nod", 0, 512), AF.Identity, 0.0, pO, "nod")
+    ms(R("sl", 0, 16), 0)
+    pAl, pV, pA, pD = R("pay", 0, 128), R("pay", 128, 256), R("pay", 512, 640), R("pay", 640, 768)
+    cp(X("al"), R("Ci", 0, 128), "a0")
+    cp(pA, R("Ci", 0, 128))
+    cp(R("Yl", 0, 120), R("fwi", 0, 120), "yl0")
+    cp(R("Fl", 64, 120), R("fwi", 64, 120))
+    act(pV, one, AF.Identity, col(12), 0.0)
+    act(pAl, one, AF.Identity, col(22), 0.0)
+    cp(R("thf", 0, 128, 1, 0, 8), R("thi", 0, 128, 1, 0, 8))
+    acc(R("P7", 0, 128), [(R("thf", 0, 128, 1, 0, 8), R("T16", 0, 128, 1, 0, 8))])
+    act(X("th16"), R("P7", 0, 128), AF.Identity, 15.0)
+    for k in (3, 4, 6, 7):
+        act(R("th16", k, 128, 16), R("one", 0, 8), AF.Copy, 0.0, BIG)
+    act(R("key", 256, 384), X("th16"), AF.Copy)
+    cp(R("fwf", 0, 120), R("fwi", 0, 120))
+    act(col(25), pR, AF.Identity, float(W0))
+    act(R("fwf", 120, 160), R("J", 0, 40), AF.Identity, col(25), 16.0)
+    for j in range(2):
+        acc(R("P6", j, 160, 2), [(R("MS", 256 * j, 256 * j + 128), R("fwf", 0, 160, 2)), (R("MS", 256 * j + 128, 256 * j + 256), R("fwf", 1, 160, 2))])
+    V = R("t4", 0, 160)
+
+    def fi(k):
+        return R("FI", k, WD, 16)
+    act(V, R("P6", 0, 160), AF.Copy)
+    act(R("t1", 0, 160), V, AF.Identity, 24576.0 - 63.5)
+    act(R("t2", 0, 160), R("t1", 0, 160), AF.Identity, -192.0, 1.0 / 128)
+    act(fi(1), R("t2", 0, 160), AF.Copy)
+    act(R("t3", 0, 160), R("t2", 0, 160), AF.Copy, 0.0, -128.0)
+    tt(fi(0), R("t3", 0, 160), V, OP.add)
+    ts(fi(3), V, float(W0), OP.is_ge)
+    ts(R("t5", 0, 160), V, 1024.0, OP.is_ge)
+    tt(R("t5", 0, 160), R("t5", 0, 160), fi(3), OP.subtract)
+    for k in (2, 5, 6, 7):
+        act(fi(k), R("t5", 0, 160), AF.Copy)
+    act(V, R("t5", 0, 160), AF.Identity, 1.0, -1.0)
+    tt(fi(4), V, R("t2", 0, 160), OP.mult)
+    for h in range(0, WD, 640):
+        add("v", [("transpose", (R("F0", h, h + 640), R("FI", h, h + 640)), {})], [R("FI", h, h + 640)], [R("F0", h, h + 640)], FIX + 320 * CY, name="tr")
+    act(R("F1", W0, WD), R("F0", W0, WD), AF.Copy)
+    for (a, b) in ((0, 960), (960, W0)):
+        act(R("YF", a, b), IND(R("Y", BS, YW), R("Yl", a // 16, b // 16)), AF.Copy, 0.0, 0.5, "YF")
+    act(X("own"), R("Y", BS, BS + 128), AF.Copy)
+
+    for t in range(RO):
+        last = t == RO - 1
+        rnd[0] = t
+        cur, nxt = ("F0", "F1") if t % 2 == 0 else ("F1", "F0")
+        Wt = W0 + S * t
+        Wn = Wt + S
+        Lw = R("Li", 0, 2048) if t == 0 else R("L", 0, 2048)
+        YFw = R("YF", 0, Wt)
+        Fw = R(cur, 0, WD)
+        own = X("own")
+        acc(R("P0", 0, 128), [(own, Id)], "ownT")
+        act(X("oT"), R("P0", 0, 128), AF.Copy, 0.0, -1.0, "oT")
+        pieces = ((0, 512, "P0"), (512, 1024, "P1"), (1024, 1536, "P2"), (1536, 1792, "P3"), (1792, 2048, "P6"))
+        for (a, b, pb) in pieces:
+            q = a // 512
+            mm([(R(pb, 0, b - a), R("oT", 0, 128, 1, 32 * q, 32 * q + 32), R("E32", a % 512, a % 512 + b - a, 1, 32 * q, 32 * q + 32), True, False)], "dA")
+        for a in range(0, 2048, TM["C1"]):
+            ts(R("G", a, a + TM["C1"]), IND(Lw, R("al", a // 16, (a + TM["C1"]) // 16)), -float(OFF), OP.add, name="G1")
+        for h in range(2):
+            pb = "P%d" % (4 + h)
+            for j in range(2):
+                acc(R(pb, 64 * j, 64 * j + 64), [(R("DD", 2048 * j + k, 2048 * j + 2048, 16), R("G", 1024 * h + k, 1024 * h + 1024, 16))
+                                                 for k in range(16)], "ext")
+            ts(R("bc", 128 * h, 128 * h + 128), R(pb, 0, 128), float(OFF), OP.add, name="bc")
+        if t == 0:
+            for h in range(0, 2048, 256):
+                cp(R("L", h, h + 256), R("Li", h, h + 256), "Lcv")
+            for h in range(0, 1024, 256):
+                cp(R("C", 512 + h, 768 + h), R("Ci", h, h + 256), "Ccv")
+        if not last:
+            act(R("C", S * t, S * t + S), pA, AF.Copy, name="Crm")
+        for (a, b, pb) in pieces:
+            o = 64 * (a // 1024)
+            for (c, d) in ((a, b),) if a else ((0, 256), (256, 512)):
+                act(R("A", c, d), IND(YFw, R("bc", o + c // 16, o + d // 16)), AF.Identity, 1023.75, 1.0, "A")
+            tt(R("B", a, b), IND(YFw, R("bc", o + 64 + a // 16, o + 64 + b // 16)), R("A", a, b), OP.add, "B")
+            mm([(R(pb, 0, b - a), Id, R("B", a, b), False, True)], "dB")
+            act(R("ab", a, b), R(pb, 0, b - a), AF.Abs, -1024.0, 1.0, "abs")
+        for h in range(2):
+            pb = "P%d" % (4 + h)
+            act(R("pay", 256 + 64 * h, 320 + 64 * h), R(pb, 0, 64), AF.Copy, name="pay")
+            act(R("pay", 384 + 64 * h, 448 + 64 * h), R(pb, 64, 128), AF.Copy, name="pay")
+        if t > 0:
+            oN = R("OH", 256, 384)
+            acc(R("P0", 0, 128), [(X("m16"), oN)], "cnt")
+            act(X("f3"), R("P0", 0, 128), AF.Identity, -51080.0, -1.0, "thr")
+            acc(R("P0", 128, 256), [(X("m16"), oN), (Id, X("f3")), (X("Idf"), X("th16"))], "cnt")
+            act(R("key", 256, 384), R("P0", 128, 256), AF.Identity, 51200.0, 1.0, "thr")
+            acc(R("P2", 0, 128), [(X("Gb"), X("x2"))], "vb")
+            act(pV, R("P2", 0, 128), AF.Identity, col(12), col(10), "pv")
+            if not last:
+                act(X("f2"), R("P2", 0, 128), AF.Identity, -1533.5, -1.0, "alt")
+                acc(R("P2", 128, 256), [(X("Gb"), X("x2")), (Id, X("f2"))], "alt")
+                act(pAl, R("P2", 128, 256), AF.Identity, col(16 + t), rh(2), "alt")
+        if not last:
+            ut = [(X("Go"), own)] + [(Id, one)] * (t + 1)
+            acc(R("P1", 0, 128), ut + [(X("Idf"), pA)], "u")
+            act(X("f1"), R("P1", 0, 128), AF.Identity, 1023.5 - 393216.0, -1.0, "dC")
+            acc(R("P1", 128, 256), ut + [(Id, X("f1"))], "u")
+            act(pD, R("P1", 128, 256), AF.Identity, 393216.0, 1.0, "dC")
+        if t > 0:
+            wstage(R("P3", 0, 56), 1, cur, 1024, W0, None, "Fg")
+            cp(R("Fl", 64, 120), R("P3", 0, 56), "Fl")
+        for (a, b) in TM["DS"]:
+            mm([(R("P7", k, 256, 16, a, b), R("ab", 16 * a + k, 16 * b, 16), R("ks", 0, 16), True, True) for k in range(16)], "D")
+        tt(R("key", 0, 256), R("P7", 0, 256), R("tie", 0, 256), OP.add, "key")
+        scan(R("mx", 0, 256), R("rs", 0, 256), R("key", 0, 256), OP.add, OP.max, "mx")
+        tt(R("OH", 0, 384), IND(R("mx", 0, 256), R("xl", 0, 24)), R("key", 0, 384), OP.is_le, "OH")
+        oP, oQ, oN = R("OH", 0, 128), R("OH", 128, 256), R("OH", 256, 384)
+        lo = 128 if last else 0
+        hi = 384 if last else 512
+        mm([(R("P5", 128 * j, 128 * j + 128), o, Id, True, True) for j, o in enumerate((oN, oN, oQ, oQ)) if 128 * j >= lo], "T1")
+        mm([(R("P6", 128 * j, 128 * j + 128), oP, Id, True, True) for j in range(hi // 128)], "T2")
+        tt(R("Z1", lo, 512), R("P5", lo, 512), R("pay", lo, 512), OP.mult, "Z1")
+        tt(R("Z2", 0, hi), R("P6", 0, hi), R("pay", 256, 256 + hi), OP.mult, "Z2")
+        wstage(R("P4", 0, 24), 0, "Z1", 128, 512, R("cw", 0, 24), "W1")
+        ts(R("l1", 0, 24), R("P4", 0, 24), float(OFF), OP.add, name="l1")
+        wstage(R("P7", 0, 24), 0, "Z2", 0, 384, R("cw", 24, 48), "W2")
+        ts(R("l2", 0, 24), R("P7", 0, 24), float(OFF), OP.add, name="l2")
+        vs, bq, cq, bp, cP, aP = R("l1", 0, 8), R("l1", 8, 16), R("l1", 16, 24), R("l2", 0, 8), R("l2", 8, 16), R("l2", 16, 24)
+        act(X("fq"), IND(Fw, bq), AF.Copy, name="fq")
+        cp(IND(Fw, vs), X("fq"), "F6")
+        nw = R("new", S * t, S * t + S)
+        act(R("A2", 0, 128), IND(YFw, bq), AF.Identity, 1023.75, 1.0, "A2")
+        tt(X("B2"), IND(YFw, cq), R("A2", 0, 128), OP.add, "B2")
+        acc(R("P0", 0, 128), [(X("nId"), own), (Id, X("B2"))], "dq")
+        act(X("n1"), R("P0", 0, 128), AF.Sign, -1024.0, 1.0, "sg")
+        acc(R("P0", 128, 256), [(Id, own), (Id, X("n1"))], "nw")
+        act(nw, R("P0", 128, 256), AF.Copy, name="new")
+        gh = GA if t % 2 == 0 else GB
+        add("g", [("send", (nw, gh, t), {})], [nw], [R("@%d" % t, 0, 1)], 1000, kind="s", name="send")
+        add("x", [("arr", (t,), {})], [R("@%d" % t, 0, 1)], [R("Y", gh, gh + 896)], 0, kind="x", lat=TM["ARR"], name="arr")
+        cp(IND(R("Y", RM, GB), R("vl", 0, 8)), nw, "Ysc")
+        act(R("A2", 128, 256), IND(YFw, bp), AF.Identity, 1023.75, 1.0, "A3")
+        tt(X("B3"), IND(YFw, cP), R("A2", 128, 256), OP.add, "B3")
+        acc(R("P3", 0, 128), [(Id, X("B3"))], "room")
+        act(R("Y", RM + S * t, RM + S * t + S), R("P3", 0, 128), AF.Identity, -1024.0, 1.0, "room")
+        if not last:
+            act(X("x1"), IND(Fw, bp), AF.Copy, name="x1")
+            if TM["SCAN"]:
+                acc(R("P2", 0, 128), [(X("Gn"), X("x1"))], "Wx")
+                scan(X("sx"), X("pick"), R("P2", 0, 128), OP.add, OP.max, "sx")
+                ts(R("x1l", 0, 8), R("sx", 15, 128, 16), col(23), OP.add, name="x1l")
+            else:
+                wstage(R("P2", 0, 8), 1, "x1", 0, 128, None, "Wx")
+                cp(R("x1l", 0, 8), R("P2", 0, 8), "x1l")
+            tt(X("x2"), IND(Fw, R("x1l", 0, 8)), R("Z1", 0, 128), OP.mult, "x2")
+            acc(R("P3", 128, 256), [(X("Idf"), pA), (Id, R("Z2", 384, 512))], "cn")
+            act(X("cn"), R("P3", 128, 256), AF.Copy, name="cn")
+            cp(IND(R("C", 0, 1536), R("vl", 0, 8)), X("cn"), "Csc")
+        for j, (a, e) in enumerate(((0, 1024), (W0, Wt))):
+            if e > a:
+                wstage(R("P%d" % (5 + j), 0, (e - a) // 16), 1, cur, a, e, None, "Fx")
+                cp(R("Fl", a // 16, e // 16), R("P%d" % (5 + j), 0, (e - a) // 16), "Fl")
+        acc(R("P1", 0, 128), [(Id, X("tri")), (X("G1r"), R("Z1", 128, 256)), (X("Go"), R("Z2", 256, 384))], "ar")
+        act(X("ar"), R("P1", 0, 128), AF.Copy, 0.0, 1.0 / 4096, "ar")
+        act(R("aw", 0, 8), R("P7", 16, 24), AF.Identity, OFF / 4096.0, 1.0 / 4096, "aw")
+        tt(X("eq"), IND(R("aw", 0, 8), R("xl", 24, 32)), X("ar"), OP.is_equal, "eq")
+        scan(X("kl"), X("keep"), X("eq"), OP.mult, OP.max, "kl")
+        tt(R("kt", 0, 8), R("kl", 15, 128, 16), R("aw", 0, 8), OP.add, "kt")
+        ts(R("sl", 0, 16, 2), R("kt", 0, 8), 4096.0, OP.mult, col(21), OP.min, name="sl")
+        act(X("lv"), IND(R("L", 0, 2048), aP), AF.Copy, name="lv")
+        for c in range(7, -1, -1):
+            tt(IND(R("L", 0, 2064), R("sl", 2 * c, 2 * c + 1)), R("lv", 16 * c, 16 * c + 16), R("nod", S * t + 16 * c, S * t + 16 * c + 16), OP.max, "Lsc")
+        if t == 0:
+            dma("s", R("lo", 0, 2048, 1, 0, 128, 2), R("L", 0, 2048, 1, 0, 128, 2), 524288, "st_le")
+        if last:
+            dma("s", R("lo", 0, 2048, 1, 1, 128, 2), R("L", 0, 2048, 1, 1, 128, 2), 524288, "st_lo")
+            dma("s", R("yo", 0, 1024), R("Y", BS, GB), 262144, "st_yb")
+            dma("s", R("yo", W0, WA), R("Y", RM, BS), 131072, "st_yr")
+            dma("s", R("yo", 1024, W0), R("Y", GB, YW), 229376, "st_yg")
+        else:
+            if TM["SCAN"]:
+                acc(R("P2", 128, 256), [(Id, X("Jb")), (X("Gv"), X("x2"))], "Wv")
+                scan(X("sv2"), X("pick"), R("P2", 128, 256), OP.add, OP.max, "sv")
+                ts(R("vl", 0, 8), R("sv2", 15, 128, 16), col(24), OP.add, name="vl")
+            else:
+                wstage(R("P2", 8, 16), 4, "x2", 0, 128, R("lw", 0, 8), "Wv")
+                ts(R("vl", 0, 8), R("P2", 8, 16), 512.0, OP.add, name="vl")
+            cp(X("al"), IND(R("C", 0, 1536), R("vl", 0, 8)), "a")
+            act(pA, IND(R("C", 0, 1536), R("vl", 0, 8)), AF.Copy, name="af")
+            act(own, IND(R("Y", RM, GB), R("vl", 0, 8)), AF.Copy, name="own")
+        for (a, b) in ((1024, 1472), (1472, W0), (W0, Wt), (0, 512), (512, 1024)):
+            if b > a:
+                act(R(nxt, a, b), IND(Fw, R("Fl", a // 16, b // 16)), AF.Copy, name="G")
+        if not last:
+            win = R("Y", GA, GB) if t % 2 == 0 else R("Y", RM, YW)
+            for j, (a, e) in enumerate(((1024, Wn), (0, 1024))):
+                pb = "P%d" % (6 - j)
+                n = (e - a) // 16
+                wstage(R(pb, 0, n), 3 if t % 2 == 0 else 2, nxt, a, e, None, "Gx")
+                ts(R("Yl", a // 16, e // 16), R(pb, 0, n), 1408.0 if t % 2 == 0 else 512.0, OP.add, name="Yl")
+                for (c, d) in ((a, a + 512), (a + 512, e)):
+                    act(R("YF", c, d), IND(win, R("Yl", c // 16, d // 16)), AF.Copy, 0.0, 0.5, "YF")
+        else:
+            for j, (a, e) in enumerate(((1024, WA), (0, 1024))):
+                pb = "P%d" % (6 - j)
+                n = (e - a) // 16
+                wstage(R(pb, 0, n), 1, nxt, a, e, None, "Gx")
+                act(R("fof", a // 16, e // 16), R(pb, 0, n), AF.Copy, name="fo")
+            dma("a", R("fo", 0, 152), R("fof", 0, 152), 77824, "st_f")
+    return ops
+
+
+def meet(x, y, same):
+    if x[1] != y[1]:
+        return False
+    if x[1][0] == "P" and not same:
+        return True
+    return x[2] < y[3] and y[2] < x[3] and x[5] < y[6] and y[5] < x[6]
+
+
+def links(ops):
+    hist = {}
+    for i, o in enumerate(ops):
+        pre = set()
+        for w0, xs in ((False, o["rd"]), (True, o["wr"])):
+            for x in xs:
+                for (j, y, w) in hist.get(x[1], []):
+                    same = ops[j]["eng"] == "p" and o["eng"] == "p"
+                    if (w or w0 or (x[1][0] == "P" and not same)) and meet(x, y, same):
+                        pre.add(j)
+        o["pre"] = sorted(pre)
+        for w0, xs in ((False, o["rd"]), (True, o["wr"])):
+            for x in xs:
+                h = hist.get(x[1], [])
+                if x[1][0] == "P" and o["eng"] != "p":
+                    h = [z for z in h if z[0] == i]
+                elif w0 and x[4] == 1 and x[7] == 1 and x[1][0] != "P":
+                    h = [z for z in h if z[0] == i or not (x[2] <= z[1][2] and z[1][3] <= x[3] and x[5] <= z[1][5] and z[1][6] <= x[6])]
+                hist[x[1]] = h + [(i, x, w0)]
+
+
+def costs(change):
+    keep = dict(TM)
+    TM.update(change)
+    ops = build()
+    c = ([o["dur"] for o in ops], [o["alt"][1] if "alt" in o else None for o in ops], [o["lat"] for o in ops], TM["HOP"], TM["HOPS"])
+    TM.update(keep)
+    return ops, c
+
+
+def place(prio, pre, eng, c, lead, back, lean):
+    dur, alt, lat, hop, hops = c
+    n = len(prio)
+    st = [None] * n
+    en = [0.0] * n
+    eng = list(eng)
+    busy = {}
+    for i0 in sorted(range(n), key=lambda k: prio[k]):
+        stack = [i0]
+        while stack:
+            i = stack[-1]
+            if st[i] is not None:
+                stack.pop()
+                continue
+            miss = [j for j in pre[i] if st[j] is None]
+            if miss:
+                stack += sorted(miss, key=lambda k: -prio[k])
+                continue
+            stack.pop()
+            best = None
+            for e in (("a", "v") if lean is not None and alt[i] is not None else (eng[i],)):
+                d = alt[i] if e == "v" and alt[i] is not None else dur[i]
+                t0 = lead[i]
+                for j in pre[i]:
+                    x = en[j] + (lat[i] if back else lat[j]) + (hops if eng[j] == e else hop)
+                    if x > t0:
+                        t0 = x
+                A, B = busy.setdefault(e, ([], []))
+                k = len(A)
+                while k > 0 and B[k - 1] > t0:
+                    k -= 1
+                while k < len(A) and t0 + d > A[k]:
+                    if B[k] > t0:
+                        t0 = B[k]
+                    k += 1
+                v = t0 + d + (lean[i] if lean is not None and e == "v" else 0.0)
+                if best is None or v < best[0]:
+                    best = (v, e, k, t0, d)
+            v, e, k, t0, d = best
+            busy[e][0].insert(k, t0)
+            busy[e][1].insert(k, t0 + d)
+            st[i] = t0
+            en[i] = t0 + d
+            eng[i] = e
+    return st, en, eng
+
+
+def replay(order, pre, eng, c, arcs=False):
+    dur, alt, lat, hop, hops = c
+    en = [0.0] * len(order)
+    by = [None] * len(order)
+    prev = {}
+    end = 0.0
+    top = 0
+    for i in order:
+        e = eng[i]
+        b = prev.get(e)
+        t0 = 0.0 if b is None else en[b]
+        for j in pre[i]:
+            x = en[j] + lat[j] + (hops if eng[j] == e else hop)
+            if x > t0:
+                t0 = x
+                b = j
+        en[i] = t0 + (alt[i] if e == "v" and alt[i] is not None else dur[i])
+        by[i] = b
+        prev[e] = i
+        if en[i] + lat[i] > end:
+            end = en[i] + lat[i]
+            top = i
+    if not arcs:
+        return end
+    out = []
+    while by[top] is not None:
+        if by[top] not in pre[top]:
+            out.append((by[top], top))
+        top = by[top]
+    return out or [(order[0], order[1])]
+
+
+def plan():
+    ops, c0 = costs({})
+    links(ops)
+    cs = [c0] + [costs(v)[1] for v in VARIANTS]
+    n = len(ops)
+    pre = [o["pre"] for o in ops]
+    post = [[] for _ in range(n)]
+    for i in range(n):
+        for j in pre[i]:
+            post[j].append(i)
+    rank = [0.0] * n
+    for i in range(n - 1, -1, -1):
+        rank[i] = max([rank[k] + c0[3] for k in post[i]] + [0.0]) + c0[2][i] + c0[0][i]
+    zero = [0.0] * n
+    eng0 = [o["eng"] for o in ops]
+    rng = np.random.default_rng(TM["SEED"])
+
+    def score(st, eng):
+        order = sorted(range(n), key=lambda k: (st[k], k))
+        v = [replay(order, pre, eng, c) for c in cs]
+        return sum(v) / len(v), v, order, st, eng
+
+    def both(st, en, eng):
+        rs, re_, _ = place([-x for x in en], post, eng, c0, c0[2], True, None)
+        return place([-x for x in re_], pre, eng, c0, zero, False, None)
+    lean = [TM["LEAN"]] * n
+    if len(START) == 2 * n:
+        z = [LETTERS.index(START[2 * i]) * 52 + LETTERS.index(START[2 * i + 1]) for i in range(n)]
+        st, en, eng = place([x // 2 for x in z], pre, ["v" if x % 2 else e for x, e in zip(z, eng0)], c0, zero, False, None)
+    else:
+        st, en, eng = both(*place([-r for r in rank], pre, eng0, c0, zero, False, lean))
+    best = score(st, eng)
+    seen = {}
+    same = {}
+    for i, o in enumerate(ops):
+        k = (o["t"], o["name"])
+        seen[k] = seen.get(k, 0) + 1
+        same.setdefault((o["name"], seen[k]) if o["t"] >= 0 else i, []).append(i)
+    kin = [None] * n
+    for v in same.values():
+        for i in v:
+            kin[i] = v
+    mark = [i for i, o in enumerate(ops) if o["name"] == "OH"]
+    now = best
+    for it in range(TM["ITA"]):
+        st, eng = now[3], list(now[4])
+        prio = list(st)
+        moves = []
+        if it == 0:
+            moves = [(i, st[i] - st[mark[2]], eng[i]) for i in range(n) if ops[i]["t"] == 2]
+        else:
+            arcs = replay(now[2], pre, now[4], cs[int(rng.integers(len(cs)))], True)
+            for _ in range(1 + int(rng.integers(2))):
+                j, i = arcs[int(rng.integers(len(arcs)))]
+                z = rng.random()
+                k = j if z < 0.15 or z >= 0.65 else i
+                e = eng[k]
+                p = st[k]
+                if z < 0.3 and c0[1][k] is not None:
+                    e = "v" if e == "a" else "a"
+                elif k == i:
+                    p = st[j] - 1 - 500 * rng.random() * (rng.random() < 0.3)
+                else:
+                    p = st[i] + 1 + 1500 * rng.random() * (rng.random() < 0.5)
+                moves.append((k, p - st[mark[max(ops[k]["t"], 0)]], e))
+        for (k, p, e) in moves:
+            for i in kin[k]:
+                prio[i] = st[mark[max(ops[i]["t"], 0)]] + p
+                eng[i] = e
+        st, en, eng = place(prio, pre, eng, c0, zero, False, None)
+        if rng.random() < TM["BOTH"]:
+            st, en, eng = both(st, en, eng)
+        sc = score(st, eng)
+        if it == 0 or sc[0] <= now[0] + TM["HEATA"] * (1 - it / TM["ITA"]) * rng.exponential():
+            now = sc
+            if sc[0] < best[0]:
+                best = sc
+    now = best
+    for it in range(TM["IT"]):
+        if rng.random() < TM["AIM"]:
+            arcs = replay(now[2], pre, now[4], cs[int(rng.integers(len(cs)))], True)
+            prio = list(now[3])
+            eng = list(now[4])
+            for _ in range(1 + int(rng.integers(2))):
+                j, i = arcs[int(rng.integers(len(arcs)))]
+                z = rng.random()
+                k = j if z < 0.2 else i
+                if z < 0.3 and c0[1][k] is not None:
+                    eng[k] = "v" if eng[k] == "a" else "a"
+                elif z < 0.65:
+                    prio[i] = prio[j] - 1 - 500 * rng.random() * (rng.random() < 0.3)
+                else:
+                    prio[j] = prio[i] + 1 + 1500 * rng.random() * (rng.random() < 0.5)
+        else:
+            bst = np.array(now[3])
+            near = np.abs(bst - rng.random() * bst.max()) < TM["WIN"][int(rng.integers(3))]
+            prio = (bst + near * rng.normal(0, TM["AMP"][int(rng.integers(3))], n)).tolist()
+            flip = near & (rng.random(n) < TM["FLIP"][int(rng.integers(3))])
+            eng = [("v" if e == "a" else "a") if flip[i] and c0[1][i] is not None else e for i, e in enumerate(now[4])]
+        st, en, eng = place(prio, pre, eng, c0, zero, False, None)
+        if rng.random() < TM["BOTH"]:
+            st, en, eng = both(st, en, eng)
+        sc = score(st, eng)
+        if sc[0] <= now[0] + TM["HEAT"] * (1 - it / TM["IT"]) * rng.exponential():
+            now = sc
+            if sc[0] < best[0]:
+                best = sc
+    for i, o in enumerate(ops):
+        if best[4][i] != o["eng"]:
+            o["eng"] = "v"
+            o["calls"], o["dur"] = o["alt"]
+    return ops, best[2], best[3], best[1], (pre, best[4])
+
+
+PLAN = []
+
+
+def rank_program(g, core, T, topo):
+    rank = T.rank_of(core)
+    if rank is None:
+        return
+    if not PLAN:
+        PLAN.append(plan())
+    ops, order = PLAN[0][:2]
+    q = {"v": g.vector, "a": g.scalar, "p": g.tensor, "g": g, "s": g.sync}
+    csem = {"v": "sv", "a": "sa", "p": "sp", "g": "sg"}
+    peers = [r for r in range(N) if r != rank]
+    far = [r for r in peers if topo.chip(T.cores[r]) != topo.chip(core)]
+    near = [r for r in peers if r not in far]
+    fe = [e for e in topo.engines(core, T.cores[far[0]]) if all(e in topo.engines(core, T.cores[r]) for r in far)]
+    ne = [e for e in topo.engines(core, T.cores[near[0]]) if e not in fe][:4]
+    arrive = len(far) * len(fe) + len(near) * len(ne)
+    done = {}
+    total = {}
+    seen = {}
+    nd = [0]
+
+    def wait(e, s, v):
+        if seen.get((e, s), 0) < v:
+            q[e].wait_ge(T.sem[s], v)
+            seen[(e, s)] = v
+
+    for i in order:
+        o = ops[i]
+        e = o["eng"]
+        if o["kind"] == "x":
+            t = o["calls"][0][1][0]
+            done[i] = ("arr%d" % t, arrive)
+            total["arr%d" % t] = arrive
+            continue
+        need = {}
+        for j in o["pre"]:
+            s, v = done[j]
+            need[s] = max(need.get(s, 0), v)
+        for s in sorted(need):
+            wait(e, s, need[s])
+        if o["kind"] == "s":
+            src, gh, t = o["calls"][0][1]
+            trs = []
+            for grp, eng in ((far, fe), (near, ne)):
+                ids = [DstId(rid=topo.addr(T.cores[r])[0], pnc=topo.addr(T.cores[r])[1]) for r in grp]
+                at = [gh + S * ((rank - r - 1) % N) for r in grp]
+                trs.append(RemoteDMATransfer(dst_ids=ids, dma_engine_mask=sum(1 << k for k in eng), remote_sem=T.sem["arr%d" % t],
+                                             srcs=[ap(T, src)], dsts=[T.Y[:, a:a + S] for a in at]))
+            g.remote_dma_fused(trs, local_sem=T.sem.sent)
+            total["sent"] = total.get("sent", 0) + len(fe) + len(ne)
+            done[i] = ("sent", total["sent"])
+        elif o["kind"] == "d":
+            s = "d%d" % nd[0]
+            nd[0] += 1
+            out, src = o["calls"][0][1]
+            q[e].dma_start(ap(T, out), ap(T, src)).then_inc(T.sem[s], 16)
+            total[s] = 16
+            done[i] = (s, 16)
+        else:
+            s = csem[e]
+            for (nm, args, kw) in o["calls"]:
+                a = [ap(T, x) for x in args]
+                k = {u: ap(T, x) for u, x in kw.items()}
+                if nm == "matmul":
+                    ins = g.tensor.matmul(*a)
+                elif nm == "activation":
+                    ins = g.scalar.activation(*a, **k)
+                elif nm == "iota":
+                    ins = g.iota(*a, **k)
+                elif nm == "affine_select":
+                    ins = g.affine_select(*a)
+                elif nm == "tensor_copy":
+                    ins = g.vector.tensor_copy(*a)
+                elif nm == "tensor_tensor":
+                    ins = g.vector.tensor_tensor(*a)
+                elif nm == "tensor_scalar":
+                    ins = g.vector.tensor_scalar(*a)
+                elif nm == "tensor_tensor_scan":
+                    ins = g.vector.tensor_tensor_scan(*a)
+                elif nm == "memset":
+                    ins = g.vector.memset(*a)
+                else:
+                    ins = g.vector.transpose(*a)
+                ins.then_inc(T.sem[s], 1)
+                total[s] = total.get(s, 0) + 1
+            done[i] = (s, total[s])
+    for s in sorted(total):
+        wait("g", s, total[s])

@@ -39,7 +39,7 @@ SCRATCH = {
     "key": sb(384, "float32"), "mx": sb(256, "float32"), "OH": sb(384, "bfloat16"),
     "l1": sb(24, "uint16"), "l2": sb(24, "uint16"), "fq": sb(128, "bfloat16"),
     "x1": sb(128, "bfloat16"), "x1l": sb(8, "uint16"), "x2": sb(128, "bfloat16"), "sx": sb(128, "float32"), "sv2": sb(128, "float32"),
-    "A2": sb(256, "float32"), "B2": sb(128, "float16"), "B3": sb(128, "float16"), "n1": sb(128, "bfloat16"), "new": sb(512, "bfloat16"),
+    "A2": sb(256, "float32"), "B2": sb(128, "float16"), "B3": sb(128, "float16"), "B4": sb(128, "int32"), "n1": sb(128, "bfloat16"), "new": sb(512, "bfloat16"),
     "cn": sb(128, "float32"), "f1": sb(128, "bfloat16"), "f2": sb(128, "bfloat16"), "f3": sb(128, "bfloat16"),
     "aw": sb(8, "float32"), "ar": sb(128, "float32"), "eq": sb(128, "float32"), "kl": sb(128, "float32"), "kt": sb(8, "float32"),
     "sl": sb(16, "uint16"), "lv": sb(128, "float32"), "nod": sb(512, "float32"), "fof": sb(152, "float32"),
@@ -47,17 +47,22 @@ SCRATCH = {
 for k_ in range(8):
     SCRATCH["P%d" % k_] = ("psum", [128, 512], "float32")
 NDMA = 16
-SEMAPHORES = ["sv", "sa", "sp", "sg", "sent"] + ["arr%d" % t for t in range(RO)] + ["d%d" % k for k in range(NDMA)]
+SEMAPHORES = ["sv", "sa", "sp", "sg", "sent"] + ["arr%d" % t for t in range(RO)] + ["hop%d" % t for t in range(RO)] + ["d%d" % k for k in range(NDMA)]
 DSZ = {"bfloat16": 2, "float16": 2, "uint16": 2, "float32": 4, "int32": 4}
 
 TM = {"CY": 1.0, "GAT": 1.56, "SCA": 3.8, "FIX": 60.0, "PCY": 0.55, "PFIX": 0.0, "HOP": 110.0, "HOPS": 70.0, "BW": 200.0, "ARR": 3000.0,
       "SCAN": 0, "C1": 512, "DS": ((0, 64), (64, 96), (96, 128)), "IT": 4000, "SEED": 1, "LEAN": 300.0,
-      "WIN": (1500, 3000, 8000), "AMP": (100, 300, 800), "FLIP": (0.0, 0.03, 0.1), "BOTH": 0.5, "HEAT": 40.0, "AIM": 0.9, "ITA": 0, "HEATA": 150.0}
-VARIANTS = [{"PCY": 0.45, "GAT": 1.2, "SCA": 2.5, "BW": 350.0}, {"PCY": 0.9, "GAT": 1.9, "SCA": 5.0, "ARR": 4500.0}]
+      "WIN": (1500, 3000, 8000), "AMP": (100, 300, 800), "FLIP": (0.0, 0.03, 0.1), "BOTH": 0.5, "HEAT": 40.0, "AIM": 0.9, "ITA": 0, "NEWV": 0, "HELP": 2, "FIXN": 60.0, "ZF": 0, "HEATA": 150.0}
+TM.update({"CY": .9, "PCY": .45, "FIX": 55.0, "FIXN": 20.0, "HOP": 200.0, "HOPS": 120.0, "ARR": 4500.0, "BW": 300.0,
+           "NEWV": 1, "ZF": 1, "IT": 7000, "BOTH": 0.3})
+VARIANTS = [{"HOP": 110.0, "HOPS": 70.0, "FIXN": 60.0, "ARR": 5500.0, "BW": 200.0},
+            {"HOP": 280.0, "HOPS": 250.0, "FIXN": 0.0, "CY": .83, "ARR": 4000.0, "BW": 400.0, "GAT": 1.2, "SCA": 2.5},
+            {"CY": 1.15, "PCY": .6, "GAT": 1.8, "SCA": 4.5}]
 
 
 LETTERS = "abcdefghijklmnopqrstuvwxyzABCDEFGHIJKLMNOPQRSTUVWXYZ"
 START = "aiaaacamakdQbOaeeYagaoaqasauaEaObcbybKbWceckcqcAcQdadgdodydIdUeacucycMcYbYcoayaAaCawaIaGbsbCdcaWaMbebMbgbuaUbEbabJchbGbqbAcbcdbxbkbVbocwcIdCcmcUdPhohufihCcEfehihIfchYcGcOcCcKdYemeMicieikbQhMighAhWhqhQdqdidwaQbSdmcWdGdKcsekfEdkaSdebmhEeceQbidAdNeieqeseUeWciaKaYdWeoeweCeEeGeOfufQfkgegOgUhahcgnhwhSiyiqiiiwcSdudsdEeeeSeufCfyfwdSegeyeKeIeAfgfqfafGjAjugSgMjggIiIgAjWkmjKjQhOfmfpfAfKfSfsfMfUfYfOfWgcgsgogugCgKgggqgwgyfIgEgbglgWhghmhsgigGgQgYhehkhyhGhKiahUioimiCiEiMisiAiGiSiYjejmjCjqiKiUjcjwiWjskakejEjSkqjijIiuiOiQjajojGjYjMkckikokukwkAkIkOkUkkkykEkGkCjkjykgjUjOkMlilqkskSkYlykKkQlelclklalmkWlglwlolulslAlKlClSlPlJlFlUmcmglGmemqmwlYmomAmIlWmamimkmzmGmMmSlMlQmLmPmmmsmumCmQmXnanmnqninonwnCncnsmEmUmYnengnknunAnynGnEnKnInUnOoanMnSnYoeokoqowoUoyogosoCoIouoEoWpaoQpcpmomoKpopEnQnWocoioooGoMoAoSoYpepkpqpwpApCpgpspypUpQoOpGpMpipupSqiqxqqpKpYqkqeqoqAqGqQqMqSrcpIpOqmqcqgqaqsquqyqIpWqEqDqOqYreqKqWrirIrmrErMrUqUrgrqrCrarkrurGrQrWrxrBrortryrOsgsksosqsysisssAsGsasurSrYrKscsesmswsEsCsKsIsOsMsYsStcsQsUtatgtmtstytQtItitAtGtOtwtKucuktYumustqtWuguysWtetltotutEtMtCtSuaueuiuquwuAuGuuuEuIwJuOuKtUuCuUuouQuYvovgvevqvtvwuWvavQvUvKvWvIuMuSvcvkvivmvAvuvyvOvEvHvSwcwqvMwawkwGwgwswEwMvYwmwuwAwewiwowwvDwWwDwUwywQwYxgxkxmxcxowOwSwKxaxexixqxsxuxwxyxCxAxMxGxWxFxIxOxUyayeymyCzaxYzgzmzoyqyMygyExKydxSykyoysywxRyyyAyGyKyOyQyUyYzczizszuyuyiyIySzeyWzlzqzxzy"
+START = "aiamaaacakdGaecKboawbQaWbiaJaKcOagaqaAaMbabubKbYcycMcWdgdqdydAdIeaekeweMfcfofEcqcIbgcgeceKauayaCasaEaGaObwaQaSaYbeeqdocUbGbAbrcscEdmbMckcmcecibybEcoaUbcbkbIbOeifafgeoeucweCeIeOdUfedKdQcAcGcucQdcfkhUiaeEeyiCfmfqeseScccCcSdOeQighYcabUdCfMiuaobCbSbWdadWdsbmfifwgwhqhAhGhObscYdefSgagsgygIhdgUhihuhghIhWieikimioiyjeiYiSiKiQdwdjdkdudEdSdYeeemgAdMegeAeWeUeGfsfyfIfYfGfQfCfKfUfuhygQkggWiqhoeYfOfWgigqgMfAgcgkgCgmgEgShkgegugGgYgggogKhehKhQhwhEgOisiAiIhahChmhSiciiiwiGiEiOiMiWiUjmjkjChMhsjajgjojujAjSjOjsjGjQkdjIjUkmkskikukykokGjcjijqjwjEjKjWjykakekkkqkwkCkIkOkSkAkKkQlmlcjMjYkMkYkEkUlAlglelqlulzlwlIlWlQmamcmglakWlilslklolGlClElUnalMlPlYmkmylSmimqmAmmmumEmMmemomwmGmsmCmKmSlLmYmWnfmImRngnqnknsnynEnGnmnCnKnQnWogmOmUncninonunInOnMnSnUnYocoooeounAnwoaoiomosoAoUoQoyoKpapioGoSpkpqpspCpMpepwoIoYokoqowoEoOoWpcoCpgpopupApEpIpQpWpypSpYqiqeoMpmpGpKpUpOqaqGqsqgqyqCqFqoqPrgraqWrkriqkqcqAqqquqwqMqIqKrcqmqSqVrerqrEqYrorwrGrsrArKrUryrIrSsarmrurCrMqRrPsesgrQrZsksusoswsAsGsKsqsEsOsUtatkrWscsismsssysMsSsQsYsWtctgtstitysIsCtetmtqtwtEuatUtCtQtYumtPucusuAuwuEuOukuGtKugtotutAtItSueuitGuquuuyuCuKuSuWvauIuUvcvmvitMtWuouYuMuQvevCvsvkvuvGvJvqvOvWwiwcwmwkvgvovwvEvAvyvQvKvMvYvUvTwgwswGwawqwywIwuwCwMwYwAwKwWxewowwwEwOwfwVwRxiwSxdxmxuxqxwxKxQxaxgxkxoxsxyxExGxIxMxOxUxSycyaysxCxAxWyeymyqyuyMzuykyCyUzCyyyQyGyYxYyiygywyEyIyOyoySyWzczgzmzozqzszAzEzKzMyKyAzfzazizkzyzwzHzI"
 
 
 def R(name, a, b, step=1, p0=0, p1=128, ps=1):
@@ -122,7 +127,7 @@ def build():
             return FIX + cnt(a) * GAT * CY
         if out[0] == "i":
             return FIX + cnt(out) * SCA * CY
-        return FIX + max(64, cnt(a) * per) * CY
+        return TM["FIXN"] + max(64, cnt(a) * per) * CY
 
     def cp(out, a, name=""):
         add("v", [("tensor_copy", (out, a), {})], [a], [out], vdur(out, a, 0.5 if a[0] == "r" and out[0] == "r" and narrow(a, out) else 1), name=name)
@@ -201,7 +206,11 @@ def build():
     dma("a", R("thi", 0, 128, 1, 0, 8), R("th", 0, 128, 1, 0, 8), 4096, "ld_t")
     dma("s", R("Ci", 128, 1024), R("cl", 128, 1024), 460000, "ld_c", [R("Li", 0, 2048)])
     ms(R("one", 0, 512), 1.0)
-    ms(R("DD", 0, 4096), 0.0)
+    if TM["ZF"]:
+        for h in range(0, 4096, 512):
+            act(R("DD", h, h + 512), R("one", 0, 512), AF.Copy, 0.0, 0.0, "z")
+    else:
+        ms(R("DD", 0, 4096), 0.0)
     ms(R("Y", RM, BS), 0.0)
     iota(R("pi", 0, 1), [[0, 1]], 0, 1)
     iota(R("pi", 6, 7), [[0, 1]], 11, 1)
@@ -425,12 +434,20 @@ def build():
         act(X("fq"), IND(Fw, bq), AF.Copy, name="fq")
         cp(IND(Fw, vs), X("fq"), "F6")
         nw = R("new", S * t, S * t + S)
-        act(R("A2", 0, 128), IND(YFw, bq), AF.Identity, 1023.75, 1.0, "A2")
-        tt(X("B2"), IND(YFw, cq), R("A2", 0, 128), OP.add, "B2")
-        acc(R("P0", 0, 128), [(X("nId"), own), (Id, X("B2"))], "dq")
-        act(X("n1"), R("P0", 0, 128), AF.Sign, -1024.0, 1.0, "sg")
-        acc(R("P0", 128, 256), [(Id, own), (Id, X("n1"))], "nw")
-        act(nw, R("P0", 128, 256), AF.Copy, name="new")
+        if TM["NEWV"]:
+            acc(R("P0", 0, 128), [(Id, own), (X("nId"), one)], "dq")
+            acc(R("P0", 128, 256), [(Id, own), (Id, one)], "nw")
+            act(R("A2", 0, 128), IND(YFw, bq), AF.Identity, -0.25, 1.0, "A2")
+            tt(X("B4"), IND(YFw, cq), R("A2", 0, 128), OP.add, "B2")
+            tt(X("n1"), X("B4"), R("P0", 0, 128), OP.max, "sg")
+            tt(nw, X("n1"), R("P0", 128, 256), OP.min, "new")
+        else:
+            act(R("A2", 0, 128), IND(YFw, bq), AF.Identity, 1023.75, 1.0, "A2")
+            tt(X("B2"), IND(YFw, cq), R("A2", 0, 128), OP.add, "B2")
+            acc(R("P0", 0, 128), [(X("nId"), own), (Id, X("B2"))], "dq")
+            act(X("n1"), R("P0", 0, 128), AF.Sign, -1024.0, 1.0, "sg")
+            acc(R("P0", 128, 256), [(Id, own), (Id, X("n1"))], "nw")
+            act(nw, R("P0", 128, 256), AF.Copy, name="new")
         gh = GA if t % 2 == 0 else GB
         add("g", [("send", (nw, gh, t), {})], [nw], [R("@%d" % t, 0, 1)], 1000, kind="s", name="send")
         add("x", [("arr", (t,), {})], [R("@%d" % t, 0, 1)], [R("Y", gh, gh + 896)], 0, kind="x", lat=TM["ARR"], name="arr")
@@ -651,7 +668,7 @@ def plan():
     lean = [TM["LEAN"]] * n
     if len(START) == 2 * n:
         z = [LETTERS.index(START[2 * i]) * 52 + LETTERS.index(START[2 * i + 1]) for i in range(n)]
-        st, en, eng = place([x // 2 for x in z], pre, ["v" if x % 2 else e for x, e in zip(z, eng0)], c0, zero, False, None)
+        st, en, eng = place([x // 2 for x in z], pre, ["v" if x % 2 and a is not None else e for x, e, a in zip(z, eng0, c0[1])], c0, zero, False, None)
     else:
         st, en, eng = both(*place([-r for r in rank], pre, eng0, c0, zero, False, lean))
     best = score(st, eng)
@@ -740,10 +757,33 @@ def plan():
 PLAN = []
 
 
+def helpers(T, topo, r):
+    core = T.cores[r]
+    far = [k for k in range(N) if topo.chip(T.cores[k]) != topo.chip(core)]
+    aides = [c for c in topo.cores_of(core) if topo.die(c) == topo.die(core) and T.rank_of(c) is None][:TM["HELP"]]
+    m = len(far) // (len(aides) + 1)
+    return aides, [far[m * j:m * j + m] for j in range(len(aides) + 1)]
+
+
 def rank_program(g, core, T, topo):
     rank = T.rank_of(core)
     if rank is None:
+        for r in range(N):
+            aides, shares = helpers(T, topo, r)
+            if core in aides:
+                grp = shares[1 + aides.index(core)]
+                eng = topo.engines(core, T.cores[grp[0]])
+                for t in range(RO):
+                    gh = GA if t % 2 == 0 else GB
+                    g.wait_ge(T.sem["hop%d" % t], len(topo.engines(T.cores[r], core)))
+                    at = [gh + S * ((r - k - 1) % N) for k in grp]
+                    g.remote_dma_fused([RemoteDMATransfer(dst_ids=[DstId(rid=topo.addr(T.cores[k])[0], pnc=topo.addr(T.cores[k])[1]) for k in grp],
+                                                          dma_engine_mask=sum(1 << k for k in eng), remote_sem=T.sem["arr%d" % t],
+                                                          srcs=[T.new[:, S * t:S * t + S]], dsts=[T.Y[:, a:a + S] for a in at])], local_sem=T.sem.sent)
+                g.wait_ge(T.sem.sent, RO * len(eng))
         return
+    aides, shares = helpers(T, topo, rank)
+    mine = shares[0]
     if not PLAN:
         PLAN.append(plan())
     ops, order = PLAN[0][:2]
@@ -753,7 +793,7 @@ def rank_program(g, core, T, topo):
     far = [r for r in peers if topo.chip(T.cores[r]) != topo.chip(core)]
     near = [r for r in peers if r not in far]
     fe = [e for e in topo.engines(core, T.cores[far[0]]) if all(e in topo.engines(core, T.cores[r]) for r in far)]
-    ne = [e for e in topo.engines(core, T.cores[near[0]]) if e not in fe][:4]
+    ne = [e for e in topo.engines(core, T.cores[near[0]]) if e not in fe][:8 if aides else 4]
     arrive = len(far) * len(fe) + len(near) * len(ne)
     done = {}
     total = {}
@@ -782,7 +822,13 @@ def rank_program(g, core, T, topo):
         if o["kind"] == "s":
             src, gh, t = o["calls"][0][1]
             trs = []
-            for grp, eng in ((far, fe), (near, ne)):
+            if aides:
+                he = topo.engines(core, aides[0])
+                g.remote_dma_fused([RemoteDMATransfer(dst_ids=[DstId(rid=topo.addr(h)[0], pnc=topo.addr(h)[1]) for h in aides],
+                                                      dma_engine_mask=sum(1 << k for k in he), remote_sem=T.sem["hop%d" % t],
+                                                      srcs=[ap(T, src)], dsts=[ap(T, src) for h in aides])], local_sem=T.sem.sent)
+                total["sent"] = total.get("sent", 0) + len(he)
+            for grp, eng in ((mine, fe), (near, ne)):
                 ids = [DstId(rid=topo.addr(T.cores[r])[0], pnc=topo.addr(T.cores[r])[1]) for r in grp]
                 at = [gh + S * ((rank - r - 1) % N) for r in grp]
                 trs.append(RemoteDMATransfer(dst_ids=ids, dma_engine_mask=sum(1 << k for k in eng), remote_sem=T.sem["arr%d" % t],

@@ -1,4 +1,3 @@
-import numpy as np
 from concourse.bass import DstId, RemoteDMATransfer
 from concourse.mybir import AluOpType, ActivationFunctionType
 
@@ -8,8 +7,11 @@ N, S, RO = 8, 128, 4
 W0, WA, WD = 1920, 2432, 2560
 GA, RM, BS, GB, YW = 0, 896, 1408, 2432, 3328
 OFF = 1216
-BIG = 1.0e6
-PK = 8192.0
+BIG = 1.0e9
+KEY = 2048.0
+RND = 1.5 * 2.0 ** 38
+HELP = 2
+PIECES = ((0, 512, "P0"), (512, 1024, "P1"), (1024, 1536, "P2"), (1536, 1792, "P3"), (1792, 1920, "P6"), (1920, 2048, "P4"))
 
 
 def sb(n, d):
@@ -20,27 +22,26 @@ SCRATCH = {
     "Y": sb(YW, "bfloat16"), "YF": sb(WA, "bfloat16"), "F0": sb(WD, "bfloat16"), "F1": sb(WD, "bfloat16"),
     "FI": sb(WD, "bfloat16"), "Li": sb(2048, "int32"), "L": sb(2064, "float32"), "Ci": sb(1024, "int32"),
     "C": sb(1536, "float32"), "fwi": sb(120, "int32"), "fwf": sb(160, "float32"), "thi": sb(128, "int32"),
-    "thf": sb(128, "float32"), "th16": sb(128, "float32"),
-    "DD": sb(4096, "bfloat16"), "J": sb(144, "float32"), "JG": sb(128, "float32"),
-    "pi": sb(8, "int32"), "pf": sb(8, "float32"), "RH": sb(16, "float32"), "col": sb(40, "float32"),
-    "Id": sb(128, "bfloat16"), "Idf": sb(128, "float32"), "R5": sb(128, "bfloat16"), "Go": sb(128, "bfloat16"), "Gb": sb(128, "bfloat16"),
-    "G1r": sb(128, "bfloat16"), "Gn": sb(128, "bfloat16"), "Gv": sb(128, "bfloat16"), "Jb": sb(128, "bfloat16"),
-    "m16": sb(128, "bfloat16"), "nId": sb(128, "bfloat16"), "one": sb(512, "bfloat16"), "onf": sb(128, "float32"),
-    "Bw": sb(5 * 144, "bfloat16"), "E32": sb(512, "bfloat16"),
-    "MS": sb(512, "float32"), "T16": sb(128, "float32"), "ks": sb(16, "bfloat16"), "tie": sb(256, "float32"),
-    "rs": sb(256, "float32"), "keep": sb(128, "float32"), "tri": sb(128, "bfloat16"), "trt": sb(128, "float32"), "pick": sb(128, "float32"),
-    "cw": sb(64, "float16"), "lw": sb(8, "bfloat16"), "lwf": sb(8, "float32"), "xi": sb(32, "int32"), "xl": sb(32, "uint16"),
+    "thf": sb(128, "float32"), "th0": sb(8, "float32"), "thr": sb(8, "float32"), "am": sb(8, "float32"),
+    "DD": sb(2048, "bfloat16"), "c4": sb(128, "float32"), "E": sb(2048, "bfloat16"), "K": sb(2048, "bfloat16"),
+    "J": sb(144, "float32"), "JG": sb(128, "float32"), "Jm": sb(128, "bfloat16"), "Im": sb(128, "bfloat16"),
+    "pi": sb(8, "int32"), "pf": sb(8, "float32"), "RH": sb(16, "float32"), "col": sb(24, "float32"),
+    "Id": sb(128, "bfloat16"), "Idf": sb(128, "float32"), "R5": sb(128, "bfloat16"), "Go": sb(128, "bfloat16"),
+    "Gc": sb(128, "bfloat16"), "Gn": sb(128, "bfloat16"), "I128": sb(128, "bfloat16"),
+    "one": sb(128, "bfloat16"), "onf": sb(128, "float32"), "Bw": sb(7 * 144, "bfloat16"), "Bt": sb(144, "float32"),
+    "MS": sb(512, "float32"), "place": sb(128, "float16"), "dq": sb(128, "float32"), "dp": sb(128, "float32"), "keep": sb(128, "float32"),
+    "tri": sb(128, "bfloat16"), "trt": sb(128, "float32"), "cw": sb(40, "float16"), "lw": sb(16, "bfloat16"),
+    "lwf": sb(24, "float32"), "xl": sb(24, "uint16"), "NI": sb(128, "int32"), "NB": sb(128, "bfloat16"),
     "t1": sb(160, "bfloat16"), "t2": sb(160, "float32"), "t3": sb(160, "float32"), "t4": sb(160, "float32"), "t5": sb(160, "float32"),
-    "Fl": sb(160, "uint16"), "Yl": sb(160, "uint16"), "vl": sb(8, "uint16"), "al": sb(128, "uint16"),
-    "G": sb(2048, "float16"), "bc": sb(256, "uint16"),
-    "pay": sb(768, "float32"), "Z1": sb(512, "float16"), "Z2": sb(512, "float16"),
-    "A": sb(2048, "float32"), "B": sb(2048, "float16"), "ab": sb(2048, "bfloat16"),
-    "own": sb(128, "bfloat16"), "oT": sb(128, "bfloat16"),
-    "key": sb(384, "float32"), "mx": sb(256, "float32"), "OH": sb(384, "bfloat16"),
-    "l1": sb(24, "uint16"), "l2": sb(24, "uint16"), "fq": sb(128, "bfloat16"),
-    "x1": sb(128, "bfloat16"), "x1l": sb(8, "uint16"), "x2": sb(128, "bfloat16"), "sx": sb(128, "float32"), "sv2": sb(128, "float32"),
-    "A2": sb(256, "float32"), "B2": sb(128, "float16"), "B3": sb(128, "float16"), "B4": sb(128, "int32"), "n1": sb(128, "bfloat16"), "new": sb(512, "bfloat16"),
-    "cn": sb(128, "float32"), "f1": sb(128, "bfloat16"), "f2": sb(128, "bfloat16"), "f3": sb(128, "bfloat16"),
+    "Fl": sb(160, "uint16"), "Yl": sb(160, "uint16"), "vm": sb(8, "uint16"), "vl": sb(32, "uint16"), "xb": sb(32, "bfloat16"),
+    "al": sb(128, "uint16"), "G": sb(2048, "float16"), "bc": sb(256, "uint16"), "bm": sb(128, "float32"), "bl": sb(128, "float32"),
+    "af": sb(128, "float32"), "dC": sb(128, "float32"), "f1": sb(128, "bfloat16"), "Z": sb(384, "float16"), "Zc": sb(128, "float32"),
+    "A": sb(2048, "float32"), "B": sb(2048, "float16"), "ab": sb(2048, "bfloat16"), "yb": sb(2048, "bfloat16"),
+    "own": sb(128, "bfloat16"), "oT": sb(128, "bfloat16"), "low": sb(128, "bfloat16"),
+    "mx": sb(256, "float32"), "ki": sb(16, "int32"), "kj": sb(16, "int32"), "jl": sb(16, "uint16"),
+    "nf": sb(8, "bfloat16"), "X": sb(8, "bfloat16"), "l1": sb(40, "uint16"), "fq": sb(128, "bfloat16"),
+    "x1": sb(128, "bfloat16"), "x1l": sb(8, "uint16"), "x2": sb(128, "bfloat16"), "alp": sb(128, "bfloat16"),
+    "n1": sb(128, "bfloat16"), "new": sb(512, "bfloat16"),
     "aw": sb(8, "float32"), "ar": sb(128, "float32"), "eq": sb(128, "float32"), "kl": sb(128, "float32"), "kt": sb(8, "float32"),
     "sl": sb(16, "uint16"), "lv": sb(128, "float32"), "nod": sb(512, "float32"), "fof": sb(152, "float32"),
 }
@@ -48,21 +49,10 @@ for k_ in range(8):
     SCRATCH["P%d" % k_] = ("psum", [128, 512], "float32")
 NDMA = 16
 SEMAPHORES = ["sv", "sa", "sp", "sg", "sent"] + ["arr%d" % t for t in range(RO)] + ["hop%d" % t for t in range(RO)] + ["d%d" % k for k in range(NDMA)]
-DSZ = {"bfloat16": 2, "float16": 2, "uint16": 2, "float32": 4, "int32": 4}
 
-TM = {"CY": 1.0, "GAT": 1.56, "SCA": 3.8, "FIX": 60.0, "PCY": 0.55, "PFIX": 0.0, "HOP": 110.0, "HOPS": 70.0, "BW": 200.0, "ARR": 3000.0,
-      "SCAN": 0, "C1": 512, "DS": ((0, 64), (64, 96), (96, 128)), "IT": 4000, "SEED": 1, "LEAN": 300.0,
-      "WIN": (1500, 3000, 8000), "AMP": (100, 300, 800), "FLIP": (0.0, 0.03, 0.1), "BOTH": 0.5, "HEAT": 40.0, "AIM": 0.9, "ITA": 0, "NEWV": 0, "HELP": 2, "FIXN": 60.0, "ZF": 0, "HEATA": 150.0}
-TM.update({"CY": .9, "PCY": .45, "FIX": 55.0, "FIXN": 20.0, "HOP": 200.0, "HOPS": 120.0, "ARR": 4500.0, "BW": 300.0,
-           "NEWV": 1, "ZF": 1, "IT": 7000, "BOTH": 0.3})
-VARIANTS = [{"HOP": 110.0, "HOPS": 70.0, "FIXN": 60.0, "ARR": 5500.0, "BW": 200.0},
-            {"HOP": 280.0, "HOPS": 250.0, "FIXN": 0.0, "CY": .83, "ARR": 4000.0, "BW": 400.0, "GAT": 1.2, "SCA": 2.5},
-            {"CY": 1.15, "PCY": .6, "GAT": 1.8, "SCA": 4.5}]
-
-
-LETTERS = "abcdefghijklmnopqrstuvwxyzABCDEFGHIJKLMNOPQRSTUVWXYZ"
-START = "aiaaacamakdQbOaeeYagaoaqasauaEaObcbybKbWceckcqcAcQdadgdodydIdUeacucycMcYbYcoayaAaCawaIaGbsbCdcaWaMbebMbgbuaUbEbabJchbGbqbAcbcdbxbkbVbocwcIdCcmcUdPhohufihCcEfehihIfchYcGcOcCcKdYemeMicieikbQhMighAhWhqhQdqdidwaQbSdmcWdGdKcsekfEdkaSdebmhEeceQbidAdNeieqeseUeWciaKaYdWeoeweCeEeGeOfufQfkgegOgUhahcgnhwhSiyiqiiiwcSdudsdEeeeSeufCfyfwdSegeyeKeIeAfgfqfafGjAjugSgMjggIiIgAjWkmjKjQhOfmfpfAfKfSfsfMfUfYfOfWgcgsgogugCgKgggqgwgyfIgEgbglgWhghmhsgigGgQgYhehkhyhGhKiahUioimiCiEiMisiAiGiSiYjejmjCjqiKiUjcjwiWjskakejEjSkqjijIiuiOiQjajojGjYjMkckikokukwkAkIkOkUkkkykEkGkCjkjykgjUjOkMlilqkskSkYlykKkQlelclklalmkWlglwlolulslAlKlClSlPlJlFlUmcmglGmemqmwlYmomAmIlWmamimkmzmGmMmSlMlQmLmPmmmsmumCmQmXnanmnqninonwnCncnsmEmUmYnengnknunAnynGnEnKnInUnOoanMnSnYoeokoqowoUoyogosoCoIouoEoWpaoQpcpmomoKpopEnQnWocoioooGoMoAoSoYpepkpqpwpApCpgpspypUpQoOpGpMpipupSqiqxqqpKpYqkqeqoqAqGqQqMqSrcpIpOqmqcqgqaqsquqyqIpWqEqDqOqYreqKqWrirIrmrErMrUqUrgrqrCrarkrurGrQrWrxrBrortryrOsgsksosqsysisssAsGsasurSrYrKscsesmswsEsCsKsIsOsMsYsStcsQsUtatgtmtstytQtItitAtGtOtwtKucuktYumustqtWuguysWtetltotutEtMtCtSuaueuiuquwuAuGuuuEuIwJuOuKtUuCuUuouQuYvovgvevqvtvwuWvavQvUvKvWvIuMuSvcvkvivmvAvuvyvOvEvHvSwcwqvMwawkwGwgwswEwMvYwmwuwAwewiwowwvDwWwDwUwywQwYxgxkxmxcxowOwSwKxaxexixqxsxuxwxyxCxAxMxGxWxFxIxOxUyayeymyCzaxYzgzmzoyqyMygyExKydxSykyoysywxRyyyAyGyKyOyQyUyYzczizszuyuyiyIySzeyWzlzqzxzy"
-START = "aiamaaacakdGaecKboawbQaWbiaJaKcOagaqaAaMbabubKbYcycMcWdgdqdydAdIeaekeweMfcfofEcqcIbgcgeceKauayaCasaEaGaObwaQaSaYbeeqdocUbGbAbrcscEdmbMckcmcecibybEcoaUbcbkbIbOeifafgeoeucweCeIeOdUfedKdQcAcGcucQdcfkhUiaeEeyiCfmfqeseScccCcSdOeQighYcabUdCfMiuaobCbSbWdadWdsbmfifwgwhqhAhGhObscYdefSgagsgygIhdgUhihuhghIhWieikimioiyjeiYiSiKiQdwdjdkdudEdSdYeeemgAdMegeAeWeUeGfsfyfIfYfGfQfCfKfUfuhygQkggWiqhoeYfOfWgigqgMfAgcgkgCgmgEgShkgegugGgYgggogKhehKhQhwhEgOisiAiIhahChmhSiciiiwiGiEiOiMiWiUjmjkjChMhsjajgjojujAjSjOjsjGjQkdjIjUkmkskikukykokGjcjijqjwjEjKjWjykakekkkqkwkCkIkOkSkAkKkQlmlcjMjYkMkYkEkUlAlglelqlulzlwlIlWlQmamcmglakWlilslklolGlClElUnalMlPlYmkmylSmimqmAmmmumEmMmemomwmGmsmCmKmSlLmYmWnfmImRngnqnknsnynEnGnmnCnKnQnWogmOmUncninonunInOnMnSnUnYocoooeounAnwoaoiomosoAoUoQoyoKpapioGoSpkpqpspCpMpepwoIoYokoqowoEoOoWpcoCpgpopupApEpIpQpWpypSpYqiqeoMpmpGpKpUpOqaqGqsqgqyqCqFqoqPrgraqWrkriqkqcqAqqquqwqMqIqKrcqmqSqVrerqrEqYrorwrGrsrArKrUryrIrSsarmrurCrMqRrPsesgrQrZsksusoswsAsGsKsqsEsOsUtatkrWscsismsssysMsSsQsYsWtctgtstitysIsCtetmtqtwtEuatUtCtQtYumtPucusuAuwuEuOukuGtKugtotutAtItSueuitGuquuuyuCuKuSuWvauIuUvcvmvitMtWuouYuMuQvevCvsvkvuvGvJvqvOvWwiwcwmwkvgvovwvEvAvyvQvKvMvYvUvTwgwswGwawqwywIwuwCwMwYwAwKwWxewowwwEwOwfwVwRxiwSxdxmxuxqxwxKxQxaxgxkxoxsxyxExGxIxMxOxUxSycyaysxCxAxWyeymyqyuyMzuykyCyUzCyyyQyGyYxYyiygywyEyIyOyoySyWzczgzmzozqzszAzEzKzMyKyAzfzazizkzyzwzHzI"
+FIRST = "m_Y ld_y ld_c0 i_p ld_f ld_t ld_l i_p5 m_sl i_Bt m_xb pi pi4 pi3 pi2 i_J pi1 m_one pf m_L i_one v:w13 pf1 cw RH w11 xl1 pf2 i_Jm w12 m_FI w15 w16 w14 s_MS1 w17 cw3 K Id w lw1 R5 lw cw1 I128 v:w10 K1 w1 w4 w3 i_dq lw2 w7 Im m_DD w2 place w8 s_MS2 s_Bt xl w9 m_FI1 E8 K2 w5 s_MS E11 R51 fw1 dq m_DD1 w6 i_JG own0 DD2 DD v:DD3 i_NI ownT+ v:K3 E6 E3 v:E10 E12 v:low+ i_trt DD1 v:K4 m_FI2 DD4 DD6 E5 s_dp v:DD7 Bw K5 E14 E7 vm0 v:E9 v:DD5 s_MS3 Go v:E13 Bw6 v:Bw1 NB K6 s_Idf tri1 m_FI3 Bw4 i_nod m_C K7 tri cw2 v:Bw3 th s_keep E4 NB1 Bw2 v:E2 a0 E15 ld_c vl0 Lcv+ Bw5 af0 E Gc fw Yl0 G3+ E1 fwM fwM1 nod Lcv2+ thW Gn NB2 Fl0 YF0_2 v:fi fi6 G1+ YF0_ oT+ Lcv1+ G+ fi1 YF0_3 dA4+ dA1+ dA3+ Crm+ G2+ th1 ext+ fi2 Ccv1+ YF0_1 ext1+ dA2+ fi7 D_+ cl+ tri2 v:fi4 fi3 Ccv+ c4+ dA+ A2+ fi8 bm+ cl1+ bc+ c41+ dA5+ fi5 A1+ bm1+ Lcv3+ B1+ A+ high+ u+ A4+ A5+ bc1+ B+ A3+ B4+ dB+ B3+ fi9 dB4+ bl+ B2+ f1+ dB3+ fi11 dB1+ A6+ u1+ fi10 fi12 abs+ dB2+ B5+ ftr abs1+ ftr2 dB5+ D+ yb2+ abs2+ D1+ ftr1 yb1+ yb+ abs3+ D2+ dC+ abs4+ D3+ abs5+ D4+ yb3+ F1 D5+ ftr3"
+ROUND = "mx mx1 ki nf D_+ kj X jl Zp Zq Za W_ room n1 W Zc new l Ysc fq alp aw F6 lv arM arr Csc ar Fx v:x1 cnt eq Wx FF1 Fl kl am kt send FF Fx1 am1 sl x1l FF2 Lsc x2 Fg Lsc1 Fl1 Lsc2 Wm thr Lsc3 FF4 Flg Lsc4 FF3 Wb Lsc5 vm Lsc6 a Wv Lsc7 v:G+ G2+ Gx vl Gx1 Yl G3+ v:G1+ own Yl1 YF1 v:YF v:xb ext+ ext1+ v:YF2 YF3 ownT+ cl+ cl1+ low+ c4+ c41+ oT+ bm+ A+ v:A1+ bc+ dA+ af bm1+ A2+ dA5+ dA3+ v:A4+ dA4+ high+ dA1+ bc1+ B+ dA2+ A3+ u+ B1+ st_le dB+ A6+ bl+ B2+ A5+ dB1+ f1+ abs+ u1+ B3+ Crm+ abs1+ dB2+ B4+ D+ B5+ dB3+ abs2+ dB4+ v:dC+ D1+ yb2+ dB5+ abs3+ yb1+ D2+ abs4+ yb+ abs5+ D3+ yb3+ D4+ D5+"
+LAST = "mx mx1 ki nf kj X jl W_ Za room Zq n1 W send l v:fq alp aw lv F6 new arM arr Ysc ar Fx1 FF1 eq Fx st_yb st_yr kl FF Fl1 kt sl Fl Lsc Lsc1 Lsc2 Lsc3 Lsc4 FF4 Lsc5 Lsc6 FF2 FF3 Lsc7 Gx st_lo Gx1 fo st_yg fo1 st_f"
 
 
 def R(name, a, b, step=1, p0=0, p1=128, ps=1):
@@ -71,12 +61,6 @@ def R(name, a, b, step=1, p0=0, p1=128, ps=1):
 
 def IND(win, off):
     return ("i", win, off)
-
-
-def cnt(x):
-    if x[0] == "i":
-        return 16 * cnt(x[2])
-    return (x[3] - x[2] + x[4] - 1) // x[4]
 
 
 def isap(x):
@@ -93,95 +77,69 @@ def ap(T, x):
     return T[x[1]][ps, cs]
 
 
-def regs(x):
-    if x[0] == "i":
-        return [x[1], x[2]]
-    return [x]
-
-
-def narrow(*xs):
-    return all(DSZ[SCRATCH[x[1]][2]] == 2 for x in xs if isap(x))
-
-
 def build():
     ops = []
     rnd = [-1]
-    CY, GAT, SCA, FIX, PCY, PFIX = TM["CY"], TM["GAT"], TM["SCA"], TM["FIX"], TM["PCY"], TM["PFIX"]
+    used = {}
 
-    def add(eng, calls, rd, wr, dur, kind="c", lat=0.0, name=""):
+    def add(eng, calls, rd, wr, name, kind="c", group=None):
         r2 = []
         w2 = []
         for x in rd:
             if isap(x):
-                r2 += regs(x)
+                r2 += [x[1], x[2]] if x[0] == "i" else [x]
         for x in wr:
             if x[0] == "i":
                 w2.append(x[1])
                 r2.append(x[2])
             else:
                 w2.append(x)
-        ops.append({"eng": eng, "calls": calls, "rd": r2, "wr": w2, "dur": dur, "kind": kind, "lat": lat, "name": name, "t": rnd[0]})
+        k = used.get((rnd[0], name), 0)
+        used[(rnd[0], name)] = k + 1
+        ops.append({"eng": eng, "calls": calls, "rd": r2, "wr": w2, "kind": kind, "name": name + (str(k) if k else ""), "t": rnd[0], "group": group})
 
-    def vdur(out, a, per):
-        if a[0] == "i":
-            return FIX + cnt(a) * GAT * CY
-        if out[0] == "i":
-            return FIX + cnt(out) * SCA * CY
-        return TM["FIXN"] + max(64, cnt(a) * per) * CY
+    def cp(out, a, name):
+        add("v", [("tensor_copy", (out, a), {})], [a], [out], name)
 
-    def cp(out, a, name=""):
-        add("v", [("tensor_copy", (out, a), {})], [a], [out], vdur(out, a, 0.5 if a[0] == "r" and out[0] == "r" and narrow(a, out) else 1), name=name)
+    def tt(out, a, b, op, name):
+        add("v", [("tensor_tensor", (out, a, b, op), {})], [a, b], [out], name)
 
-    def tt(out, a, b, op, name=""):
-        per = 1 if (a[0] == "r" and a[1][0] == "P") or b[1][0] == "P" else 2
-        add("v", [("tensor_tensor", (out, a, b, op), {})], [a, b], [out], vdur(out, a, per), name=name)
-
-    def ts(out, a, s1, o1, s2=None, o2=None, name=""):
+    def ts(out, a, s1, o1, s2, o2, name):
         args = (out, a, s1, None, o1) if o2 is None else (out, a, s1, s2, o1, o2)
-        add("v", [("tensor_scalar", args, {})], [a, s1, s2], [out], vdur(out, a, 0.5 if a[0] == "r" and narrow(a, out) else 1), name=name)
+        add("v", [("tensor_scalar", args, {})], [a, s1, s2], [out], name)
 
-    def scan(out, d0, d1, o0, o1, name=""):
-        add("v", [("tensor_tensor_scan", (out, d0, d1, 0.0, o0, o1), {})], [d0, d1], [out], vdur(out, d0, 1), name=name)
+    def scan(out, d0, d1, first, o0, o1, name):
+        add("v", [("tensor_tensor_scan", (out, d0, d1, first, o0, o1), {})], [d0, d1], [out], name)
 
-    def ms(out, val):
-        add("v", [("memset", (out, val), {})], [], [out], vdur(out, out, 0.5 if narrow(out) else 1), name="ms")
+    def ms(out, val, name):
+        add("v", [("memset", (out, val), {})], [], [out], name)
 
-    def act(out, a, f=AF.Identity, bias=0.0, scale=1.0, name=""):
-        add("a", [("activation", (out, a, f), {"bias": bias, "scale": scale})], [a, bias, scale], [out], vdur(out, a, 1), name=name)
-        if f in (AF.Copy, AF.Identity):
-            if scale == 0.0 and not isap(bias):
-                c = ("memset", (out, bias), {})
-            elif scale == 1.0 and bias == 0.0:
-                c = ("tensor_copy", (out, a), {})
+    def act(out, a, name, f=AF.Identity, bias=0.0, scale=1.0):
+        add("a", [("activation", (out, a, f), {"bias": bias, "scale": scale})], [a, bias, scale], [out], name)
+        if f == AF.Identity:
+            if scale == 1.0 and bias == 0.0:
+                ops[-1]["alt"] = [("tensor_copy", (out, a), {})]
             else:
-                c = ("tensor_scalar", (out, a, scale, bias, OP.mult, OP.add), {})
-            ops[-1]["alt"] = ([c], vdur(out, a, 0.5 if a[0] == "r" and narrow(a, out) else 1))
+                ops[-1]["alt"] = [("tensor_scalar", (out, a, scale, bias, OP.mult, OP.add), {})]
 
-    def mm(items, name=""):
-        calls = []
-        rd = []
-        wr = []
-        dur = 0.0
-        for (o, l, r, st, sp) in items:
-            calls.append(("matmul", (o, l, r, st, sp), {}))
-            rd += [l, r]
-            wr.append(o)
-            dur += PFIX + max(min(64, cnt(l)), cnt(r)) * PCY * (4 if SCRATCH[l[1]][2] == "float32" else 1)
-        add("p", calls, rd, wr, dur + 60, name=name)
+    def mm(items, name, group=None):
+        add("p", [("matmul", x, {}) for x in items], [x[1] for x in items] + [x[2] for x in items], [x[0] for x in items], name, group=group)
 
-    def acc(out, pairs, name=""):
+    def acc(out, pairs, name):
         mm([(out, l, r, j == 0, j == len(pairs) - 1) for j, (l, r) in enumerate(pairs)], name)
 
-    def iota(out, pat, base, cm):
+    def iota(out, pat, base, cm, name):
         kw = {} if SCRATCH[out[1]][2] == "int32" else {"allow_small_or_imprecise_dtypes": True}
-        add("g", [("iota", (out, pat, base, cm), kw)], [], [out, R("@g", 0, 1)], 130 + 2 * cnt(out) * CY, name="io")
+        add("g", [("iota", (out, pat, base, cm), kw)], [], [out], name)
 
-    def sel(out, a, pat, op, fill, base, cm):
-        add("g", [("affine_select", (out, a, pat, op, fill, base, cm), {})], [a], [out, R("@g", 0, 1)], 170 + 2 * cnt(out) * CY, name="sel")
+    def sel(out, a, pat, op, fill, base, cm, name):
+        add("g", [("affine_select", (out, a, pat, op, fill, base, cm), {})], [a], [out], name)
 
-    def dma(q, out, a, nbytes, name="", after=()):
-        add(q, [("dma_start", (out, a), {})], ([a] if a[1] in SCRATCH else []) + list(after), [out] if out[1] in SCRATCH else [], 60, kind="d",
-            lat=2000 + nbytes / TM["BW"], name=name)
+    def gcopy(out, a, name):
+        sel(out, a, [[0, out[3] - out[2]]], OP.is_ge, 0.0, 0, 0, name)
+
+    def dma(q, out, a, name, after=()):
+        add(q, [("dma_start", (out, a), {})], ([a] if a[1] in SCRATCH else []) + list(after), [out] if out[1] in SCRATCH else [], name, kind="d")
 
     def col(k):
         return R("col", k, k + 1)
@@ -193,163 +151,145 @@ def build():
         return R(name, 0, 128)
     Id, one = X("Id"), X("one")
 
-    def wstage(out, w, src, a, b, first=None, name=""):
-        it = [] if first is None else [(Id, first)]
-        for r in range(16):
-            it.append((R("Bw", 144 * w + 15 - r, 144 * w + 143 - r), R(src, a + r, b, 16)))
-        acc(out, it, name)
+    def shift(w, r):
+        return R("Bw", 144 * w + 15 - r, 144 * w + 143 - r)
 
-    dma("s", R("Ci", 0, 128), R("cl", 0, 128), 65536, "ld_c0")
-    dma("a", R("fwi", 0, 120), R("fw0", 0, 120), 61440, "ld_f")
-    dma("s", R("Li", 0, 2048), R("lk", 0, 2048), 1600000, "ld_l")
-    dma("a", R("Y", BS, YW), R("y0", 0, W0), 1000000, "ld_y")
-    dma("a", R("thi", 0, 128, 1, 0, 8), R("th", 0, 128, 1, 0, 8), 4096, "ld_t")
-    dma("s", R("Ci", 128, 1024), R("cl", 128, 1024), 460000, "ld_c", [R("Li", 0, 2048)])
-    ms(R("one", 0, 512), 1.0)
-    if TM["ZF"]:
-        for h in range(0, 4096, 512):
-            act(R("DD", h, h + 512), R("one", 0, 512), AF.Copy, 0.0, 0.0, "z")
-    else:
-        ms(R("DD", 0, 4096), 0.0)
-    ms(R("Y", RM, BS), 0.0)
-    iota(R("pi", 0, 1), [[0, 1]], 0, 1)
-    iota(R("pi", 6, 7), [[0, 1]], 11, 1)
-    iota(R("J", 0, 144), [[1, 144]], 0, 0)
-    iota(X("JG"), [[1, 8], [0, 16]], 0, 0)
-    iota(R("E32", 0, 512), [[1, 32], [0, 16]], 0, 0)
-    iota(X("onf"), [[0, 128]], 1, 0)
-    iota(X("trt"), [[0, 8], [1, 16]], 0, 0)
-    iota(R("tie", 0, 256), [[0, 16], [-1, 16]], 15, 0)
-    iota(X("Jb"), [[1, 128]], 0, 0)
-    iota(X("m16"), [[0, 128]], -16, 0)
-    iota(R("xi", 0, 16), [[16, 16]], 15, 0)
-    iota(R("xi", 16, 24), [[16, 8]], 15, 0)
-    iota(R("xi", 24, 32), [[1, 8]], 0, 0)
-    iota(R("rs", 0, 256), [[0, 256]], 0, 0)
-    sel(R("rs", 0, 256), R("rs", 0, 256), [[0, 16], [1, 16]], OP.is_gt, -BIG, 0, 0)
-    sel(X("keep"), X("onf"), [[0, 8], [1, 16]], OP.is_gt, 0.0, 0, 0)
-    sel(X("Idf"), X("onf"), [[1, 128]], OP.is_equal, 0.0, 0, -1)
-    iota(X("T16"), [[0, 128]], 16, 0)
-    sel(X("T16"), X("T16"), [[1, 8], [0, 16]], OP.is_equal, 0.0, 0, -1)
+    def rows(out, w, src, a, b, name, first=None):
+        acc(out, ([] if first is None else [(Id, first)]) + [(shift(w, r), R(src, a + r, b, 16)) for r in range(16)], name)
+
+    dma("s", R("Ci", 0, 128), R("cl", 0, 128), "ld_c0")
+    dma("a", R("fwi", 0, 120), R("fw0", 0, 120), "ld_f")
+    dma("s", R("Li", 0, 2048), R("lk", 0, 2048), "ld_l")
+    dma("a", R("Y", BS, YW), R("y0", 0, W0), "ld_y")
+    dma("a", R("thi", 0, 128, 1, 0, 8), R("th", 0, 128, 1, 0, 8), "ld_t")
+    dma("s", R("Ci", 128, 1024), R("cl", 128, 1024), "ld_c", [R("Li", 0, 2048)])
+    iota(R("pi", 0, 1), [[0, 1]], 0, 1, "i_p")
+    iota(R("pi", 6, 7), [[0, 1]], 11, 1, "i_p5")
+    iota(R("J", 0, 144), [[1, 144]], 0, 0, "i_J")
+    iota(X("JG"), [[1, 8], [0, 16]], 0, 0, "i_JG")
+    iota(X("Jm"), [[1, 16], [16, 8]], 0, 0, "i_Jm")
+    iota(X("onf"), [[0, 128]], 1, 0, "i_one")
+    iota(X("trt"), [[0, 8], [1, 16]], 0, 0, "i_trt")
+    iota(X("NI"), [[0, 4], [1, 32]], 1, 0, "i_NI")
+    iota(X("dq"), [[0, 128]], -2, 0, "i_dq")
+    sel(X("dp"), X("onf"), [[0, 8], [-1, 16]], OP.is_gt, -1.0, 15, 0, "s_dp")
+    sel(X("keep"), X("onf"), [[0, 8], [1, 16]], OP.is_gt, 0.0, 0, 0, "s_keep")
+    sel(X("Idf"), X("onf"), [[1, 128]], OP.is_equal, 0.0, 0, -1, "s_Idf")
+    iota(R("Bt", 0, 144), [[0, 144]], -int(KEY), 0, "i_Bt")
+    sel(R("Bt", 0, 144), R("Bt", 0, 144), [[1, 144]], OP.is_equal, 0.0, -15, -16, "s_Bt")
     for j in range(4):
-        sel(R("MS", 128 * j, 128 * j + 128), X("onf"), [[32, 4], [1000, 2], [1, 16]], OP.is_equal, 0.0, 16 * (j // 2) - 1000 * (j % 2), -1)
+        sel(R("MS", 128 * j, 128 * j + 128), X("onf"), [[32, 4], [1000, 2], [1, 16]], OP.is_equal, 0.0, 16 * (j // 2) - 1000 * (j % 2), -1, "s_MS")
+    iota(R("nod", 0, 512), [[1, 512]], W0, 0, "i_nod")
+    ms(one, 1.0, "m_one")
+    ms(R("Y", RM, BS), 0.0, "m_Y")
     for h in range(0, WD, 640):
-        ms(R("FI", h, h + 640), 0.0)
-    act(R("C", 0, 512), R("one", 0, 512), AF.Copy, 0.0, 0.0, "zc")
-    act(R("L", 2048, 2064), R("one", 0, 16), AF.Copy, 0.0, 0.0)
-    ts(R("pi", 1, 2), R("pi", 0, 1), 15, OP.bitwise_and)
-    ts(R("pi", 2, 3), R("pi", 0, 1), 4, OP.arith_shift_right)
-    ts(R("pi", 3, 4), R("pi", 6, 7), 15, OP.bitwise_and)
-    ts(R("pi", 4, 5), R("pi", 0, 1), 1, OP.bitwise_and)
-    ts(R("pi", 7, 8), R("pi", 0, 1), 31, OP.bitwise_and)
-    cp(R("pf", 0, 5), R("pi", 0, 5))
-    cp(R("pf", 7, 8), R("pi", 7, 8))
-    ts(R("E32", 0, 512), R("E32", 0, 512), R("pf", 7, 8), OP.is_equal)
-    ts(R("pf", 5, 6), R("pf", 2, 3), 16.0, OP.mult, 15.0, OP.add)
-    ts(R("pf", 6, 7), R("pf", 2, 3), 16.0, OP.mult, R("pf", 3, 4), OP.add)
-    pP, pR, pG, p5, pO, pW = [R("pf", k, k + 1) for k in (0, 1, 2, 6, 4, 5)]
-    ts(Id, X("J"), pP, OP.is_equal)
-    ts(X("R5"), X("J"), p5, OP.is_equal)
-    act(X("nId"), Id, AF.Copy, 0.0, -1.0)
-    for j, m in enumerate(("Id", "R5")):
-        for h in range(8):
-            act(R("DD", 2048 * j + 256 * h, 2048 * j + 256 * h + 256, 17), R(m, 16 * h, 16 * h + 16), AF.Copy, name="DD")
-    ts(R("RH", 0, 16), R("J", 0, 16), pR, OP.is_equal)
-    ts(X("Go"), X("JG"), pG, OP.is_equal)
-    ts(R("Bw", 0, 144), R("J", 0, 144), pW, OP.is_equal)
-    ts(R("ks", 0, 8), R("J", 0, 8), pG, OP.is_equal, 16.0, OP.mult)
-    ts(R("ks", 8, 16), R("J", 0, 8), pG, OP.is_equal, -16.0, OP.mult)
-    act(col(0), rh(1), AF.Identity, rh(0), 128.0)
-    act(col(1), rh(3), AF.Identity, col(0), -2432.0)
-    act(col(2), rh(2), AF.Identity, col(1), -2432.0)
-    act(col(3), rh(2), AF.Identity, rh(4), 1.0)
-    act(col(4), rh(6), AF.Identity, col(3), 1.0)
-    act(col(5), rh(3), AF.Identity, rh(7), 1.0)
-    act(col(6), rh(5), AF.Identity, col(5), -1.0)
-    act(col(7), col(6), AF.Copy, 0.0, -2432.0)
-    act(col(8), col(4), AF.Identity, col(7), 128.0)
-    act(col(9), rh(1), AF.Copy, 0.0, -32.0)
-    act(col(10), rh(0), AF.Copy, 0.0, 128.0)
-    act(col(11), rh(1), AF.Copy, 0.0, 128.0)
-    act(col(12), rh(0), AF.Identity, col(11), -2560.0)
-    act(col(13), rh(4), AF.Identity, rh(5), 1.0)
-    act(col(14), col(5), AF.Identity, col(13), 1.0)
-    act(col(15), rh(2), AF.Identity, rh(6), -1.0)
-    act(col(16), col(15), AF.Identity, col(14), 15.0)
-    act(col(22), rh(2), AF.Identity, col(16), 1.0)
-    act(col(19), rh(2), AF.Identity, col(14), 1537.0)
-    for t in (1, 2):
-        act(col(16 + t), col(15), AF.Identity, col(19), 15.0 + t)
-    act(col(21), pR, AF.Identity, 2048.0, 1.0)
-    for w, c in ((1, 0), (2, 1), (3, 2)):
-        act(R("Bw", 144 * w, 144 * w + 144), R("Bw", 0, 144), AF.Identity, 0.0, col(c))
-    act(X("Gb"), X("Go"), AF.Identity, 0.0, col(4))
-    act(X("G1r"), X("Go"), AF.Identity, 0.0, col(9))
-    if TM["SCAN"]:
-        act(X("Gn"), X("Go"), AF.Identity, 0.0, col(0))
-        act(X("Gv"), X("Go"), AF.Identity, 0.0, col(8))
-        act(col(23), rh(15), AF.Identity, -PK, PK)
-        act(col(24), rh(15), AF.Identity, 512.0 - PK, PK)
-        ts(X("sx"), X("trt"), pR, OP.is_equal, -3 * PK, OP.mult)
-        ts(X("sv2"), X("trt"), -1.0, OP.add, pR, OP.is_equal)
-        act(X("sv2"), X("sv2"), AF.Copy, 0.0, PK)
-        tt(X("pick"), X("sx"), X("sv2"), OP.add)
-    else:
-        act(R("Bw", 144 * 4, 144 * 5), R("Bw", 0, 144), AF.Identity, 0.0, col(8))
-    ts(X("eq"), X("trt"), pR, OP.is_gt, -8192.0, OP.mult)
-    ts(X("kl"), X("trt"), pR, OP.is_equal, 4096.0, OP.mult)
-    tt(X("tri"), X("eq"), X("kl"), OP.add)
-    act(R("lwf", 0, 8), R("J", 0, 8), AF.Identity, pR, 16.0)
-    act(R("lw", 0, 8), R("lwf", 0, 8), AF.Copy)
-    ts(R("vl", 0, 8), R("lwf", 0, 8), 512.0, OP.add)
-    ts(R("cw", 0, 8), R("lwf", 0, 8), float(WA - OFF), OP.add)
-    ts(R("cw", 8, 40), R("J", 0, 32), 0.0, OP.mult)
-    ts(R("cw", 40, 48), R("J", 0, 8), 0.0, OP.mult, -float(OFF), OP.add)
-    cp(R("xl", 0, 32), R("xi", 0, 32))
-    iota(R("nod", 0, 512), [[1, 512]], W0, 0)
-    act(R("nod", 0, 512), R("nod", 0, 512), AF.Identity, 0.0, pO, "nod")
-    ms(R("sl", 0, 16), 0)
-    pAl, pV, pA, pD = R("pay", 0, 128), R("pay", 128, 256), R("pay", 512, 640), R("pay", 640, 768)
-    cp(X("al"), R("Ci", 0, 128), "a0")
-    cp(pA, R("Ci", 0, 128))
-    cp(R("Yl", 0, 120), R("fwi", 0, 120), "yl0")
-    cp(R("Fl", 64, 120), R("fwi", 64, 120))
-    act(pV, one, AF.Identity, col(12), 0.0)
-    act(pAl, one, AF.Identity, col(22), 0.0)
-    cp(R("thf", 0, 128, 1, 0, 8), R("thi", 0, 128, 1, 0, 8))
-    acc(R("P7", 0, 128), [(R("thf", 0, 128, 1, 0, 8), R("T16", 0, 128, 1, 0, 8))])
-    act(X("th16"), R("P7", 0, 128), AF.Identity, 15.0)
-    for k in (3, 4, 6, 7):
-        act(R("th16", k, 128, 16), R("one", 0, 8), AF.Copy, 0.0, BIG)
-    act(R("key", 256, 384), X("th16"), AF.Copy)
-    cp(R("fwf", 0, 120), R("fwi", 0, 120))
-    act(col(25), pR, AF.Identity, float(W0))
-    act(R("fwf", 120, 160), R("J", 0, 40), AF.Identity, col(25), 16.0)
+        ms(R("FI", h, h + 640), 0.0, "m_FI")
+    for h in range(0, 2048, 1024):
+        ms(R("DD", h, h + 1024), 0.0, "m_DD")
+    ms(R("C", 0, 512), 0.0, "m_C")
+    ms(R("L", 2048, 2064), 0.0, "m_L")
+    ms(R("sl", 0, 16), 0, "m_sl")
+    ms(R("xb", 0, 8), -19.0, "m_xb")
+    ts(R("pi", 1, 2), R("pi", 0, 1), 15, OP.bitwise_and, None, None, "pi")
+    ts(R("pi", 2, 3), R("pi", 0, 1), 4, OP.arith_shift_right, None, None, "pi")
+    ts(R("pi", 3, 4), R("pi", 6, 7), 15, OP.bitwise_and, None, None, "pi")
+    ts(R("pi", 4, 5), R("pi", 0, 1), 1, OP.bitwise_and, None, None, "pi")
+    ts(R("pi", 5, 6), R("pi", 0, 1), 7, OP.bitwise_and, None, None, "pi")
+    cp(R("pf", 0, 6), R("pi", 0, 6), "pf")
+    pP, pR, pG, pO, p8, p5, pW = [R("pf", k, k + 1) for k in (0, 1, 2, 4, 5, 6, 7)]
+    act(p5, pG, "pf", bias=R("pf", 3, 4), scale=16.0)
+    act(pW, pG, "pf", bias=15.0, scale=16.0)
+    ts(Id, X("J"), pP, OP.is_equal, None, None, "Id")
+    ts(X("R5"), X("J"), p5, OP.is_equal, 4096.0, OP.mult, "R5")
+    tt(X("R5"), X("R5"), Id, OP.add, "R5")
+    ts(R("RH", 0, 16), R("J", 0, 16), pR, OP.is_equal, None, None, "RH")
+    ts(X("Go"), X("JG"), pG, OP.is_equal, None, None, "Go")
+    ts(R("Bw", 0, 144), R("J", 0, 144), pW, OP.is_equal, None, None, "Bw")
+    ts(X("Im"), X("Jm"), pP, OP.is_equal, None, None, "Im")
+    for h in range(8):
+        act(R("DD", 256 * h, 256 * h + 256, 17), R("R5", 16 * h, 16 * h + 16), "DD")
+    for k in range(16):
+        act(R("E", k, 2048, 16), X("Im"), "E")
+    act(R("K", 0, 16), R("RH", 0, 16), "K")
+    for k in range(4, 11):
+        act(R("K", 2 ** k, 2 ** (k + 1)), R("K", 0, 2 ** k), "K")
+    act(col(0), rh(1), "w", bias=rh(0), scale=128.0)
+    act(col(1), rh(3), "w", bias=col(0), scale=-2432.0)
+    act(col(2), rh(2), "w", bias=col(1), scale=-2432.0)
+    act(col(3), rh(2), "w", bias=rh(4))
+    act(col(4), rh(3), "w", bias=rh(5))
+    act(col(5), col(4), "w", scale=-19.0, bias=col(3))
+    act(col(6), col(5), "w", scale=128.0)
+    act(col(7), rh(3), "w", bias=rh(4))
+    act(col(8), col(7), "w", bias=rh(6))
+    act(col(9), col(7), "w", bias=rh(5))
+    act(col(10), rh(6), "w", scale=-4096.0)
+    act(col(11), pR, "w", bias=2048.0)
+    act(col(12), pR, "w", scale=-128.0, bias=KEY)
+    act(col(17), pR, "w", scale=256.0, bias=2.0 ** 23 - 2018)
+    act(col(13), pR, "w", bias=float(W0))
+    act(col(14), pR, "w", scale=8.0)
+    act(col(15), pR, "w", scale=0.125)
+    act(col(16), p8, "w", scale=15.875, bias=col(15))
+    for w, c in ((1, col(0)), (2, col(1)), (3, col(2)), (4, col(6)), (5, col(3)), (6, KEY)):
+        act(R("Bw", 144 * w, 144 * w + 144), R("Bw", 0, 144), "Bw", scale=c)
+    act(X("Gn"), X("Go"), "Gn", scale=col(10))
+    act(X("Gc"), X("Go"), "Gc", scale=-KEY)
+    act(X("I128"), Id, "I128", scale=128.0)
+    ts(X("eq"), X("trt"), pR, OP.is_gt, -8192.0, OP.mult, "tri")
+    ts(X("kl"), X("trt"), pR, OP.is_equal, 4096.0, OP.mult, "tri")
+    tt(X("tri"), X("eq"), X("kl"), OP.add, "tri")
+    ts(X("place"), X("J"), -1.0, OP.mult, col(12), OP.add, "place")
+    act(R("dq", 15, 128, 16), R("J", 0, 8), "dq", bias=col(17), scale=32.0)
+    act(R("lwf", 0, 8), R("J", 0, 8), "lw", bias=col(16), scale=2.0)
+    act(R("lwf", 8, 16), R("J", 0, 8), "lw", bias=pR, scale=16.0)
+    act(R("lw", 0, 16), R("lwf", 0, 16), "lw")
+    cp(R("vm", 0, 8), R("lwf", 0, 8), "vm0")
+    ts(R("vl", 0, 8), R("lwf", 8, 16), 512.0, OP.add, None, None, "vl0")
+    ts(R("xl", 0, 8), R("J", 0, 8), col(14), OP.add, None, None, "xl")
+    cp(R("xl", 8, 16), R("J", 0, 8), "xl")
+    ts(R("cw", 0, 16), R("J", 0, 16), 0.0, OP.mult, None, None, "cw")
+    ts(R("cw", 16, 24), R("J", 0, 8), 0.0, OP.mult, -float(OFF), OP.add, "cw")
+    ts(R("cw", 24, 32), R("lwf", 8, 16), float(WA - OFF), OP.add, None, None, "cw")
+    ts(R("cw", 32, 40), R("J", 0, 8), 0.0, OP.mult, 19.0 - OFF, OP.add, "cw")
+    act(R("nod", 0, 512), R("nod", 0, 512), "nod", scale=pO)
+    ts(X("NI"), X("NI"), 7, OP.bitwise_and, None, None, "NB")
+    ts(X("NB"), X("NI"), rh(2), OP.mult, col(8), OP.add, "NB")
+    act(R("NB", 19, 128, 32), R("J", 15, 19), "NB", bias=col(9), scale=rh(2))
+    cp(X("al"), IND(R("Ci", 0, 128), R("vm", 0, 8)), "a0")
+    cp(X("af"), R("Ci", 0, 128), "af0")
+    cp(R("Yl", 0, 120), R("fwi", 0, 120), "Yl0")
+    cp(R("Fl", 64, 120), R("fwi", 64, 120), "Fl0")
+    cp(R("thf", 0, 128, 1, 0, 8), R("thi", 0, 128, 1, 0, 8), "th")
+    acc(R("P7", 0, 8), [(R("Bt", 15 - r, 143 - r, 1, 0, 8), R("thf", r, 128, 16, 0, 8)) for r in range(16)], "thW")
+    act(R("th0", 0, 8), R("P7", 0, 8), "th", bias=-KEY)
+    cp(R("fwf", 0, 120), R("fwi", 0, 120), "fw")
+    act(R("fwf", 120, 160), R("J", 0, 40), "fw", bias=col(13), scale=16.0)
     for j in range(2):
-        acc(R("P6", j, 160, 2), [(R("MS", 256 * j, 256 * j + 128), R("fwf", 0, 160, 2)), (R("MS", 256 * j + 128, 256 * j + 256), R("fwf", 1, 160, 2))])
+        acc(R("P6", j, 160, 2), [(R("MS", 256 * j, 256 * j + 128), R("fwf", 0, 160, 2)), (R("MS", 256 * j + 128, 256 * j + 256), R("fwf", 1, 160, 2))], "fwM")
     V = R("t4", 0, 160)
 
     def fi(k):
         return R("FI", k, WD, 16)
-    act(V, R("P6", 0, 160), AF.Copy)
-    act(R("t1", 0, 160), V, AF.Identity, 24576.0 - 63.5)
-    act(R("t2", 0, 160), R("t1", 0, 160), AF.Identity, -192.0, 1.0 / 128)
-    act(fi(1), R("t2", 0, 160), AF.Copy)
-    act(R("t3", 0, 160), R("t2", 0, 160), AF.Copy, 0.0, -128.0)
-    tt(fi(0), R("t3", 0, 160), V, OP.add)
-    ts(fi(3), V, float(W0), OP.is_ge)
-    ts(R("t5", 0, 160), V, 1024.0, OP.is_ge)
-    tt(R("t5", 0, 160), R("t5", 0, 160), fi(3), OP.subtract)
-    for k in (2, 5, 6, 7):
-        act(fi(k), R("t5", 0, 160), AF.Copy)
-    act(V, R("t5", 0, 160), AF.Identity, 1.0, -1.0)
-    tt(fi(4), V, R("t2", 0, 160), OP.mult)
+    act(V, R("P6", 0, 160), "fi")
+    act(R("t1", 0, 160), V, "fi", bias=24576.0 - 63.5)
+    act(R("t2", 0, 160), R("t1", 0, 160), "fi", bias=-192.0, scale=1.0 / 128)
+    act(fi(1), R("t2", 0, 160), "fi")
+    act(R("t3", 0, 160), R("t2", 0, 160), "fi", scale=-128.0)
+    tt(fi(0), R("t3", 0, 160), V, OP.add, "fi")
+    ts(fi(3), V, float(W0), OP.is_ge, None, None, "fi")
+    ts(R("t5", 0, 160), V, 1024.0, OP.is_ge, None, None, "fi")
+    tt(R("t5", 0, 160), R("t5", 0, 160), fi(3), OP.subtract, "fi")
+    for k in (2, 5):
+        act(fi(k), R("t5", 0, 160), "fi")
+    act(V, R("t5", 0, 160), "fi", bias=1.0, scale=-1.0)
+    tt(fi(4), V, R("t2", 0, 160), OP.mult, "fi")
     for h in range(0, WD, 640):
-        add("v", [("transpose", (R("F0", h, h + 640), R("FI", h, h + 640)), {})], [R("FI", h, h + 640)], [R("F0", h, h + 640)], FIX + 320 * CY, name="tr")
-    act(R("F1", W0, WD), R("F0", W0, WD), AF.Copy)
-    for (a, b) in ((0, 960), (960, W0)):
-        act(R("YF", a, b), IND(R("Y", BS, YW), R("Yl", a // 16, b // 16)), AF.Copy, 0.0, 0.5, "YF")
-    act(X("own"), R("Y", BS, BS + 128), AF.Copy)
+        add("v", [("transpose", (R("F0", h, h + 640), R("FI", h, h + 640)), {})], [R("FI", h, h + 640)], [R("F0", h, h + 640)], "ftr")
+    gcopy(R("F1", W0, WD), R("F0", W0, WD), "F1")
+    for a in range(0, W0, 480):
+        act(R("YF", a, a + 480), IND(R("Y", BS, YW), R("Yl", a // 16, a // 16 + 30)), "YF0_", scale=0.5)
+    act(X("own"), R("Y", BS, BS + 128), "own0")
 
     for t in range(RO):
         last = t == RO - 1
@@ -360,175 +300,149 @@ def build():
         Lw = R("Li", 0, 2048) if t == 0 else R("L", 0, 2048)
         YFw = R("YF", 0, Wt)
         Fw = R(cur, 0, WD)
-        own = X("own")
-        acc(R("P0", 0, 128), [(own, Id)], "ownT")
-        act(X("oT"), R("P0", 0, 128), AF.Copy, 0.0, -1.0, "oT")
-        pieces = ((0, 512, "P0"), (512, 1024, "P1"), (1024, 1536, "P2"), (1536, 1792, "P3"), (1792, 2048, "P6"))
-        for (a, b, pb) in pieces:
-            q = a // 512
-            mm([(R(pb, 0, b - a), R("oT", 0, 128, 1, 32 * q, 32 * q + 32), R("E32", a % 512, a % 512 + b - a, 1, 32 * q, 32 * q + 32), True, False)], "dA")
-        for a in range(0, 2048, TM["C1"]):
-            ts(R("G", a, a + TM["C1"]), IND(Lw, R("al", a // 16, (a + TM["C1"]) // 16)), -float(OFF), OP.add, name="G1")
+        own, af = X("own"), X("af")
+        vl = R("vl", 8 * t, 8 * t + 8)
+        for a in range(0, 2048, 512):
+            if t == 0:
+                ts(R("G", a, a + 512), IND(Lw, R("al", a // 16, a // 16 + 32)), -float(OFF), OP.add, None, None, "G")
+            else:
+                act(R("G", a, a + 512), IND(Lw, R("al", a // 16, a // 16 + 32)), "G", bias=-float(OFF))
         for h in range(2):
             pb = "P%d" % (4 + h)
-            for j in range(2):
-                acc(R(pb, 64 * j, 64 * j + 64), [(R("DD", 2048 * j + k, 2048 * j + 2048, 16), R("G", 1024 * h + k, 1024 * h + 1024, 16))
-                                                 for k in range(16)], "ext")
-            ts(R("bc", 128 * h, 128 * h + 128), R(pb, 0, 128), float(OFF), OP.add, name="bc")
+            hb = R(pb, 0, 64)
+            acc(hb, [(R("DD", k, 2048, 16), R("G", 1024 * h + k, 1024 * h + 1024, 16)) for k in range(16)], "ext")
+            ts(R("bc", 128 * h, 128 * h + 64), hb, 1.0 / 4096, OP.mult, float(OFF), OP.add, "cl")
+            ts(R("c4", 64 * h, 64 * h + 64), hb, RND / 8, OP.add, -RND / 8, OP.add, "c4")
+            tt(R("bm", 64 * h, 64 * h + 64), hb, R("c4", 64 * h, 64 * h + 64), OP.subtract, "bm")
+            ts(R("bc", 128 * h + 64, 128 * h + 128), R("bm", 64 * h, 64 * h + 64), float(OFF), OP.add, None, None, "bc")
+        act(X("bl"), IND(X("bm"), R("xl", 0, 8)), "bl")
         if t == 0:
-            for h in range(0, 2048, 256):
-                cp(R("L", h, h + 256), R("Li", h, h + 256), "Lcv")
-            for h in range(0, 1024, 256):
-                cp(R("C", 512 + h, 768 + h), R("Ci", h, h + 256), "Ccv")
+            for h in range(0, 2048, 512):
+                gcopy(R("L", h, h + 512), R("Li", h, h + 512), "Lcv")
+            for h in range(0, 1024, 512):
+                gcopy(R("C", 512 + h, 1024 + h), R("Ci", h, h + 512), "Ccv")
         if not last:
-            act(R("C", S * t, S * t + S), pA, AF.Copy, name="Crm")
-        for (a, b, pb) in pieces:
+            gcopy(R("C", S * t, S * t + S), af, "Crm")
+        acc(R("P0", 0, 128), [(own, Id)], "ownT")
+        act(X("oT"), R("P0", 0, 128), "oT", scale=-1.0)
+        mm([(X("P7"), Id, X("place"), True, False)], "D_", "D")
+        for (a, b, pb) in PIECES:
+            mm([(R(pb, 0, b - a), X("oT"), R("E", a, b), True, False)], "dA", pb)
+        for (a, b, pb) in PIECES:
             o = 64 * (a // 1024)
             for (c, d) in ((a, b),) if a else ((0, 256), (256, 512)):
-                act(R("A", c, d), IND(YFw, R("bc", o + c // 16, o + d // 16)), AF.Identity, 1023.75, 1.0, "A")
+                act(R("A", c, d), IND(YFw, R("bc", o + c // 16, o + d // 16)), "A", bias=1023.75)
             tt(R("B", a, b), IND(YFw, R("bc", o + 64 + a // 16, o + 64 + b // 16)), R("A", a, b), OP.add, "B")
-            mm([(R(pb, 0, b - a), Id, R("B", a, b), False, True)], "dB")
-            act(R("ab", a, b), R(pb, 0, b - a), AF.Abs, -1024.0, 1.0, "abs")
-        for h in range(2):
-            pb = "P%d" % (4 + h)
-            act(R("pay", 256 + 64 * h, 320 + 64 * h), R(pb, 0, 64), AF.Copy, name="pay")
-            act(R("pay", 384 + 64 * h, 448 + 64 * h), R(pb, 64, 128), AF.Copy, name="pay")
-        if t > 0:
-            oN = R("OH", 256, 384)
-            acc(R("P0", 0, 128), [(X("m16"), oN)], "cnt")
-            act(X("f3"), R("P0", 0, 128), AF.Identity, -51080.0, -1.0, "thr")
-            acc(R("P0", 128, 256), [(X("m16"), oN), (Id, X("f3")), (X("Idf"), X("th16"))], "cnt")
-            act(R("key", 256, 384), R("P0", 128, 256), AF.Identity, 51200.0, 1.0, "thr")
-            acc(R("P2", 0, 128), [(X("Gb"), X("x2"))], "vb")
-            act(pV, R("P2", 0, 128), AF.Identity, col(12), col(10), "pv")
-            if not last:
-                act(X("f2"), R("P2", 0, 128), AF.Identity, -1533.5, -1.0, "alt")
-                acc(R("P2", 128, 256), [(X("Gb"), X("x2")), (Id, X("f2"))], "alt")
-                act(pAl, R("P2", 128, 256), AF.Identity, col(16 + t), rh(2), "alt")
+            mm([(R(pb, 0, b - a), Id, R("B", a, b), False, True)], "dB", pb)
+            act(R("ab", a, b), R(pb, 0, b - a), "abs", AF.Abs, -1024.0)
+            mm([(X("P7"), shift(6, r), R("ab", 128 * r, 128 * r + 128), False, r == 15) for r in range(a // 128, b // 128)], "D", "D")
+        for a in range(0, 2048, 512):
+            ts(R("yb", a, a + 512), R("B", a, a + 512), -1024.0, OP.add, None, None, "yb")
+        act(X("low"), own, "low", bias=-1.0)
+        acc(R("P5", 256, 384), [(Id, own), (Id, one)], "high")
         if not last:
-            ut = [(X("Go"), own)] + [(Id, one)] * (t + 1)
-            acc(R("P1", 0, 128), ut + [(X("Idf"), pA)], "u")
-            act(X("f1"), R("P1", 0, 128), AF.Identity, 1023.5 - 393216.0, -1.0, "dC")
-            acc(R("P1", 128, 256), ut + [(Id, X("f1"))], "u")
-            act(pD, R("P1", 128, 256), AF.Identity, 393216.0, 1.0, "dC")
-        if t > 0:
-            wstage(R("P3", 0, 56), 1, cur, 1024, W0, None, "Fg")
-            cp(R("Fl", 64, 120), R("P3", 0, 56), "Fl")
-        for (a, b) in TM["DS"]:
-            mm([(R("P7", k, 256, 16, a, b), R("ab", 16 * a + k, 16 * b, 16), R("ks", 0, 16), True, True) for k in range(16)], "D")
-        tt(R("key", 0, 256), R("P7", 0, 256), R("tie", 0, 256), OP.add, "key")
-        scan(R("mx", 0, 256), R("rs", 0, 256), R("key", 0, 256), OP.add, OP.max, "mx")
-        tt(R("OH", 0, 384), IND(R("mx", 0, 256), R("xl", 0, 24)), R("key", 0, 384), OP.is_le, "OH")
-        oP, oQ, oN = R("OH", 0, 128), R("OH", 128, 256), R("OH", 256, 384)
-        lo = 128 if last else 0
-        hi = 384 if last else 512
-        mm([(R("P5", 128 * j, 128 * j + 128), o, Id, True, True) for j, o in enumerate((oN, oN, oQ, oQ)) if 128 * j >= lo], "T1")
-        mm([(R("P6", 128 * j, 128 * j + 128), oP, Id, True, True) for j in range(hi // 128)], "T2")
-        tt(R("Z1", lo, 512), R("P5", lo, 512), R("pay", lo, 512), OP.mult, "Z1")
-        tt(R("Z2", 0, hi), R("P6", 0, hi), R("pay", 256, 256 + hi), OP.mult, "Z2")
-        wstage(R("P4", 0, 24), 0, "Z1", 128, 512, R("cw", 0, 24), "W1")
-        ts(R("l1", 0, 24), R("P4", 0, 24), float(OFF), OP.add, name="l1")
-        wstage(R("P7", 0, 24), 0, "Z2", 0, 384, R("cw", 24, 48), "W2")
-        ts(R("l2", 0, 24), R("P7", 0, 24), float(OFF), OP.add, name="l2")
-        vs, bq, cq, bp, cP, aP = R("l1", 0, 8), R("l1", 8, 16), R("l1", 16, 24), R("l2", 0, 8), R("l2", 8, 16), R("l2", 16, 24)
-        act(X("fq"), IND(Fw, bq), AF.Copy, name="fq")
-        cp(IND(Fw, vs), X("fq"), "F6")
+            acc(R("P5", 0, 128), [(X("Go"), own), (X("Idf"), af)], "u")
+            act(X("f1"), R("P5", 0, 128), "f1", bias=1022.5 - t - 393216.0, scale=-1.0)
+            acc(R("P5", 128, 256), [(X("Go"), own), (Id, X("f1"))], "u")
+            act(X("dC"), R("P5", 128, 256), "dC", bias=393217.0 + t)
+        scan(R("mx", 0, 128), X("P7"), X("dq"), BIG, OP.min, OP.add, "mx")
+        scan(R("mx", 128, 256), X("P7"), X("dp"), 0.0, OP.max, OP.mult, "mx")
+        cp(R("ki", 0, 16), R("mx", 15, 256, 16), "ki")
+        ts(R("kj", 0, 16), R("ki", 0, 16), 2047, OP.bitwise_and, None, None, "kj")
+        cp(R("jl", 0, 16), R("kj", 0, 16), "jl")
+        jq, jp = R("jl", 0, 8), R("jl", 8, 16)
+        tt(R("nf", 0, 8), R("mx", 143, 256, 16), R("thr" if t else "th0", 0, 8), OP.is_ge, "nf")
+        tt(R("X", 0, 8), R("nf", 0, 8), R("xb", 8 * t, 8 * t + 8), OP.mult, "X")
         nw = R("new", S * t, S * t + S)
-        if TM["NEWV"]:
-            acc(R("P0", 0, 128), [(Id, own), (X("nId"), one)], "dq")
-            acc(R("P0", 128, 256), [(Id, own), (Id, one)], "nw")
-            act(R("A2", 0, 128), IND(YFw, bq), AF.Identity, -0.25, 1.0, "A2")
-            tt(X("B4"), IND(YFw, cq), R("A2", 0, 128), OP.add, "B2")
-            tt(X("n1"), X("B4"), R("P0", 0, 128), OP.max, "sg")
-            tt(nw, X("n1"), R("P0", 128, 256), OP.min, "new")
-        else:
-            act(R("A2", 0, 128), IND(YFw, bq), AF.Identity, 1023.75, 1.0, "A2")
-            tt(X("B2"), IND(YFw, cq), R("A2", 0, 128), OP.add, "B2")
-            acc(R("P0", 0, 128), [(X("nId"), own), (Id, X("B2"))], "dq")
-            act(X("n1"), R("P0", 0, 128), AF.Sign, -1024.0, 1.0, "sg")
-            acc(R("P0", 128, 256), [(Id, own), (Id, X("n1"))], "nw")
-            act(nw, R("P0", 128, 256), AF.Copy, name="new")
+        tt(X("n1"), IND(R("yb", 0, 2048), jq), X("low"), OP.max, "n1")
+        tt(nw, X("n1"), R("P5", 256, 384), OP.min, "new")
         gh = GA if t % 2 == 0 else GB
-        add("g", [("send", (nw, gh, t), {})], [nw], [R("@%d" % t, 0, 1)], 1000, kind="s", name="send")
-        add("x", [("arr", (t,), {})], [R("@%d" % t, 0, 1)], [R("Y", gh, gh + 896)], 0, kind="x", lat=TM["ARR"], name="arr")
-        cp(IND(R("Y", RM, GB), R("vl", 0, 8)), nw, "Ysc")
-        act(R("A2", 128, 256), IND(YFw, bp), AF.Identity, 1023.75, 1.0, "A3")
-        tt(X("B3"), IND(YFw, cP), R("A2", 128, 256), OP.add, "B3")
-        acc(R("P3", 0, 128), [(Id, X("B3"))], "room")
-        act(R("Y", RM + S * t, RM + S * t + S), R("P3", 0, 128), AF.Identity, -1024.0, 1.0, "room")
+        add("g", [("send", (nw, gh, t), {})], [nw], [R("@%d" % t, 0, 1)], "send", kind="s")
+        add("x", [("arr", (t,), {})], [R("@%d" % t, 0, 1)], [R("Y", gh, gh + 896)], "arr", kind="x")
+        act(R("Y", RM + S * t, RM + S * t + S), IND(R("yb", 0, 2048), jp), "room")
+        cp(IND(R("Y", RM, GB), vl), nw, "Ysc")
+        Kw = R("K", 0, 2048)
+        tt(R("Z", 0, 128), IND(Kw, jq), X("bl"), OP.mult, "Zq")
         if not last:
-            act(X("x1"), IND(Fw, bp), AF.Copy, name="x1")
-            if TM["SCAN"]:
-                acc(R("P2", 0, 128), [(X("Gn"), X("x1"))], "Wx")
-                scan(X("sx"), X("pick"), R("P2", 0, 128), OP.add, OP.max, "sx")
-                ts(R("x1l", 0, 8), R("sx", 15, 128, 16), col(23), OP.add, name="x1l")
-            else:
-                wstage(R("P2", 0, 8), 1, "x1", 0, 128, None, "Wx")
-                cp(R("x1l", 0, 8), R("P2", 0, 8), "x1l")
-            tt(X("x2"), IND(Fw, R("x1l", 0, 8)), R("Z1", 0, 128), OP.mult, "x2")
-            acc(R("P3", 128, 256), [(X("Idf"), pA), (Id, R("Z2", 384, 512))], "cn")
-            act(X("cn"), R("P3", 128, 256), AF.Copy, name="cn")
-            cp(IND(R("C", 0, 1536), R("vl", 0, 8)), X("cn"), "Csc")
+            tt(R("Z", 128, 256), IND(Kw, jp), X("bl"), OP.mult, "Zp")
+        tt(R("Z", 256, 384), IND(Kw, jp), af, OP.mult, "Za")
+        mm([(R("P0", 0, 40), Id, R("cw", 0, 40), True, False), (R("P0", 24, 32), X("I128"), R("X", 0, 8), False, False),
+            (R("P0", 32, 40), Id, R("X", 0, 8), False, False)], "W_", "W")
+        mm([(R("P0", 0, 24), shift(0, r), R("Z", r, 384, 16), False, r == 15) for r in range(16)], "W", "W")
+        ts(R("l1", 0, 40), R("P0", 0, 40), float(OFF), OP.add, None, None, "l")
+        bq, bp, aP, vs, vb = [R("l1", 8 * k, 8 * k + 8) for k in range(5)]
+        act(X("fq"), IND(Fw, bq), "fq")
+        cp(IND(Fw, vs), X("fq"), "F6")
+        act(X("alp"), IND(R("NB", 32 * t, 32 * t + 32), vb), "alp")
+        if not last:
+            act(X("x1"), IND(Fw, bp), "x1")
+            rows(R("P2", 0, 8), 1, "x1", 0, 128, "Wx")
+            cp(R("x1l", 0, 8), R("P2", 0, 8), "x1l")
+            tt(X("x2"), IND(Fw, R("x1l", 0, 8)), X("alp"), OP.mult, "x2")
+            acc(R("P2", 8, 16), [(Id, R("lw", 0, 8))] + [(shift(4, r), R("x2", 16 * (r % 8) + r // 8, 16 * (r % 8) + 16, 2)) for r in range(16)], "Wm")
+            ts(R("vm", 0, 8), R("P2", 8, 16), 512.0, OP.add, None, None, "vm")
+            tt(X("Zc"), IND(Kw, jp), X("dC"), OP.mult, "Zc")
+            tt(IND(R("C", 0, 1536), vl), X("Zc"), af, OP.add, "Csc")
+            cp(X("al"), IND(R("C", 0, 1536), R("vm", 0, 8)), "a")
         for j, (a, e) in enumerate(((0, 1024), (W0, Wt))):
             if e > a:
-                wstage(R("P%d" % (5 + j), 0, (e - a) // 16), 1, cur, a, e, None, "Fx")
-                cp(R("Fl", a // 16, e // 16), R("P%d" % (5 + j), 0, (e - a) // 16), "Fl")
-        acc(R("P1", 0, 128), [(Id, X("tri")), (X("G1r"), R("Z1", 128, 256)), (X("Go"), R("Z2", 256, 384))], "ar")
-        act(X("ar"), R("P1", 0, 128), AF.Copy, 0.0, 1.0 / 4096, "ar")
-        act(R("aw", 0, 8), R("P7", 16, 24), AF.Identity, OFF / 4096.0, 1.0 / 4096, "aw")
-        tt(X("eq"), IND(R("aw", 0, 8), R("xl", 24, 32)), X("ar"), OP.is_equal, "eq")
-        scan(X("kl"), X("keep"), X("eq"), OP.mult, OP.max, "kl")
+                rows(R("P%d" % (3 + j), 0, (e - a) // 16), 1, cur, a, e, "Fx")
+                cp(R("Fl", a // 16, e // 16), R("P%d" % (3 + j), 0, (e - a) // 16), "Fl")
+        acc(R("P1", 0, 128), [(Id, X("tri")), (X("Go"), R("Z", 256, 384)), (X("Gn"), X("alp"))], "arM")
+        act(X("ar"), R("P1", 0, 128), "ar", scale=1.0 / 4096)
+        ts(R("aw", 0, 8), aP, 1.0 / 4096, OP.mult, None, None, "aw")
+        tt(X("eq"), IND(R("aw", 0, 8), R("xl", 8, 16)), X("ar"), OP.is_equal, "eq")
+        scan(X("kl"), X("keep"), X("eq"), 0.0, OP.mult, OP.max, "kl")
         tt(R("kt", 0, 8), R("kl", 15, 128, 16), R("aw", 0, 8), OP.add, "kt")
-        ts(R("sl", 0, 16, 2), R("kt", 0, 8), 4096.0, OP.mult, col(21), OP.min, name="sl")
-        act(X("lv"), IND(R("L", 0, 2048), aP), AF.Copy, name="lv")
+        ts(R("sl", 0, 16, 2), R("kt", 0, 8), 4096.0, OP.mult, col(11), OP.min, "sl")
+        act(X("lv"), IND(R("L", 0, 2048), aP), "lv")
         for c in range(7, -1, -1):
             tt(IND(R("L", 0, 2064), R("sl", 2 * c, 2 * c + 1)), R("lv", 16 * c, 16 * c + 16), R("nod", S * t + 16 * c, S * t + 16 * c + 16), OP.max, "Lsc")
         if t == 0:
-            dma("s", R("lo", 0, 2048, 1, 0, 128, 2), R("L", 0, 2048, 1, 0, 128, 2), 524288, "st_le")
+            dma("s", R("lo", 0, 2048, 1, 0, 128, 2), R("L", 0, 2048, 1, 0, 128, 2), "st_le")
         if last:
-            dma("s", R("lo", 0, 2048, 1, 1, 128, 2), R("L", 0, 2048, 1, 1, 128, 2), 524288, "st_lo")
-            dma("s", R("yo", 0, 1024), R("Y", BS, GB), 262144, "st_yb")
-            dma("s", R("yo", W0, WA), R("Y", RM, BS), 131072, "st_yr")
-            dma("s", R("yo", 1024, W0), R("Y", GB, YW), 229376, "st_yg")
+            dma("s", R("lo", 0, 2048, 1, 1, 128, 2), R("L", 0, 2048, 1, 1, 128, 2), "st_lo")
+            dma("s", R("yo", 0, 1024), R("Y", BS, GB), "st_yb")
+            dma("s", R("yo", W0, WA), R("Y", RM, BS), "st_yr")
+            dma("s", R("yo", 1024, W0), R("Y", GB, YW), "st_yg")
         else:
-            if TM["SCAN"]:
-                acc(R("P2", 128, 256), [(Id, X("Jb")), (X("Gv"), X("x2"))], "Wv")
-                scan(X("sv2"), X("pick"), R("P2", 128, 256), OP.add, OP.max, "sv")
-                ts(R("vl", 0, 8), R("sv2", 15, 128, 16), col(24), OP.add, name="vl")
-            else:
-                wstage(R("P2", 8, 16), 4, "x2", 0, 128, R("lw", 0, 8), "Wv")
-                ts(R("vl", 0, 8), R("P2", 8, 16), 512.0, OP.add, name="vl")
-            cp(X("al"), IND(R("C", 0, 1536), R("vl", 0, 8)), "a")
-            act(pA, IND(R("C", 0, 1536), R("vl", 0, 8)), AF.Copy, name="af")
-            act(own, IND(R("Y", RM, GB), R("vl", 0, 8)), AF.Copy, name="own")
-        for (a, b) in ((1024, 1472), (1472, W0), (W0, Wt), (0, 512), (512, 1024)):
+            vn = R("vl", 8 * t + 8, 8 * t + 16)
+            rows(R("P0", 64, 72), 4, "x2", 0, 128, "Wv", R("lw", 8, 16))
+            rows(R("P0", 72, 80), 5, "x2", 0, 128, "Wb")
+            ts(vn, R("P0", 64, 72), 512.0, OP.add, None, None, "vl")
+            act(R("xb", 8 * t + 8, 8 * t + 16), R("P0", 72, 80), "xb", bias=-19.0)
+            act(af, IND(R("C", 0, 1536), vn), "af")
+            act(own, IND(R("Y", RM, GB), vn), "own")
+        for (a, b) in ((1024, 1472), (1472, W0), (0, 512), (512, 1024), (W0, Wt)):
             if b > a:
-                act(R(nxt, a, b), IND(Fw, R("Fl", a // 16, b // 16)), AF.Copy, name="G")
+                act(R(nxt, a, b), IND(Fw, R("Fl", a // 16, b // 16)), "FF")
         if not last:
-            win = R("Y", GA, GB) if t % 2 == 0 else R("Y", RM, YW)
-            for j, (a, e) in enumerate(((1024, Wn), (0, 1024))):
-                pb = "P%d" % (6 - j)
-                n = (e - a) // 16
-                wstage(R(pb, 0, n), 3 if t % 2 == 0 else 2, nxt, a, e, None, "Gx")
-                ts(R("Yl", a // 16, e // 16), R(pb, 0, n), 1408.0 if t % 2 == 0 else 512.0, OP.add, name="Yl")
+            acc(R("P1", 448, 449), [(X("Gc"), R("nf", c, c + 1)) for c in range(8)], "cnt")
+            ts(R("am", 0, 1), R("P1", 448, 449), -7.5 * KEY, OP.add, RND, OP.add, "am")
+            ts(R("am", 1, 2), R("am", 0, 1), -RND, OP.add, R("P1", 448, 449), OP.subtract, "am")
+            act(R("thr", 0, 8), R("th0", 0, 8), "thr", bias=R("am", 1, 2))
+            rows(R("P1", 384, 440), 1, nxt, 1024, W0, "Fg")
+            cp(R("Fl", 64, 120), R("P1", 384, 440), "Flg")
+        win = R("Y", GA, GB) if t % 2 == 0 else R("Y", RM, YW)
+        for j, (a, e) in enumerate(((1024, Wn), (0, 1024))):
+            pb = ("P6", "P3")[j]
+            n = (e - a) // 16
+            rows(R(pb, 0, n), 1 if last else 3 - t % 2, nxt, a, e, "Gx")
+            if last:
+                act(R("fof", a // 16, e // 16), R(pb, 0, n), "fo")
+            else:
+                ts(R("Yl", a // 16, e // 16), R(pb, 0, n), 1408.0 if t % 2 == 0 else 512.0, OP.add, None, None, "Yl")
                 for (c, d) in ((a, a + 512), (a + 512, e)):
-                    act(R("YF", c, d), IND(win, R("Yl", c // 16, d // 16)), AF.Copy, 0.0, 0.5, "YF")
-        else:
-            for j, (a, e) in enumerate(((1024, WA), (0, 1024))):
-                pb = "P%d" % (6 - j)
-                n = (e - a) // 16
-                wstage(R(pb, 0, n), 1, nxt, a, e, None, "Gx")
-                act(R("fof", a // 16, e // 16), R(pb, 0, n), AF.Copy, name="fo")
-            dma("a", R("fo", 0, 152), R("fof", 0, 152), 77824, "st_f")
+                    act(R("YF", c, d), IND(win, R("Yl", c // 16, d // 16)), "YF", scale=0.5)
+        if last:
+            dma("a", R("fo", 0, 152), R("fof", 0, 152), "st_f")
     return ops
 
 
 def meet(x, y, same):
-    if x[1] != y[1]:
-        return False
     if x[1][0] == "P" and not same:
         return True
-    return x[2] < y[3] and y[2] < x[3] and x[5] < y[6] and y[5] < x[6]
+    return x[2] < y[3] and y[2] < x[3] and x[5] < y[6] and y[5] < x[6] and (x[4] != y[4] or (x[2] - y[2]) % x[4] == 0)
 
 
 def links(ops):
@@ -541,6 +455,9 @@ def links(ops):
                     same = ops[j]["eng"] == "p" and o["eng"] == "p"
                     if (w or w0 or (x[1][0] == "P" and not same)) and meet(x, y, same):
                         pre.add(j)
+        if o["group"]:
+            pre |= set([j for j in range(i) if ops[j]["group"] == o["group"] and ops[j]["t"] == o["t"]][-1:])
+        o["soft"] = [j for j in pre if o["group"] and ops[j]["group"] == o["group"] and ops[j]["t"] == o["t"]]
         o["pre"] = sorted(pre)
         for w0, xs in ((False, o["rd"]), (True, o["wr"])):
             for x in xs:
@@ -552,206 +469,35 @@ def links(ops):
                 hist[x[1]] = h + [(i, x, w0)]
 
 
-def costs(change):
-    keep = dict(TM)
-    TM.update(change)
+def plan(first=None, mid=None, end=None):
     ops = build()
-    c = ([o["dur"] for o in ops], [o["alt"][1] if "alt" in o else None for o in ops], [o["lat"] for o in ops], TM["HOP"], TM["HOPS"])
-    TM.update(keep)
-    return ops, c
-
-
-def place(prio, pre, eng, c, lead, back, lean):
-    dur, alt, lat, hop, hops = c
-    n = len(prio)
-    st = [None] * n
-    en = [0.0] * n
-    eng = list(eng)
-    busy = {}
-    for i0 in sorted(range(n), key=lambda k: prio[k]):
+    links(ops)
+    at = {(o["t"], o["name"]): i for i, o in enumerate(ops)}
+    want = []
+    for t, names in ((-1, first or FIRST), (0, mid or ROUND), (1, mid or ROUND), (2, mid or ROUND), (3, end or LAST)):
+        for w in names.split():
+            e, nm = w.split(":") if ":" in w else (None, w)
+            i = at.get((t + 1, nm[:-1]) if nm[-1] == "+" else (t, nm))
+            if i is not None:
+                want.append(i)
+                if e == "v" and "alt" in ops[i]:
+                    ops[i]["eng"] = "v"
+                    ops[i]["calls"] = ops[i]["alt"]
+    order = []
+    done = set()
+    for i0 in want + list(range(len(ops))):
         stack = [i0]
         while stack:
             i = stack[-1]
-            if st[i] is not None:
-                stack.pop()
-                continue
-            miss = [j for j in pre[i] if st[j] is None]
+            miss = [j for j in ops[i]["pre"] if j not in done]
             if miss:
-                stack += sorted(miss, key=lambda k: -prio[k])
-                continue
-            stack.pop()
-            best = None
-            for e in (("a", "v") if lean is not None and alt[i] is not None else (eng[i],)):
-                d = alt[i] if e == "v" and alt[i] is not None else dur[i]
-                t0 = lead[i]
-                for j in pre[i]:
-                    x = en[j] + (lat[i] if back else lat[j]) + (hops if eng[j] == e else hop)
-                    if x > t0:
-                        t0 = x
-                A, B = busy.setdefault(e, ([], []))
-                k = len(A)
-                while k > 0 and B[k - 1] > t0:
-                    k -= 1
-                while k < len(A) and t0 + d > A[k]:
-                    if B[k] > t0:
-                        t0 = B[k]
-                    k += 1
-                v = t0 + d + (lean[i] if lean is not None and e == "v" else 0.0)
-                if best is None or v < best[0]:
-                    best = (v, e, k, t0, d)
-            v, e, k, t0, d = best
-            busy[e][0].insert(k, t0)
-            busy[e][1].insert(k, t0 + d)
-            st[i] = t0
-            en[i] = t0 + d
-            eng[i] = e
-    return st, en, eng
-
-
-def replay(order, pre, eng, c, arcs=False):
-    dur, alt, lat, hop, hops = c
-    en = [0.0] * len(order)
-    by = [None] * len(order)
-    prev = {}
-    end = 0.0
-    top = 0
-    for i in order:
-        e = eng[i]
-        b = prev.get(e)
-        t0 = 0.0 if b is None else en[b]
-        for j in pre[i]:
-            x = en[j] + lat[j] + (hops if eng[j] == e else hop)
-            if x > t0:
-                t0 = x
-                b = j
-        en[i] = t0 + (alt[i] if e == "v" and alt[i] is not None else dur[i])
-        by[i] = b
-        prev[e] = i
-        if en[i] + lat[i] > end:
-            end = en[i] + lat[i]
-            top = i
-    if not arcs:
-        return end
-    out = []
-    while by[top] is not None:
-        if by[top] not in pre[top]:
-            out.append((by[top], top))
-        top = by[top]
-    return out or [(order[0], order[1])]
-
-
-def plan():
-    ops, c0 = costs({})
-    links(ops)
-    cs = [c0] + [costs(v)[1] for v in VARIANTS]
-    n = len(ops)
-    pre = [o["pre"] for o in ops]
-    post = [[] for _ in range(n)]
-    for i in range(n):
-        for j in pre[i]:
-            post[j].append(i)
-    rank = [0.0] * n
-    for i in range(n - 1, -1, -1):
-        rank[i] = max([rank[k] + c0[3] for k in post[i]] + [0.0]) + c0[2][i] + c0[0][i]
-    zero = [0.0] * n
-    eng0 = [o["eng"] for o in ops]
-    rng = np.random.default_rng(TM["SEED"])
-
-    def score(st, eng):
-        order = sorted(range(n), key=lambda k: (st[k], k))
-        v = [replay(order, pre, eng, c) for c in cs]
-        return sum(v) / len(v), v, order, st, eng
-
-    def both(st, en, eng):
-        rs, re_, _ = place([-x for x in en], post, eng, c0, c0[2], True, None)
-        return place([-x for x in re_], pre, eng, c0, zero, False, None)
-    lean = [TM["LEAN"]] * n
-    if len(START) == 2 * n:
-        z = [LETTERS.index(START[2 * i]) * 52 + LETTERS.index(START[2 * i + 1]) for i in range(n)]
-        st, en, eng = place([x // 2 for x in z], pre, ["v" if x % 2 and a is not None else e for x, e, a in zip(z, eng0, c0[1])], c0, zero, False, None)
-    else:
-        st, en, eng = both(*place([-r for r in rank], pre, eng0, c0, zero, False, lean))
-    best = score(st, eng)
-    seen = {}
-    same = {}
-    for i, o in enumerate(ops):
-        k = (o["t"], o["name"])
-        seen[k] = seen.get(k, 0) + 1
-        same.setdefault((o["name"], seen[k]) if o["t"] >= 0 else i, []).append(i)
-    kin = [None] * n
-    for v in same.values():
-        for i in v:
-            kin[i] = v
-    mark = [i for i, o in enumerate(ops) if o["name"] == "OH"]
-    now = best
-    for it in range(TM["ITA"]):
-        st, eng = now[3], list(now[4])
-        prio = list(st)
-        moves = []
-        if it == 0:
-            moves = [(i, st[i] - st[mark[2]], eng[i]) for i in range(n) if ops[i]["t"] == 2]
-        else:
-            arcs = replay(now[2], pre, now[4], cs[int(rng.integers(len(cs)))], True)
-            for _ in range(1 + int(rng.integers(2))):
-                j, i = arcs[int(rng.integers(len(arcs)))]
-                z = rng.random()
-                k = j if z < 0.15 or z >= 0.65 else i
-                e = eng[k]
-                p = st[k]
-                if z < 0.3 and c0[1][k] is not None:
-                    e = "v" if e == "a" else "a"
-                elif k == i:
-                    p = st[j] - 1 - 500 * rng.random() * (rng.random() < 0.3)
-                else:
-                    p = st[i] + 1 + 1500 * rng.random() * (rng.random() < 0.5)
-                moves.append((k, p - st[mark[max(ops[k]["t"], 0)]], e))
-        for (k, p, e) in moves:
-            for i in kin[k]:
-                prio[i] = st[mark[max(ops[i]["t"], 0)]] + p
-                eng[i] = e
-        st, en, eng = place(prio, pre, eng, c0, zero, False, None)
-        if rng.random() < TM["BOTH"]:
-            st, en, eng = both(st, en, eng)
-        sc = score(st, eng)
-        if it == 0 or sc[0] <= now[0] + TM["HEATA"] * (1 - it / TM["ITA"]) * rng.exponential():
-            now = sc
-            if sc[0] < best[0]:
-                best = sc
-    now = best
-    for it in range(TM["IT"]):
-        if rng.random() < TM["AIM"]:
-            arcs = replay(now[2], pre, now[4], cs[int(rng.integers(len(cs)))], True)
-            prio = list(now[3])
-            eng = list(now[4])
-            for _ in range(1 + int(rng.integers(2))):
-                j, i = arcs[int(rng.integers(len(arcs)))]
-                z = rng.random()
-                k = j if z < 0.2 else i
-                if z < 0.3 and c0[1][k] is not None:
-                    eng[k] = "v" if eng[k] == "a" else "a"
-                elif z < 0.65:
-                    prio[i] = prio[j] - 1 - 500 * rng.random() * (rng.random() < 0.3)
-                else:
-                    prio[j] = prio[i] + 1 + 1500 * rng.random() * (rng.random() < 0.5)
-        else:
-            bst = np.array(now[3])
-            near = np.abs(bst - rng.random() * bst.max()) < TM["WIN"][int(rng.integers(3))]
-            prio = (bst + near * rng.normal(0, TM["AMP"][int(rng.integers(3))], n)).tolist()
-            flip = near & (rng.random(n) < TM["FLIP"][int(rng.integers(3))])
-            eng = [("v" if e == "a" else "a") if flip[i] and c0[1][i] is not None else e for i, e in enumerate(now[4])]
-        st, en, eng = place(prio, pre, eng, c0, zero, False, None)
-        if rng.random() < TM["BOTH"]:
-            st, en, eng = both(st, en, eng)
-        sc = score(st, eng)
-        if sc[0] <= now[0] + TM["HEAT"] * (1 - it / TM["IT"]) * rng.exponential():
-            now = sc
-            if sc[0] < best[0]:
-                best = sc
-    for i, o in enumerate(ops):
-        if best[4][i] != o["eng"]:
-            o["eng"] = "v"
-            o["calls"], o["dur"] = o["alt"]
-    return ops, best[2], best[3], best[1], (pre, best[4])
+                stack.append(miss[0])
+            else:
+                stack.pop()
+                if i not in done:
+                    done.add(i)
+                    order.append(i)
+    return ops, order
 
 
 PLAN = []
@@ -760,9 +506,13 @@ PLAN = []
 def helpers(T, topo, r):
     core = T.cores[r]
     far = [k for k in range(N) if topo.chip(T.cores[k]) != topo.chip(core)]
-    aides = [c for c in topo.cores_of(core) if topo.die(c) == topo.die(core) and T.rank_of(c) is None][:TM["HELP"]]
+    aides = [c for c in topo.cores_of(core) if topo.die(c) == topo.die(core) and T.rank_of(c) is None][:HELP]
     m = len(far) // (len(aides) + 1)
     return aides, [far[m * j:m * j + m] for j in range(len(aides) + 1)]
+
+
+def dst(topo, c):
+    return DstId(rid=topo.addr(c)[0], pnc=topo.addr(c)[1])
 
 
 def rank_program(g, core, T, topo):
@@ -777,7 +527,7 @@ def rank_program(g, core, T, topo):
                     gh = GA if t % 2 == 0 else GB
                     g.wait_ge(T.sem["hop%d" % t], len(topo.engines(T.cores[r], core)))
                     at = [gh + S * ((r - k - 1) % N) for k in grp]
-                    g.remote_dma_fused([RemoteDMATransfer(dst_ids=[DstId(rid=topo.addr(T.cores[k])[0], pnc=topo.addr(T.cores[k])[1]) for k in grp],
+                    g.remote_dma_fused([RemoteDMATransfer(dst_ids=[dst(topo, T.cores[k]) for k in grp],
                                                           dma_engine_mask=sum(1 << k for k in eng), remote_sem=T.sem["arr%d" % t],
                                                           srcs=[T.new[:, S * t:S * t + S]], dsts=[T.Y[:, a:a + S] for a in at])], local_sem=T.sem.sent)
                 g.wait_ge(T.sem.sent, RO * len(eng))
@@ -786,14 +536,14 @@ def rank_program(g, core, T, topo):
     mine = shares[0]
     if not PLAN:
         PLAN.append(plan())
-    ops, order = PLAN[0][:2]
+    ops, order = PLAN[0]
     q = {"v": g.vector, "a": g.scalar, "p": g.tensor, "g": g, "s": g.sync}
     csem = {"v": "sv", "a": "sa", "p": "sp", "g": "sg"}
     peers = [r for r in range(N) if r != rank]
     far = [r for r in peers if topo.chip(T.cores[r]) != topo.chip(core)]
     near = [r for r in peers if r not in far]
     fe = [e for e in topo.engines(core, T.cores[far[0]]) if all(e in topo.engines(core, T.cores[r]) for r in far)]
-    ne = [e for e in topo.engines(core, T.cores[near[0]]) if e not in fe][:8 if aides else 4]
+    ne = [e for e in topo.engines(core, T.cores[near[0]]) if e not in fe]
     arrive = len(far) * len(fe) + len(near) * len(ne)
     done = {}
     total = {}
@@ -815,26 +565,23 @@ def rank_program(g, core, T, topo):
             continue
         need = {}
         for j in o["pre"]:
-            s, v = done[j]
-            need[s] = max(need.get(s, 0), v)
+            if j not in o["soft"]:
+                s, v = done[j]
+                need[s] = max(need.get(s, 0), v)
         for s in sorted(need):
             wait(e, s, need[s])
         if o["kind"] == "s":
             src, gh, t = o["calls"][0][1]
+            he = topo.engines(core, aides[0])
+            g.remote_dma_fused([RemoteDMATransfer(dst_ids=[dst(topo, h) for h in aides], dma_engine_mask=sum(1 << k for k in he),
+                                                  remote_sem=T.sem["hop%d" % t], srcs=[ap(T, src)], dsts=[ap(T, src) for h in aides])], local_sem=T.sem.sent)
             trs = []
-            if aides:
-                he = topo.engines(core, aides[0])
-                g.remote_dma_fused([RemoteDMATransfer(dst_ids=[DstId(rid=topo.addr(h)[0], pnc=topo.addr(h)[1]) for h in aides],
-                                                      dma_engine_mask=sum(1 << k for k in he), remote_sem=T.sem["hop%d" % t],
-                                                      srcs=[ap(T, src)], dsts=[ap(T, src) for h in aides])], local_sem=T.sem.sent)
-                total["sent"] = total.get("sent", 0) + len(he)
             for grp, eng in ((mine, fe), (near, ne)):
-                ids = [DstId(rid=topo.addr(T.cores[r])[0], pnc=topo.addr(T.cores[r])[1]) for r in grp]
                 at = [gh + S * ((rank - r - 1) % N) for r in grp]
-                trs.append(RemoteDMATransfer(dst_ids=ids, dma_engine_mask=sum(1 << k for k in eng), remote_sem=T.sem["arr%d" % t],
-                                             srcs=[ap(T, src)], dsts=[T.Y[:, a:a + S] for a in at]))
+                trs.append(RemoteDMATransfer(dst_ids=[dst(topo, T.cores[r]) for r in grp], dma_engine_mask=sum(1 << k for k in eng),
+                                             remote_sem=T.sem["arr%d" % t], srcs=[ap(T, src)], dsts=[T.Y[:, a:a + S] for a in at]))
             g.remote_dma_fused(trs, local_sem=T.sem.sent)
-            total["sent"] = total.get("sent", 0) + len(fe) + len(ne)
+            total["sent"] = total.get("sent", 0) + len(he) + len(fe) + len(ne)
             done[i] = ("sent", total["sent"])
         elif o["kind"] == "d":
             s = "d%d" % nd[0]

@@ -10,6 +10,10 @@ OFF = 1216
 BIG = 1.0e9
 KEY = 2048.0
 RND = 1.5 * 2.0 ** 38
+PACK = True
+SC = 4
+YBP = ((0, 1024), (1024, 1536), (1536, 2048))
+FFP = ((1024, 1472), (1472, W0), (0, 512), (512, 768), (768, 1024))
 HELP = 2
 PIECES = ((0, 512, "P0"), (512, 1024, "P1"), (1024, 1536, "P2"), (1536, 1792, "P3"), (1792, 1920, "P6"), (1920, 2048, "P4"))
 
@@ -22,9 +26,9 @@ SCRATCH = {
     "Y": sb(YW, "bfloat16"), "YF": sb(WA, "bfloat16"), "F0": sb(WD, "bfloat16"), "F1": sb(WD, "bfloat16"),
     "FI": sb(WD, "bfloat16"), "Li": sb(2048, "int32"), "L": sb(2064, "float32"), "Ci": sb(1024, "int32"),
     "C": sb(1536, "float32"), "fwi": sb(120, "int32"), "fwf": sb(160, "float32"), "thi": sb(128, "int32"),
-    "thf": sb(128, "float32"), "th0": sb(8, "float32"), "thr": sb(8, "float32"), "am": sb(8, "float32"),
-    "DD": sb(2048, "bfloat16"), "c4": sb(128, "float32"), "E": sb(2048, "bfloat16"), "K": sb(2048, "bfloat16"),
-    "J": sb(144, "float32"), "JG": sb(128, "float32"), "Jm": sb(128, "bfloat16"), "Im": sb(128, "bfloat16"),
+    "thf": sb(128, "float32"), "th0": sb(16, "float32"), "thr": sb(8, "float32"), "am": sb(8, "float32"),
+    "DD": sb(4096, "bfloat16"), "c4": sb(128, "float32"), "E": sb(2048, "bfloat16"), "K": sb(2048, "bfloat16"),
+    "J": sb(152, "float32"), "JG": sb(128, "float32"), "Jm": sb(128, "bfloat16"), "Im": sb(128, "bfloat16"),
     "pi": sb(8, "int32"), "pf": sb(8, "float32"), "RH": sb(16, "float32"), "col": sb(24, "float32"),
     "Id": sb(128, "bfloat16"), "Idf": sb(128, "float32"), "R5": sb(128, "bfloat16"), "Go": sb(128, "bfloat16"),
     "Gc": sb(128, "bfloat16"), "Gn": sb(128, "bfloat16"), "I128": sb(128, "bfloat16"),
@@ -34,12 +38,12 @@ SCRATCH = {
     "lwf": sb(24, "float32"), "xl": sb(24, "uint16"), "NI": sb(128, "int32"), "NB": sb(128, "bfloat16"),
     "t1": sb(160, "bfloat16"), "t2": sb(160, "float32"), "t3": sb(160, "float32"), "t4": sb(160, "float32"), "t5": sb(160, "float32"),
     "Fl": sb(160, "uint16"), "Yl": sb(160, "uint16"), "vm": sb(8, "uint16"), "vl": sb(32, "uint16"), "xb": sb(32, "bfloat16"),
-    "al": sb(128, "uint16"), "G": sb(2048, "float16"), "bc": sb(256, "uint16"), "bm": sb(128, "float32"), "bl": sb(128, "float32"),
-    "af": sb(128, "float32"), "dC": sb(128, "float32"), "f1": sb(128, "bfloat16"), "Z": sb(384, "float16"), "Zc": sb(128, "float32"),
+    "al": sb(128, "uint16"), "G": sb(2048, "float16"), "bc": sb(256, "uint16"), "bm": sb(128, "float32"), "bl": sb(128, "float16"),
+    "af": sb(128, "float32"), "c3": sb(128, "bfloat16"), "oP": sb(128, "bfloat16"), "f1": sb(128, "bfloat16"), "Z": sb(384, "float16"), "Zc": sb(128, "float32"),
     "A": sb(2048, "float32"), "B": sb(2048, "float16"), "ab": sb(2048, "bfloat16"), "yb": sb(2048, "bfloat16"),
     "own": sb(128, "bfloat16"), "oT": sb(128, "bfloat16"), "low": sb(128, "bfloat16"),
-    "mx": sb(256, "float32"), "ki": sb(16, "int32"), "kj": sb(16, "int32"), "jl": sb(16, "uint16"),
-    "nf": sb(8, "bfloat16"), "X": sb(8, "bfloat16"), "l1": sb(40, "uint16"), "fq": sb(128, "bfloat16"),
+    "mx": sb(256, "int32"), "ki": sb(16, "int32"), "kj": sb(16, "int32"), "jl": sb(16, "uint16"),
+    "nf": sb(16, "bfloat16"), "X": sb(8, "bfloat16"), "l1": sb(40, "uint16"), "fq": sb(128, "bfloat16"),
     "x1": sb(128, "bfloat16"), "x1l": sb(8, "uint16"), "x2": sb(128, "bfloat16"), "alp": sb(128, "bfloat16"),
     "n1": sb(128, "bfloat16"), "new": sb(512, "bfloat16"),
     "aw": sb(8, "float32"), "ar": sb(128, "float32"), "eq": sb(128, "float32"), "kl": sb(128, "float32"), "kt": sb(8, "float32"),
@@ -53,6 +57,21 @@ SEMAPHORES = ["sv", "sa", "sp", "sg", "sent"] + ["arr%d" % t for t in range(RO)]
 FIRST = "m_Y ld_y ld_c0 i_p ld_f ld_t ld_l i_p5 m_sl i_Bt m_xb pi pi4 pi3 pi2 i_J pi1 m_one pf m_L i_one v:w13 pf1 cw RH w11 xl1 pf2 i_Jm w12 m_FI w15 w16 w14 s_MS1 w17 cw3 K Id w lw1 R5 lw cw1 I128 v:w10 K1 w1 w4 w3 i_dq lw2 w7 Im m_DD w2 place w8 s_MS2 s_Bt xl w9 m_FI1 E8 K2 w5 s_MS E11 R51 fw1 dq m_DD1 w6 i_JG own0 DD2 DD v:DD3 i_NI ownT+ v:K3 E6 E3 v:E10 E12 v:low+ i_trt DD1 v:K4 m_FI2 DD4 DD6 E5 s_dp v:DD7 Bw K5 E14 E7 vm0 v:E9 v:DD5 s_MS3 Go v:E13 Bw6 v:Bw1 NB K6 s_Idf tri1 m_FI3 Bw4 i_nod m_C K7 tri cw2 v:Bw3 th s_keep E4 NB1 Bw2 v:E2 a0 E15 ld_c vl0 Lcv+ Bw5 af0 E Gc fw Yl0 G3+ E1 fwM fwM1 nod Lcv2+ thW Gn NB2 Fl0 YF0_2 v:fi fi6 G1+ YF0_ oT+ Lcv1+ G+ fi1 YF0_3 dA4+ dA1+ dA3+ Crm+ G2+ th1 ext+ fi2 Ccv1+ YF0_1 ext1+ dA2+ fi7 D_+ cl+ tri2 v:fi4 fi3 Ccv+ c4+ dA+ A2+ fi8 bm+ cl1+ bc+ c41+ dA5+ fi5 A1+ bm1+ Lcv3+ B1+ A+ high+ u+ A4+ A5+ bc1+ B+ A3+ B4+ dB+ B3+ fi9 dB4+ bl+ B2+ f1+ dB3+ fi11 dB1+ A6+ u1+ fi10 fi12 abs+ dB2+ B5+ ftr abs1+ ftr2 dB5+ D+ yb2+ abs2+ D1+ ftr1 yb1+ yb+ abs3+ D2+ dC+ abs4+ D3+ abs5+ D4+ yb3+ F1 D5+ ftr3"
 ROUND = "mx mx1 ki nf D_+ kj X jl Zp Zq Za W_ room n1 W Zc new l Ysc fq alp aw F6 lv arM arr Csc ar Fx v:x1 cnt eq Wx FF1 Fl kl am kt send FF Fx1 am1 sl x1l FF2 Lsc x2 Fg Lsc1 Fl1 Lsc2 Wm thr Lsc3 FF4 Flg Lsc4 FF3 Wb Lsc5 vm Lsc6 a Wv Lsc7 v:G+ G2+ Gx vl Gx1 Yl G3+ v:G1+ own Yl1 YF1 v:YF v:xb ext+ ext1+ v:YF2 YF3 ownT+ cl+ cl1+ low+ c4+ c41+ oT+ bm+ A+ v:A1+ bc+ dA+ af bm1+ A2+ dA5+ dA3+ v:A4+ dA4+ high+ dA1+ bc1+ B+ dA2+ A3+ u+ B1+ st_le dB+ A6+ bl+ B2+ A5+ dB1+ f1+ abs+ u1+ B3+ Crm+ abs1+ dB2+ B4+ D+ B5+ dB3+ abs2+ dB4+ v:dC+ D1+ yb2+ dB5+ abs3+ yb1+ D2+ abs4+ yb+ abs5+ D3+ yb3+ D4+ D5+"
 LAST = "mx mx1 ki nf kj X jl W_ Za room Zq n1 W send l v:fq alp aw lv F6 new arM arr Ysc ar Fx1 FF1 eq Fx st_yb st_yr kl FF Fl1 kt sl Fl Lsc Lsc1 Lsc2 Lsc3 Lsc4 FF4 Lsc5 Lsc6 FF2 FF3 Lsc7 Gx st_lo Gx1 fo st_yg fo1 st_f"
+
+
+FIRST = "m_FI i_p ld_c0 ld_f ld_t pi3 pi pi2 pi4 m_one ld_y ld_l i_J pi1 m_xb i_Jm i_p5 pf cw1 i_one i_dq i_Bt i_JG xl1 RH s_MS1 Im w13 Id pf2 w18 pf1 m_FI1 w14 cw3 cw R5 w19 w15 lw1 K w E10 w12 lw s_Bt E3 w16 E6 v:I128 place v:w3 R51 E11 K1 w11 s_MS2 m_DD v:w4 v:K2 E8 dq w1 E12 v:E4 v:w8 m_DD1 DD3 Go v:K3 E7 cw2 v:fw1 w7 i_trt w17 Fl0 lw2 i_NI w2 w5 w9 DD1 v:DD5 E14 Bw v:w10 v:own0 s_MS v:DD7 v:Gc v:DD6 E15 v:E5 s_MS3 DD ownT+ v:low+ vm0 af0 m_FI2 w6 DD2 NB tri K4 s_dp Yl0 E2 fwM Bw4 YF0_ fw a0 fwM1 m_FI3 Bw6 DD4 v:Bw3 E13 v:Bw5 E dA2+ v:E9 v:K5 s_Idf NB1 oT+ E1 Crm+ v:Bw2 fi6 v:K6 v:fi s_keep tri1 xl NB2 dA1+ dA3+ v:K7 v:fi2 ld_c v:Gn fi1 dA4+ dA+ Bw1 G1+ Lcv+ G3+ fi5 fi3 vl0 Lcv2+ G+ v:G2+ tri2 ext1+ Lcv1+ YF0_3 ext+ v:fi8 fi7 v:fi4 thW cl1+ v:th v:YF0_2 ftr2 ftr1 YF0_1 Lcv3+ ftr3 Ccv+ c41+ v:cl+ c4+ ftr bm1+ bm+ A2+ v:bc1+ bc+ v:A6+ v:A5+ u+ B5+ high+ dA5+ B4+ A+ A1+ B1+ dB4+ Ccv1+ A4+ f1+ dB5+ B+ F1 dB1+ A3+ bl+ B3+ th1 dB+ abs5+ B2+ u1+ D_+ v:dC+ v:yb3+ abs+ dB3+ abs1+ v:yb2+ dB2+ D1+ D+ abs2+ abs3+ abs4+ D2+ D3+ v:yb+ v:yb1+ D5+ D4+"
+ROUND = "nod mx mp kq kp jq jp nf D_+ room Zq Wq Zp X Za n1 W_ W lq Zc new fq send Csc alp arr F6 aw lv Ysc l arM Fx v:x1 cnt eq Wx v:Fl kl am kt Fx1 FF1 FF Fg am1 sl v:x1l FF2 Lsc x2 Wm v:Fl1 Lsc1 Lsc4 Lsc2 Lsc3 Wb Lsc5 Lsc6 FF4 Wv Lsc7 v:FF3 vm Flg v:G+ v:vl thr Gx1 Gx ar ext1+ Yl1 v:G1+ Crm+ own a G2+ v:YF2 G3+ xb Yl YF3 YF1 ext+ ownT+ v:af v:YF v:cl+ c41+ v:cl1+ c4+ oT+ bm1+ A+ dA+ bm+ v:A1+ dA4+ dA3+ v:bc+ A2+ v:A4+ dA2+ high+ u+ B+ B1+ bc1+ A3+ bl+ dB+ st_le dA1+ low+ B2+ dB1+ dA5+ u1+ A5+ A6+ abs+ B3+ B4+ dB2+ f1+ abs1+ D+ B5+ dB3+ abs2+ dB4+ v:yb+ D1+ v:yb1+ dB5+ v:yb3+ abs3+ v:dC+ abs4+ abs5+ D3+ yb2+ D4+ D2+ D5+"
+LAST = "v:nod mx mp kq kp jq jp nf X Zq W_ n1 Za Wq new Ysc W send lq v:fq st_yb st_yr room l alp F6 lv arM aw Fx1 FF1 v:ar arr eq Fx FF kl v:Fl1 kt sl Fl Lsc FF4 Lsc1 Lsc2 Lsc3 Lsc4 Lsc5 Lsc6 FF2 st_lo Lsc7 v:FF3 Gx v:fo fo1 Gx1 st_f st_yg"
+
+
+FIRST = "m_FI ld_c0 i_p ld_f ld_t ld_l ld_y i_p5 i_J m_xb m_one pi1 pi4 pi3 i_Jm pi2 pi xl1 pf i_one cw3 m_FI1 pf1 pf2 i_dq w15 cw w12 Id w18 Im w13 cw1 lw1 i_Bt RH w16 R5 w19 E10 v:I128 cw2 E4 s_MS1 place K v:w4 w14 m_DD1 w w3 E6 s_Bt lw E11 v:fw1 E3 v:K1 i_JG R51 w11 E7 w1 v:E8 lw2 v:w7 i_trt w17 v:E12 w5 m_DD dq w2 E14 s_MS2 Fl0 w6 v:w8 E15 Go i_NI K2 Bw Yl0 af0 v:E5 v:w9 fw s_MS v:DD2 v:Gc K3 vm0 DD v:w10 Bw4 v:DD7 s_MS3 m_FI2 E2 DD3 fwM Bw3 v:DD5 v:K4 DD6 s_dp v:Bw5 Bw6 NB fwM1 DD4 m_FI3 a0 s_Idf E13 v:E9 v:K5 E tri s_keep DD1 ld_c tri1 G1+ v:E1 vl0 Crm+ NB1 fi6 xl v:Bw2 v:K6 Lcv+ G3+ v:Gn v:fi v:G2+ fi1 NB2 Lcv2+ th v:fi2 YF0_3 v:own0 v:K7 ownT+ ext1+ fi5 fi8 tri2 Bw1 Lcv1+ low+ fi3 oT+ G+ fi7 v:fi4 dA4+ v:YF0_2 dA+ dA2+ dA3+ Lcv3+ YF0_ ftr2 ext+ ftr dA1+ cl1+ ftr3 YF0_1 thW Ccv+ c41+ v:cl+ c4+ bm1+ ftr1 A2+ bm+ v:A6+ v:bc1+ v:A5+ F1 v:bc+ B5+ A+ B4+ high+ dA5+ B1+ A4+ dB5+ dB4+ u+ Ccv1+ A1+ B3+ A3+ dB1+ B+ dB3+ bl+ th1 B2+ th2 abs5+ dB+ abs1+ D_+ abs3+ m_nf m_c3 abs+ dB2+ abs2+ D+ D1+ abs4+ D2+ D3+ D4+ D5+ pb+"
+ROUND = "f1 nod u1 mx pa mp kq kp nf D_+ v:jq X jp n1 cnt oP Zq Ws lv n2 ls new Wq room Zp Za am send alp Zc am1 W Csc lq am2 fq Ysc arM thr l F6 arr ar aw eq Fx FF v:x1 kl Fx1 Csc1 Fl kt FF1 Ysc1 Wx sl Lsc Fl1 Lsc1 FF2 v:x1l Fg Lsc2 x2 Lsc3 Wm Lsc4 Flg FF5 Lsc5 Lsc6 Wv v:FF3 vm a Wb Lsc7 v:FF4 G1+ Gx v:G+ Gx1 vl xb Yl v:G2+ G3+ ext+ v:own Yl1 YF1 v:YF ext1+ ownT+ v:cl+ v:YF2 YF3 v:cl1+ oT+ c4+ af c41+ v:low+ bm+ dA+ bm1+ A+ v:A1+ dA5+ Crm+ st_le high+ dA2+ A2+ v:bc+ v:bl+ dA3+ dA1+ B+ u+ A3+ dA4+ B1+ dB+ bc1+ A4+ B2+ A5+ dB1+ abs+ B3+ abs1+ dB2+ v:A6+ D+ B4+ dB3+ abs2+ D1+ B5+ dB4+ abs3+ dB5+ D2+ abs4+ abs5+ D3+ D4+ D5+ pb+"
+LAST = "pa nod mx mp kq nf v:jq kp n1 jp X Zq oP Ws n2 room new Wq ls Za lv send v:alp W Ysc lq fq arM Ysc1 l F6 ar st_yr arr aw st_yb eq FF1 Fx kl kt Fx1 sl FF v:Fl Lsc Lsc1 Lsc2 v:Fl1 Lsc3 FF5 Lsc4 Lsc5 Lsc6 FF2 Lsc7 Gx v:FF3 st_lo v:FF4 fo Gx1 st_yg fo1 st_f"
+
+
+FIRST = "ld_c0 m_FI i_p ld_f ld_l ld_y ld_t i_p5 i_J m_one pi4 pi1 m_xb pi i_Jm pi2 pi3 xl1 pf i_one m_FI1 pf1 pf2 Id i_Bt w15 Im w12 cw1 w13 RH w18 cw3 lw1 v:I128 i_dq w16 R5 w19 E4 v:w4 cw E10 s_MS1 cw2 K v:fw1 w14 m_DD1 w3 w E6 i_JG lw w1 R51 E7 s_Bt E11 v:w7 E3 place w11 v:E8 K1 m_DD s_MS2 dq lw2 w5 E14 i_trt Fl0 v:w8 E15 Go w2 Bw K2 i_NI w17 v:E12 af0 v:w9 w6 v:E5 DD3 v:DD2 s_MS K3 m_FI2 Yl0 E2 vm0 fw v:Gc s_MS3 v:DD5 Bw4 v:K4 v:Bw3 DD6 fwM v:DD7 DD4 tri w10 s_dp Bw6 v:Bw5 fwM1 v:K5 a0 NB s_Idf DD m_FI3 DD1 E E13 v:E1 s_keep ld_c NB1 G3+ vl0 tri1 fi6 Crm+ v:E9 v:K6 Lcv+ v:Gn xl G1+ v:Bw2 v:fi v:G2+ NB2 fi1 Lcv2+ YF0_3 v:fi2 v:own0 v:K7 ownT+ ext1+ tri2 Bw1 low+ fi5 oT+ Lcv1+ fi3 fi8 G+ dA4+ v:fi4 dA2+ fi7 v:YF0_2 dA+ dA3+ YF0_1 Lcv3+ ext+ v:cl1+ ftr2 ftr3 dA1+ th YF0_ c41+ ftr thW Ccv+ v:cl+ c4+ ftr1 A2+ bm+ bm1+ v:A6+ v:bc1+ v:A5+ F1 B5+ bc+ A+ B4+ high+ B1+ A4+ dA5+ dB5+ dB4+ u+ Ccv1+ A1+ B3+ A3+ dB1+ B+ dB3+ bl+ B2+ th1 th2 abs1+ D_+ dB+ abs3+ v:yb+ abs+ dB2+ v:yb1+ abs2+ v:yb2+ D+ m_nf m_c3 D1+ abs5+ abs4+ D2+ D3+ D4+ D5+ pb+"
+ROUND = "nod f1 mx pa mp kq u1 kp nf v:jq D_+ X jp n1 cnt oP Zq Ws room new Zp am Wq ls Za send am1 Zc alp Csc am2 W lq Ysc thr fq arM Csc1 l arr F6 ar aw lv eq Fx FF1 v:x1 kl Wx kt Ysc1 FF sl Fx1 Lsc v:x1l Lsc1 Fl x2 FF2 Fg Lsc2 v:Fl1 Lsc3 Wm Lsc4 Lsc5 FF5 v:Flg Wv Lsc6 v:FF3 vm a Wb Lsc7 v:FF4 G1+ Gx v:G+ Gx1 vl xb Yl v:G2+ G3+ ext+ v:own YF1 v:Yl1 ext1+ v:YF ownT+ cl+ v:YF2 YF3 c4+ oT+ v:cl1+ c41+ A+ bm+ v:A1+ dA+ dA5+ st_le A2+ dA2+ v:bc+ v:low+ bm1+ dA4+ B+ dA3+ high+ dA1+ bc1+ A3+ B1+ dB+ A4+ B2+ af dB1+ A5+ Crm+ u+ abs+ B3+ dB2+ abs1+ v:A6+ D+ B4+ dB3+ abs2+ B5+ dB4+ v:yb+ D1+ abs3+ dB5+ D2+ abs4+ v:yb1+ abs5+ D3+ v:yb2+ bl+ D4+ D5+ pb+"
+LAST = "pa v:nod mx mp kq nf kp jq X jp Zq Ws oP n1 room Wq new ls Za Ysc send W v:alp lq fq Ysc1 arM F6 l st_yr st_yb ar arr aw lv eq Fx FF1 kl Fx1 kt FF sl v:Fl Lsc Lsc1 Fl1 Lsc2 FF5 Lsc3 Lsc4 Lsc5 FF2 Lsc6 Gx Lsc7 v:FF3 st_lo v:FF4 fo Gx1 st_yg fo1 st_f"
 
 
 def R(name, a, b, step=1, p0=0, p1=128, ps=1):
@@ -165,7 +184,7 @@ def build():
     dma("s", R("Ci", 128, 1024), R("cl", 128, 1024), "ld_c", [R("Li", 0, 2048)])
     iota(R("pi", 0, 1), [[0, 1]], 0, 1, "i_p")
     iota(R("pi", 6, 7), [[0, 1]], 11, 1, "i_p5")
-    iota(R("J", 0, 144), [[1, 144]], 0, 0, "i_J")
+    iota(R("J", 0, 152), [[1, 152]], 0, 0, "i_J")
     iota(X("JG"), [[1, 8], [0, 16]], 0, 0, "i_JG")
     iota(X("Jm"), [[1, 16], [16, 8]], 0, 0, "i_Jm")
     iota(X("onf"), [[0, 128]], 1, 0, "i_one")
@@ -179,17 +198,14 @@ def build():
     sel(R("Bt", 0, 144), R("Bt", 0, 144), [[1, 144]], OP.is_equal, 0.0, -15, -16, "s_Bt")
     for j in range(4):
         sel(R("MS", 128 * j, 128 * j + 128), X("onf"), [[32, 4], [1000, 2], [1, 16]], OP.is_equal, 0.0, 16 * (j // 2) - 1000 * (j % 2), -1, "s_MS")
-    iota(R("nod", 0, 512), [[1, 512]], W0, 0, "i_nod")
     ms(one, 1.0, "m_one")
-    ms(R("Y", RM, BS), 0.0, "m_Y")
-    for h in range(0, WD, 640):
-        ms(R("FI", h, h + 640), 0.0, "m_FI")
-    for h in range(0, 2048, 1024):
+    for h in range(0, WA, 608):
+        ms(R("FI", h, h + 608), 0.0, "m_FI")
+    for h in range(0, 2048 if PACK else 4096, 1024):
         ms(R("DD", h, h + 1024), 0.0, "m_DD")
-    ms(R("C", 0, 512), 0.0, "m_C")
-    ms(R("L", 2048, 2064), 0.0, "m_L")
-    ms(R("sl", 0, 16), 0, "m_sl")
     ms(R("xb", 0, 8), -19.0, "m_xb")
+    ms(R("nf", 8, 9), 7.5 / 16, "m_nf")
+    ms(X("c3"), 393216.0, "m_c3")
     ts(R("pi", 1, 2), R("pi", 0, 1), 15, OP.bitwise_and, None, None, "pi")
     ts(R("pi", 2, 3), R("pi", 0, 1), 4, OP.arith_shift_right, None, None, "pi")
     ts(R("pi", 3, 4), R("pi", 6, 7), 15, OP.bitwise_and, None, None, "pi")
@@ -200,14 +216,16 @@ def build():
     act(p5, pG, "pf", bias=R("pf", 3, 4), scale=16.0)
     act(pW, pG, "pf", bias=15.0, scale=16.0)
     ts(Id, X("J"), pP, OP.is_equal, None, None, "Id")
-    ts(X("R5"), X("J"), p5, OP.is_equal, 4096.0, OP.mult, "R5")
-    tt(X("R5"), X("R5"), Id, OP.add, "R5")
+    ts(X("R5"), X("J"), p5, OP.is_equal, 4096.0 if PACK else 1.0, OP.mult, "R5")
+    if PACK:
+        tt(X("R5"), X("R5"), Id, OP.add, "R5")
     ts(R("RH", 0, 16), R("J", 0, 16), pR, OP.is_equal, None, None, "RH")
     ts(X("Go"), X("JG"), pG, OP.is_equal, None, None, "Go")
     ts(R("Bw", 0, 144), R("J", 0, 144), pW, OP.is_equal, None, None, "Bw")
     ts(X("Im"), X("Jm"), pP, OP.is_equal, None, None, "Im")
-    for h in range(8):
-        act(R("DD", 256 * h, 256 * h + 256, 17), R("R5", 16 * h, 16 * h + 16), "DD")
+    for j, m in enumerate(("R5",) if PACK else ("Id", "R5")):
+        for h in range(8):
+            act(R("DD", 2048 * j + 256 * h, 2048 * j + 256 * h + 256, 17), R(m, 16 * h, 16 * h + 16), "DD")
     for k in range(16):
         act(R("E", k, 2048, 16), X("Im"), "E")
     act(R("K", 0, 16), R("RH", 0, 16), "K")
@@ -221,13 +239,15 @@ def build():
     act(col(5), col(4), "w", scale=-19.0, bias=col(3))
     act(col(6), col(5), "w", scale=128.0)
     act(col(7), rh(3), "w", bias=rh(4))
-    act(col(8), col(7), "w", bias=rh(6))
+    act(col(18), rh(2), "w", bias=rh(6), scale=-8.0)
+    act(col(8), col(7), "w", bias=col(18))
     act(col(9), col(7), "w", bias=rh(5))
     act(col(10), rh(6), "w", scale=-4096.0)
     act(col(11), pR, "w", bias=2048.0)
     act(col(12), pR, "w", scale=-128.0, bias=KEY)
     act(col(17), pR, "w", scale=256.0, bias=2.0 ** 23 - 2018)
-    act(col(13), pR, "w", bias=float(W0))
+    act(col(13), pO, "w", scale=128.0)
+    act(R("col", 20, 24), R("J", 15, 19), "w", scale=col(13))
     act(col(14), pR, "w", scale=8.0)
     act(col(15), pR, "w", scale=0.125)
     act(col(16), p8, "w", scale=15.875, bias=col(15))
@@ -248,45 +268,41 @@ def build():
     ts(R("vl", 0, 8), R("lwf", 8, 16), 512.0, OP.add, None, None, "vl0")
     ts(R("xl", 0, 8), R("J", 0, 8), col(14), OP.add, None, None, "xl")
     cp(R("xl", 8, 16), R("J", 0, 8), "xl")
-    ts(R("cw", 0, 16), R("J", 0, 16), 0.0, OP.mult, None, None, "cw")
+    ts(R("cw", 8, 16), R("J", 0, 8), 0.0, OP.mult, None, None, "cw")
     ts(R("cw", 16, 24), R("J", 0, 8), 0.0, OP.mult, -float(OFF), OP.add, "cw")
     ts(R("cw", 24, 32), R("lwf", 8, 16), float(WA - OFF), OP.add, None, None, "cw")
     ts(R("cw", 32, 40), R("J", 0, 8), 0.0, OP.mult, 19.0 - OFF, OP.add, "cw")
-    act(R("nod", 0, 512), R("nod", 0, 512), "nod", scale=pO)
     ts(X("NI"), X("NI"), 7, OP.bitwise_and, None, None, "NB")
     ts(X("NB"), X("NI"), rh(2), OP.mult, col(8), OP.add, "NB")
-    act(R("NB", 19, 128, 32), R("J", 15, 19), "NB", bias=col(9), scale=rh(2))
-    cp(X("al"), IND(R("Ci", 0, 128), R("vm", 0, 8)), "a0")
-    cp(X("af"), R("Ci", 0, 128), "af0")
-    cp(R("Yl", 0, 120), R("fwi", 0, 120), "Yl0")
-    cp(R("Fl", 64, 120), R("fwi", 64, 120), "Fl0")
-    cp(R("thf", 0, 128, 1, 0, 8), R("thi", 0, 128, 1, 0, 8), "th")
+    act(R("NB", 19, 128, 32), R("J", 7, 11), "NB", bias=col(9), scale=rh(2))
+    act(X("al"), IND(R("Ci", 0, 128), R("vm", 0, 8)), "a0")
+    act(X("af"), R("Ci", 0, 128), "af0")
+    act(R("Yl", 0, 120), R("fwi", 0, 120), "Yl0")
+    act(R("Fl", 64, 120), R("fwi", 64, 120), "Fl0")
+    act(R("thf", 0, 128, 1, 0, 8), R("thi", 0, 128, 1, 0, 8), "th")
     acc(R("P7", 0, 8), [(R("Bt", 15 - r, 143 - r, 1, 0, 8), R("thf", r, 128, 16, 0, 8)) for r in range(16)], "thW")
     act(R("th0", 0, 8), R("P7", 0, 8), "th", bias=-KEY)
-    cp(R("fwf", 0, 120), R("fwi", 0, 120), "fw")
-    act(R("fwf", 120, 160), R("J", 0, 40), "fw", bias=col(13), scale=16.0)
+    act(R("th0", 8, 16), R("P7", 0, 8), "th", bias=-8.5 * KEY)
+    act(R("fwf", 0, 120), R("fwi", 0, 120), "fw")
+    act(R("fwf", 120, 152), R("J", 120, 152), "fw", bias=pR, scale=16.0)
     for j in range(2):
-        acc(R("P6", j, 160, 2), [(R("MS", 256 * j, 256 * j + 128), R("fwf", 0, 160, 2)), (R("MS", 256 * j + 128, 256 * j + 256), R("fwf", 1, 160, 2))], "fwM")
-    V = R("t4", 0, 160)
+        acc(R("P6", j, 152, 2), [(R("MS", 256 * j, 256 * j + 128), R("fwf", 0, 152, 2)), (R("MS", 256 * j + 128, 256 * j + 256), R("fwf", 1, 152, 2))], "fwM")
+    V, t1 = R("t4", 0, 152), R("t1", 0, 152)
 
-    def fi(k):
-        return R("FI", k, WD, 16)
-    act(V, R("P6", 0, 160), "fi")
-    act(R("t1", 0, 160), V, "fi", bias=24576.0 - 63.5)
-    act(R("t2", 0, 160), R("t1", 0, 160), "fi", bias=-192.0, scale=1.0 / 128)
-    act(fi(1), R("t2", 0, 160), "fi")
-    act(R("t3", 0, 160), R("t2", 0, 160), "fi", scale=-128.0)
-    tt(fi(0), R("t3", 0, 160), V, OP.add, "fi")
-    ts(fi(3), V, float(W0), OP.is_ge, None, None, "fi")
-    ts(R("t5", 0, 160), V, 1024.0, OP.is_ge, None, None, "fi")
-    tt(R("t5", 0, 160), R("t5", 0, 160), fi(3), OP.subtract, "fi")
+    def fi(k, a=0, b=WA):
+        return R("FI", a + k, b, 16)
+    act(t1, R("P6", 0, 152), "fi", bias=24576.0 - 63.5)
+    act(V, R("P6", 0, 152), "fi", bias=24576.0)
+    act(fi(1), t1, "fi", bias=-192.0, scale=1.0 / 128)
+    tt(fi(0), V, t1, OP.subtract, "fi")
     for k in (2, 5):
-        act(fi(k), R("t5", 0, 160), "fi")
-    act(V, R("t5", 0, 160), "fi", bias=1.0, scale=-1.0)
-    tt(fi(4), V, R("t2", 0, 160), OP.mult, "fi")
-    for h in range(0, WD, 640):
-        add("v", [("transpose", (R("F0", h, h + 640), R("FI", h, h + 640)), {})], [R("FI", h, h + 640)], [R("F0", h, h + 640)], "ftr")
-    gcopy(R("F1", W0, WD), R("F0", W0, WD), "F1")
+        ts(fi(k, 0, W0), R("t4", 0, 120), 24576.0 + 1024, OP.is_ge, None, None, "fi")
+    ms(fi(3, W0), 1.0, "fi")
+    ts(fi(4, 0, W0), fi(1, 0, W0), 8.0, OP.min, None, None, "fi")
+    act(fi(4, W0), fi(1, W0), "fi")
+    for h in range(0, WA, 608):
+        add("v", [("transpose", (R("F0", h, h + 608), R("FI", h, h + 608)), {})], [R("FI", h, h + 608)], [R("F0", h, h + 608)], "ftr")
+    gcopy(R("F1", W0, WA), R("F0", W0, WA), "F1")
     for a in range(0, W0, 480):
         act(R("YF", a, a + 480), IND(R("Y", BS, YW), R("Yl", a // 16, a // 16 + 30)), "YF0_", scale=0.5)
     act(X("own"), R("Y", BS, BS + 128), "own0")
@@ -303,18 +319,21 @@ def build():
         own, af = X("own"), X("af")
         vl = R("vl", 8 * t, 8 * t + 8)
         for a in range(0, 2048, 512):
-            if t == 0:
-                ts(R("G", a, a + 512), IND(Lw, R("al", a // 16, a // 16 + 32)), -float(OFF), OP.add, None, None, "G")
-            else:
-                act(R("G", a, a + 512), IND(Lw, R("al", a // 16, a // 16 + 32)), "G", bias=-float(OFF))
+            act(R("G", a, a + 512), IND(Lw, R("al", a // 16, a // 16 + 32)), "G", bias=-float(OFF))
         for h in range(2):
             pb = "P%d" % (4 + h)
             hb = R(pb, 0, 64)
-            acc(hb, [(R("DD", k, 2048, 16), R("G", 1024 * h + k, 1024 * h + 1024, 16)) for k in range(16)], "ext")
-            ts(R("bc", 128 * h, 128 * h + 64), hb, 1.0 / 4096, OP.mult, float(OFF), OP.add, "cl")
-            ts(R("c4", 64 * h, 64 * h + 64), hb, RND / 8, OP.add, -RND / 8, OP.add, "c4")
-            tt(R("bm", 64 * h, 64 * h + 64), hb, R("c4", 64 * h, 64 * h + 64), OP.subtract, "bm")
-            ts(R("bc", 128 * h + 64, 128 * h + 128), R("bm", 64 * h, 64 * h + 64), float(OFF), OP.add, None, None, "bc")
+            if PACK:
+                acc(hb, [(R("DD", k, 2048, 16), R("G", 1024 * h + k, 1024 * h + 1024, 16)) for k in range(16)], "ext")
+                act(R("bc", 128 * h, 128 * h + 64), hb, "cl", bias=float(OFF), scale=1.0 / 4096)
+                ts(R("c4", 64 * h, 64 * h + 64), hb, RND / 8, OP.add, -RND / 8, OP.add, "c4")
+                tt(R("bm", 64 * h, 64 * h + 64), hb, R("c4", 64 * h, 64 * h + 64), OP.subtract, "bm")
+                act(R("bc", 128 * h + 64, 128 * h + 128), R("bm", 64 * h, 64 * h + 64), "bc", bias=float(OFF))
+            else:
+                for j in range(2):
+                    acc(R(pb, 64 * j, 64 * j + 64), [(R("DD", 2048 * j + k, 2048 * j + 2048, 16), R("G", 1024 * h + k, 1024 * h + 1024, 16)) for k in range(16)], "ext")
+                act(R("bc", 128 * h, 128 * h + 128), R(pb, 0, 128), "bc", bias=float(OFF))
+                act(R("bm", 64 * h, 64 * h + 64), hb, "bm")
         act(X("bl"), IND(X("bm"), R("xl", 0, 8)), "bl")
         if t == 0:
             for h in range(0, 2048, 512):
@@ -336,23 +355,31 @@ def build():
             mm([(R(pb, 0, b - a), Id, R("B", a, b), False, True)], "dB", pb)
             act(R("ab", a, b), R(pb, 0, b - a), "abs", AF.Abs, -1024.0)
             mm([(X("P7"), shift(6, r), R("ab", 128 * r, 128 * r + 128), False, r == 15) for r in range(a // 128, b // 128)], "D", "D")
-        for a in range(0, 2048, 512):
-            ts(R("yb", a, a + 512), R("B", a, a + 512), -1024.0, OP.add, None, None, "yb")
+        for (a, b) in YBP:
+            act(R("yb", a, b), R("B", a, b), "yb", bias=-1024.0)
         act(X("low"), own, "low", bias=-1.0)
         acc(R("P5", 256, 384), [(Id, own), (Id, one)], "high")
         if not last:
             acc(R("P5", 0, 128), [(X("Go"), own), (X("Idf"), af)], "u")
             act(X("f1"), R("P5", 0, 128), "f1", bias=1022.5 - t - 393216.0, scale=-1.0)
-            acc(R("P5", 128, 256), [(X("Go"), own), (Id, X("f1"))], "u")
-            act(X("dC"), R("P5", 128, 256), "dC", bias=393217.0 + t)
-        scan(R("mx", 0, 128), X("P7"), X("dq"), BIG, OP.min, OP.add, "mx")
-        scan(R("mx", 128, 256), X("P7"), X("dp"), 0.0, OP.max, OP.mult, "mx")
-        cp(R("ki", 0, 16), R("mx", 15, 256, 16), "ki")
-        ts(R("kj", 0, 16), R("ki", 0, 16), 2047, OP.bitwise_and, None, None, "kj")
-        cp(R("jl", 0, 16), R("kj", 0, 16), "jl")
+            acc(R("P5", 128, 256), [(X("Go"), own), (Id, X("f1")), (Id, X("c3"))] + [(Id, one)] * (t + 1), "u")
+            acc(R("P5", 384, 512), [(Id, X("bl"))], "pb")
+        acc(R("P5", 0, 128), [(X("Idf"), af)], "pa")
         jq, jp = R("jl", 0, 8), R("jl", 8, 16)
+        scan(R("mx", 0, 128), X("P7"), X("dq"), BIG, OP.min, OP.add, "mx")
+        ts(R("kj", 0, 8), R("mx", 15, 128, 16), 2047, OP.bitwise_and, None, None, "kq")
+        act(jq, R("kj", 0, 8), "jq")
+        scan(R("mx", 128, 256), X("P7"), X("dp"), 0.0, OP.max, OP.mult, "mp")
+        ts(R("kj", 8, 16), R("mx", 143, 256, 16), 2047, OP.bitwise_and, None, None, "kp")
+        act(jp, R("kj", 8, 16), "jp")
         tt(R("nf", 0, 8), R("mx", 143, 256, 16), R("thr" if t else "th0", 0, 8), OP.is_ge, "nf")
         tt(R("X", 0, 8), R("nf", 0, 8), R("xb", 8 * t, 8 * t + 8), OP.mult, "X")
+        if not last:
+            acc(R("P6", 448, 449), [(X("Gc"), R("nf", c, c + 1)) for c in range(9)], "cnt")
+            act(R("am", 0, 1), R("P6", 448, 449), "am", bias=RND)
+            act(R("am", 1, 2), R("am", 0, 1), "am", bias=-RND)
+            act(R("am", 2, 3), R("P6", 448, 449), "am", bias=R("am", 1, 2), scale=-1.0)
+            act(R("thr", 0, 8), R("th0", 8, 16), "thr", bias=R("am", 2, 3))
         nw = R("new", S * t, S * t + S)
         tt(X("n1"), IND(R("yb", 0, 2048), jq), X("low"), OP.max, "n1")
         tt(nw, X("n1"), R("P5", 256, 384), OP.min, "new")
@@ -360,16 +387,21 @@ def build():
         add("g", [("send", (nw, gh, t), {})], [nw], [R("@%d" % t, 0, 1)], "send", kind="s")
         add("x", [("arr", (t,), {})], [R("@%d" % t, 0, 1)], [R("Y", gh, gh + 896)], "arr", kind="x")
         act(R("Y", RM + S * t, RM + S * t + S), IND(R("yb", 0, 2048), jp), "room")
-        cp(IND(R("Y", RM, GB), vl), nw, "Ysc")
+        for h in range(0, 8, SC):
+            cp(IND(R("Y", RM, GB), R("vl", 8 * t + h, 8 * t + h + SC)), R("new", S * t + 16 * h, S * t + 16 * (h + SC)), "Ysc")
         Kw = R("K", 0, 2048)
         tt(R("Z", 0, 128), IND(Kw, jq), X("bl"), OP.mult, "Zq")
+        rows(R("P2", 0, 8), 0, "Z", 0, 128, "Wq")
+        act(R("l1", 0, 8), R("P2", 0, 8), "lq", bias=float(OFF))
+        act(X("oP"), IND(Kw, jp), "oP")
         if not last:
-            tt(R("Z", 128, 256), IND(Kw, jp), X("bl"), OP.mult, "Zp")
-        tt(R("Z", 256, 384), IND(Kw, jp), af, OP.mult, "Za")
-        mm([(R("P0", 0, 40), Id, R("cw", 0, 40), True, False), (R("P0", 24, 32), X("I128"), R("X", 0, 8), False, False),
-            (R("P0", 32, 40), Id, R("X", 0, 8), False, False)], "W_", "W")
-        mm([(R("P0", 0, 24), shift(0, r), R("Z", r, 384, 16), False, r == 15) for r in range(16)], "W", "W")
-        ts(R("l1", 0, 40), R("P0", 0, 40), float(OFF), OP.add, None, None, "l")
+            tt(R("Z", 128, 256), R("P5", 384, 512), X("oP"), OP.mult, "Zp")
+        tt(R("Z", 256, 384), R("P5", 0, 128), X("oP"), OP.mult, "Za")
+        mm([(R("P3", 24, 40), Id, R("cw", 24, 40), True, False), (R("P3", 24, 32), X("I128"), R("X", 0, 8), False, False),
+            (R("P3", 32, 40), Id, R("X", 0, 8), False, True)], "Ws")
+        act(R("l1", 24, 40), R("P3", 24, 40), "ls", bias=float(OFF))
+        rows(R("P0", 8, 24), 0, "Z", 128, 384, "W", R("cw", 8, 24))
+        act(R("l1", 8, 24), R("P0", 8, 24), "l", bias=float(OFF))
         bq, bp, aP, vs, vb = [R("l1", 8 * k, 8 * k + 8) for k in range(5)]
         act(X("fq"), IND(Fw, bq), "fq")
         cp(IND(Fw, vs), X("fq"), "F6")
@@ -377,27 +409,29 @@ def build():
         if not last:
             act(X("x1"), IND(Fw, bp), "x1")
             rows(R("P2", 0, 8), 1, "x1", 0, 128, "Wx")
-            cp(R("x1l", 0, 8), R("P2", 0, 8), "x1l")
+            act(R("x1l", 0, 8), R("P2", 0, 8), "x1l")
             tt(X("x2"), IND(Fw, R("x1l", 0, 8)), X("alp"), OP.mult, "x2")
             acc(R("P2", 8, 16), [(Id, R("lw", 0, 8))] + [(shift(4, r), R("x2", 16 * (r % 8) + r // 8, 16 * (r % 8) + 16, 2)) for r in range(16)], "Wm")
-            ts(R("vm", 0, 8), R("P2", 8, 16), 512.0, OP.add, None, None, "vm")
-            tt(X("Zc"), IND(Kw, jp), X("dC"), OP.mult, "Zc")
-            tt(IND(R("C", 0, 1536), vl), X("Zc"), af, OP.add, "Csc")
-            cp(X("al"), IND(R("C", 0, 1536), R("vm", 0, 8)), "a")
+            act(R("vm", 0, 8), R("P2", 8, 16), "vm", bias=512.0)
+            tt(X("Zc"), R("P5", 128, 256), X("oP"), OP.mult, "Zc")
+            for h in range(0, 8, SC):
+                tt(IND(R("C", 0, 1536), R("vl", 8 * t + h, 8 * t + h + SC)), R("Zc", 16 * h, 16 * (h + SC)), R("af", 16 * h, 16 * (h + SC)), OP.add, "Csc")
+            act(X("al"), IND(R("C", 0, 1536), R("vm", 0, 8)), "a")
         for j, (a, e) in enumerate(((0, 1024), (W0, Wt))):
             if e > a:
                 rows(R("P%d" % (3 + j), 0, (e - a) // 16), 1, cur, a, e, "Fx")
-                cp(R("Fl", a // 16, e // 16), R("P%d" % (3 + j), 0, (e - a) // 16), "Fl")
+                act(R("Fl", a // 16, e // 16), R("P%d" % (3 + j), 0, (e - a) // 16), "Fl")
         acc(R("P1", 0, 128), [(Id, X("tri")), (X("Go"), R("Z", 256, 384)), (X("Gn"), X("alp"))], "arM")
         act(X("ar"), R("P1", 0, 128), "ar", scale=1.0 / 4096)
-        ts(R("aw", 0, 8), aP, 1.0 / 4096, OP.mult, None, None, "aw")
+        act(R("aw", 0, 8), aP, "aw", scale=1.0 / 4096)
+        act(X("nod"), X("J"), "nod", bias=col(20 + t), scale=pO)
         tt(X("eq"), IND(R("aw", 0, 8), R("xl", 8, 16)), X("ar"), OP.is_equal, "eq")
         scan(X("kl"), X("keep"), X("eq"), 0.0, OP.mult, OP.max, "kl")
         tt(R("kt", 0, 8), R("kl", 15, 128, 16), R("aw", 0, 8), OP.add, "kt")
         ts(R("sl", 0, 16, 2), R("kt", 0, 8), 4096.0, OP.mult, col(11), OP.min, "sl")
         act(X("lv"), IND(R("L", 0, 2048), aP), "lv")
         for c in range(7, -1, -1):
-            tt(IND(R("L", 0, 2064), R("sl", 2 * c, 2 * c + 1)), R("lv", 16 * c, 16 * c + 16), R("nod", S * t + 16 * c, S * t + 16 * c + 16), OP.max, "Lsc")
+            tt(IND(R("L", 0, 2064), R("sl", 2 * c, 2 * c + 1)), R("lv", 16 * c, 16 * c + 16), R("nod", 16 * c, 16 * c + 16), OP.max, "Lsc")
         if t == 0:
             dma("s", R("lo", 0, 2048, 1, 0, 128, 2), R("L", 0, 2048, 1, 0, 128, 2), "st_le")
         if last:
@@ -409,20 +443,16 @@ def build():
             vn = R("vl", 8 * t + 8, 8 * t + 16)
             rows(R("P0", 64, 72), 4, "x2", 0, 128, "Wv", R("lw", 8, 16))
             rows(R("P0", 72, 80), 5, "x2", 0, 128, "Wb")
-            ts(vn, R("P0", 64, 72), 512.0, OP.add, None, None, "vl")
+            act(vn, R("P0", 64, 72), "vl", bias=512.0)
             act(R("xb", 8 * t + 8, 8 * t + 16), R("P0", 72, 80), "xb", bias=-19.0)
             act(af, IND(R("C", 0, 1536), vn), "af")
             act(own, IND(R("Y", RM, GB), vn), "own")
-        for (a, b) in ((1024, 1472), (1472, W0), (0, 512), (512, 1024), (W0, Wt)):
+        for (a, b) in FFP + ((W0, Wt),):
             if b > a:
                 act(R(nxt, a, b), IND(Fw, R("Fl", a // 16, b // 16)), "FF")
         if not last:
-            acc(R("P1", 448, 449), [(X("Gc"), R("nf", c, c + 1)) for c in range(8)], "cnt")
-            ts(R("am", 0, 1), R("P1", 448, 449), -7.5 * KEY, OP.add, RND, OP.add, "am")
-            ts(R("am", 1, 2), R("am", 0, 1), -RND, OP.add, R("P1", 448, 449), OP.subtract, "am")
-            act(R("thr", 0, 8), R("th0", 0, 8), "thr", bias=R("am", 1, 2))
             rows(R("P1", 384, 440), 1, nxt, 1024, W0, "Fg")
-            cp(R("Fl", 64, 120), R("P1", 384, 440), "Flg")
+            act(R("Fl", 64, 120), R("P1", 384, 440), "Flg")
         win = R("Y", GA, GB) if t % 2 == 0 else R("Y", RM, YW)
         for j, (a, e) in enumerate(((1024, Wn), (0, 1024))):
             pb = ("P6", "P3")[j]
@@ -431,7 +461,7 @@ def build():
             if last:
                 act(R("fof", a // 16, e // 16), R(pb, 0, n), "fo")
             else:
-                ts(R("Yl", a // 16, e // 16), R(pb, 0, n), 1408.0 if t % 2 == 0 else 512.0, OP.add, None, None, "Yl")
+                act(R("Yl", a // 16, e // 16), R(pb, 0, n), "Yl", bias=1408.0 if t % 2 == 0 else 512.0)
                 for (c, d) in ((a, a + 512), (a + 512, e)):
                     act(R("YF", c, d), IND(win, R("Yl", c // 16, d // 16)), "YF", scale=0.5)
         if last:
@@ -449,12 +479,15 @@ def links(ops):
     hist = {}
     for i, o in enumerate(ops):
         pre = set()
+        o["raw"] = set()
         for w0, xs in ((False, o["rd"]), (True, o["wr"])):
             for x in xs:
                 for (j, y, w) in hist.get(x[1], []):
                     same = ops[j]["eng"] == "p" and o["eng"] == "p"
                     if (w or w0 or (x[1][0] == "P" and not same)) and meet(x, y, same):
                         pre.add(j)
+                        if w or o["kind"] != "c" or ops[j]["kind"] != "c":
+                            o["raw"].add(j)
         if o["group"]:
             pre |= set([j for j in range(i) if ops[j]["group"] == o["group"] and ops[j]["t"] == o["t"]][-1:])
         o["soft"] = [j for j in pre if o["group"] and ops[j]["group"] == o["group"] and ops[j]["t"] == o["t"]]
@@ -565,7 +598,7 @@ def rank_program(g, core, T, topo):
             continue
         need = {}
         for j in o["pre"]:
-            if j not in o["soft"]:
+            if j not in o["soft"] and (j in o["raw"] or ops[j]["eng"] != e):
                 s, v = done[j]
                 need[s] = max(need.get(s, 0), v)
         for s in sorted(need):

from concourse.bass import DstId, RemoteDMATransfer
from concourse.mybir import AluOpType, ActivationFunctionType

OP = AluOpType
AF = ActivationFunctionType
N, S, RO = 8, 128, 4
W0, WA, WD = 1920, 2432, 2560
GA, RM, BS, GB, YW = 0, 896, 1408, 2432, 3328
OFF = 1216
BIG = 1.0e9
KEY = 2048.0
RND = 1.5 * 2.0 ** 38
PACK = True
SC = 4
YBP = ((0, 1024), (1024, 1536), (1536, 2048))
FFP = ((1024, 1472), (1472, W0), (0, 512), (512, 768), (768, 1024))
HELP = 2
PIECES = ((0, 512, "P0"), (512, 1024, "P1"), (1024, 1536, "P2"), (1536, 1792, "P3"), (1792, 1920, "P6"), (1920, 2048, "P4"))


def sb(n, d):
    return ("sbuf", [128, n], d)


SCRATCH = {
    "Y": sb(YW, "bfloat16"), "YF": sb(WA, "bfloat16"), "F0": sb(WD, "bfloat16"), "F1": sb(WD, "bfloat16"),
    "FI": sb(WD, "bfloat16"), "Li": sb(2048, "int32"), "L": sb(2064, "float32"), "Ci": sb(1024, "int32"),
    "C": sb(1536, "float32"), "fwi": sb(120, "int32"), "fwf": sb(160, "float32"), "thi": sb(128, "int32"),
    "thf": sb(128, "float32"), "th0": sb(16, "float32"), "thr": sb(8, "float32"), "am": sb(8, "float32"),
    "DD": sb(4096, "bfloat16"), "c4": sb(128, "float32"), "E": sb(2048, "bfloat16"), "K": sb(2048, "bfloat16"),
    "J": sb(152, "float32"), "JG": sb(128, "float32"), "Jm": sb(128, "bfloat16"), "Im": sb(128, "bfloat16"),
    "pi": sb(8, "int32"), "pf": sb(8, "float32"), "RH": sb(16, "float32"), "col": sb(24, "float32"),
    "Id": sb(128, "bfloat16"), "Idf": sb(128, "float32"), "R5": sb(128, "bfloat16"), "Go": sb(128, "bfloat16"),
    "Gc": sb(128, "bfloat16"), "Gn": sb(128, "bfloat16"), "I128": sb(128, "bfloat16"),
    "one": sb(128, "bfloat16"), "onf": sb(128, "float32"), "Bw": sb(7 * 144, "bfloat16"), "Bt": sb(144, "float32"),
    "MS": sb(512, "float32"), "place": sb(128, "float16"), "dq": sb(128, "float32"), "dp": sb(128, "float32"), "keep": sb(128, "float32"),
    "tri": sb(128, "bfloat16"), "trt": sb(128, "float32"), "cw": sb(40, "float16"), "lw": sb(16, "bfloat16"),
    "lwf": sb(24, "float32"), "xl": sb(24, "uint16"), "NI": sb(128, "int32"), "NB": sb(128, "bfloat16"),
    "t1": sb(160, "bfloat16"), "t2": sb(160, "float32"), "t3": sb(160, "float32"), "t4": sb(160, "float32"), "t5": sb(160, "float32"),
    "Fl": sb(160, "uint16"), "Yl": sb(160, "uint16"), "vm": sb(8, "uint16"), "vl": sb(32, "uint16"), "xb": sb(32, "bfloat16"),
    "al": sb(128, "uint16"), "G": sb(2048, "float16"), "bc": sb(256, "uint16"), "bm": sb(128, "float32"), "bl": sb(128, "float16"),
    "af": sb(128, "float32"), "c3": sb(128, "bfloat16"), "oP": sb(128, "bfloat16"), "f1": sb(128, "bfloat16"), "Z": sb(384, "float16"), "Zc": sb(128, "float32"),
    "A": sb(2048, "float32"), "B": sb(2048, "float16"), "ab": sb(2048, "bfloat16"), "yb": sb(2048, "bfloat16"),
    "own": sb(128, "bfloat16"), "oT": sb(128, "bfloat16"), "low": sb(128, "bfloat16"),
    "mx": sb(256, "int32"), "ki": sb(16, "int32"), "kj": sb(16, "int32"), "jl": sb(16, "uint16"),
    "nf": sb(16, "bfloat16"), "X": sb(8, "bfloat16"), "l1": sb(40, "uint16"), "fq": sb(128, "bfloat16"),
    "x1": sb(128, "bfloat16"), "x1l": sb(8, "uint16"), "x2": sb(128, "bfloat16"), "alp": sb(128, "bfloat16"),
    "n1": sb(128, "bfloat16"), "new": sb(512, "bfloat16"),
    "aw": sb(8, "float32"), "ar": sb(128, "float32"), "eq": sb(128, "float32"), "kl": sb(128, "float32"), "kt": sb(8, "float32"),
    "sl": sb(16, "uint16"), "lv": sb(128, "float32"), "nod": sb(512, "float32"), "fof": sb(152, "float32"),
}
for k_ in range(8):
    SCRATCH["P%d" % k_] = ("psum", [128, 512], "float32")
NDMA = 16
SEMAPHORES = ["sv", "sa", "sp", "sg", "sent"] + ["arr%d" % t for t in range(RO)] + ["hop%d" % t for t in range(RO)] + ["d%d" % k for k in range(NDMA)]

FIRST = "m_Y ld_y ld_c0 i_p ld_f ld_t ld_l i_p5 m_sl i_Bt m_xb pi pi4 pi3 pi2 i_J pi1 m_one pf m_L i_one v:w13 pf1 cw RH w11 xl1 pf2 i_Jm w12 m_FI w15 w16 w14 s_MS1 w17 cw3 K Id w lw1 R5 lw cw1 I128 v:w10 K1 w1 w4 w3 i_dq lw2 w7 Im m_DD w2 place w8 s_MS2 s_Bt xl w9 m_FI1 E8 K2 w5 s_MS E11 R51 fw1 dq m_DD1 w6 i_JG own0 DD2 DD v:DD3 i_NI ownT+ v:K3 E6 E3 v:E10 E12 v:low+ i_trt DD1 v:K4 m_FI2 DD4 DD6 E5 s_dp v:DD7 Bw K5 E14 E7 vm0 v:E9 v:DD5 s_MS3 Go v:E13 Bw6 v:Bw1 NB K6 s_Idf tri1 m_FI3 Bw4 i_nod m_C K7 tri cw2 v:Bw3 th s_keep E4 NB1 Bw2 v:E2 a0 E15 ld_c vl0 Lcv+ Bw5 af0 E Gc fw Yl0 G3+ E1 fwM fwM1 nod Lcv2+ thW Gn NB2 Fl0 YF0_2 v:fi fi6 G1+ YF0_ oT+ Lcv1+ G+ fi1 YF0_3 dA4+ dA1+ dA3+ Crm+ G2+ th1 ext+ fi2 Ccv1+ YF0_1 ext1+ dA2+ fi7 D_+ cl+ tri2 v:fi4 fi3 Ccv+ c4+ dA+ A2+ fi8 bm+ cl1+ bc+ c41+ dA5+ fi5 A1+ bm1+ Lcv3+ B1+ A+ high+ u+ A4+ A5+ bc1+ B+ A3+ B4+ dB+ B3+ fi9 dB4+ bl+ B2+ f1+ dB3+ fi11 dB1+ A6+ u1+ fi10 fi12 abs+ dB2+ B5+ ftr abs1+ ftr2 dB5+ D+ yb2+ abs2+ D1+ ftr1 yb1+ yb+ abs3+ D2+ dC+ abs4+ D3+ abs5+ D4+ yb3+ F1 D5+ ftr3"
ROUND = "mx mx1 ki nf D_+ kj X jl Zp Zq Za W_ room n1 W Zc new l Ysc fq alp aw F6 lv arM arr Csc ar Fx v:x1 cnt eq Wx FF1 Fl kl am kt send FF Fx1 am1 sl x1l FF2 Lsc x2 Fg Lsc1 Fl1 Lsc2 Wm thr Lsc3 FF4 Flg Lsc4 FF3 Wb Lsc5 vm Lsc6 a Wv Lsc7 v:G+ G2+ Gx vl Gx1 Yl G3+ v:G1+ own Yl1 YF1 v:YF v:xb ext+ ext1+ v:YF2 YF3 ownT+ cl+ cl1+ low+ c4+ c41+ oT+ bm+ A+ v:A1+ bc+ dA+ af bm1+ A2+ dA5+ dA3+ v:A4+ dA4+ high+ dA1+ bc1+ B+ dA2+ A3+ u+ B1+ st_le dB+ A6+ bl+ B2+ A5+ dB1+ f1+ abs+ u1+ B3+ Crm+ abs1+ dB2+ B4+ D+ B5+ dB3+ abs2+ dB4+ v:dC+ D1+ yb2+ dB5+ abs3+ yb1+ D2+ abs4+ yb+ abs5+ D3+ yb3+ D4+ D5+"
LAST = "mx mx1 ki nf kj X jl W_ Za room Zq n1 W send l v:fq alp aw lv F6 new arM arr Ysc ar Fx1 FF1 eq Fx st_yb st_yr kl FF Fl1 kt sl Fl Lsc Lsc1 Lsc2 Lsc3 Lsc4 FF4 Lsc5 Lsc6 FF2 FF3 Lsc7 Gx st_lo Gx1 fo st_yg fo1 st_f"


FIRST = "m_FI i_p ld_c0 ld_f ld_t pi3 pi pi2 pi4 m_one ld_y ld_l i_J pi1 m_xb i_Jm i_p5 pf cw1 i_one i_dq i_Bt i_JG xl1 RH s_MS1 Im w13 Id pf2 w18 pf1 m_FI1 w14 cw3 cw R5 w19 w15 lw1 K w E10 w12 lw s_Bt E3 w16 E6 v:I128 place v:w3 R51 E11 K1 w11 s_MS2 m_DD v:w4 v:K2 E8 dq w1 E12 v:E4 v:w8 m_DD1 DD3 Go v:K3 E7 cw2 v:fw1 w7 i_trt w17 Fl0 lw2 i_NI w2 w5 w9 DD1 v:DD5 E14 Bw v:w10 v:own0 s_MS v:DD7 v:Gc v:DD6 E15 v:E5 s_MS3 DD ownT+ v:low+ vm0 af0 m_FI2 w6 DD2 NB tri K4 s_dp Yl0 E2 fwM Bw4 YF0_ fw a0 fwM1 m_FI3 Bw6 DD4 v:Bw3 E13 v:Bw5 E dA2+ v:E9 v:K5 s_Idf NB1 oT+ E1 Crm+ v:Bw2 fi6 v:K6 v:fi s_keep tri1 xl NB2 dA1+ dA3+ v:K7 v:fi2 ld_c v:Gn fi1 dA4+ dA+ Bw1 G1+ Lcv+ G3+ fi5 fi3 vl0 Lcv2+ G+ v:G2+ tri2 ext1+ Lcv1+ YF0_3 ext+ v:fi8 fi7 v:fi4 thW cl1+ v:th v:YF0_2 ftr2 ftr1 YF0_1 Lcv3+ ftr3 Ccv+ c41+ v:cl+ c4+ ftr bm1+ bm+ A2+ v:bc1+ bc+ v:A6+ v:A5+ u+ B5+ high+ dA5+ B4+ A+ A1+ B1+ dB4+ Ccv1+ A4+ f1+ dB5+ B+ F1 dB1+ A3+ bl+ B3+ th1 dB+ abs5+ B2+ u1+ D_+ v:dC+ v:yb3+ abs+ dB3+ abs1+ v:yb2+ dB2+ D1+ D+ abs2+ abs3+ abs4+ D2+ D3+ v:yb+ v:yb1+ D5+ D4+"
ROUND = "nod mx mp kq kp jq jp nf D_+ room Zq Wq Zp X Za n1 W_ W lq Zc new fq send Csc alp arr F6 aw lv Ysc l arM Fx v:x1 cnt eq Wx v:Fl kl am kt Fx1 FF1 FF Fg am1 sl v:x1l FF2 Lsc x2 Wm v:Fl1 Lsc1 Lsc4 Lsc2 Lsc3 Wb Lsc5 Lsc6 FF4 Wv Lsc7 v:FF3 vm Flg v:G+ v:vl thr Gx1 Gx ar ext1+ Yl1 v:G1+ Crm+ own a G2+ v:YF2 G3+ xb Yl YF3 YF1 ext+ ownT+ v:af v:YF v:cl+ c41+ v:cl1+ c4+ oT+ bm1+ A+ dA+ bm+ v:A1+ dA4+ dA3+ v:bc+ A2+ v:A4+ dA2+ high+ u+ B+ B1+ bc1+ A3+ bl+ dB+ st_le dA1+ low+ B2+ dB1+ dA5+ u1+ A5+ A6+ abs+ B3+ B4+ dB2+ f1+ abs1+ D+ B5+ dB3+ abs2+ dB4+ v:yb+ D1+ v:yb1+ dB5+ v:yb3+ abs3+ v:dC+ abs4+ abs5+ D3+ yb2+ D4+ D2+ D5+"
LAST = "v:nod mx mp kq kp jq jp nf X Zq W_ n1 Za Wq new Ysc W send lq v:fq st_yb st_yr room l alp F6 lv arM aw Fx1 FF1 v:ar arr eq Fx FF kl v:Fl1 kt sl Fl Lsc FF4 Lsc1 Lsc2 Lsc3 Lsc4 Lsc5 Lsc6 FF2 st_lo Lsc7 v:FF3 Gx v:fo fo1 Gx1 st_f st_yg"


FIRST = "m_FI ld_c0 i_p ld_f ld_t ld_l ld_y i_p5 i_J m_xb m_one pi1 pi4 pi3 i_Jm pi2 pi xl1 pf i_one cw3 m_FI1 pf1 pf2 i_dq w15 cw w12 Id w18 Im w13 cw1 lw1 i_Bt RH w16 R5 w19 E10 v:I128 cw2 E4 s_MS1 place K v:w4 w14 m_DD1 w w3 E6 s_Bt lw E11 v:fw1 E3 v:K1 i_JG R51 w11 E7 w1 v:E8 lw2 v:w7 i_trt w17 v:E12 w5 m_DD dq w2 E14 s_MS2 Fl0 w6 v:w8 E15 Go i_NI K2 Bw Yl0 af0 v:E5 v:w9 fw s_MS v:DD2 v:Gc K3 vm0 DD v:w10 Bw4 v:DD7 s_MS3 m_FI2 E2 DD3 fwM Bw3 v:DD5 v:K4 DD6 s_dp v:Bw5 Bw6 NB fwM1 DD4 m_FI3 a0 s_Idf E13 v:E9 v:K5 E tri s_keep DD1 ld_c tri1 G1+ v:E1 vl0 Crm+ NB1 fi6 xl v:Bw2 v:K6 Lcv+ G3+ v:Gn v:fi v:G2+ fi1 NB2 Lcv2+ th v:fi2 YF0_3 v:own0 v:K7 ownT+ ext1+ fi5 fi8 tri2 Bw1 Lcv1+ low+ fi3 oT+ G+ fi7 v:fi4 dA4+ v:YF0_2 dA+ dA2+ dA3+ Lcv3+ YF0_ ftr2 ext+ ftr dA1+ cl1+ ftr3 YF0_1 thW Ccv+ c41+ v:cl+ c4+ bm1+ ftr1 A2+ bm+ v:A6+ v:bc1+ v:A5+ F1 v:bc+ B5+ A+ B4+ high+ dA5+ B1+ A4+ dB5+ dB4+ u+ Ccv1+ A1+ B3+ A3+ dB1+ B+ dB3+ bl+ th1 B2+ th2 abs5+ dB+ abs1+ D_+ abs3+ m_nf m_c3 abs+ dB2+ abs2+ D+ D1+ abs4+ D2+ D3+ D4+ D5+ pb+"
ROUND = "f1 nod u1 mx pa mp kq kp nf D_+ v:jq X jp n1 cnt oP Zq Ws lv n2 ls new Wq room Zp Za am send alp Zc am1 W Csc lq am2 fq Ysc arM thr l F6 arr ar aw eq Fx FF v:x1 kl Fx1 Csc1 Fl kt FF1 Ysc1 Wx sl Lsc Fl1 Lsc1 FF2 v:x1l Fg Lsc2 x2 Lsc3 Wm Lsc4 Flg FF5 Lsc5 Lsc6 Wv v:FF3 vm a Wb Lsc7 v:FF4 G1+ Gx v:G+ Gx1 vl xb Yl v:G2+ G3+ ext+ v:own Yl1 YF1 v:YF ext1+ ownT+ v:cl+ v:YF2 YF3 v:cl1+ oT+ c4+ af c41+ v:low+ bm+ dA+ bm1+ A+ v:A1+ dA5+ Crm+ st_le high+ dA2+ A2+ v:bc+ v:bl+ dA3+ dA1+ B+ u+ A3+ dA4+ B1+ dB+ bc1+ A4+ B2+ A5+ dB1+ abs+ B3+ abs1+ dB2+ v:A6+ D+ B4+ dB3+ abs2+ D1+ B5+ dB4+ abs3+ dB5+ D2+ abs4+ abs5+ D3+ D4+ D5+ pb+"
LAST = "pa nod mx mp kq nf v:jq kp n1 jp X Zq oP Ws n2 room new Wq ls Za lv send v:alp W Ysc lq fq arM Ysc1 l F6 ar st_yr arr aw st_yb eq FF1 Fx kl kt Fx1 sl FF v:Fl Lsc Lsc1 Lsc2 v:Fl1 Lsc3 FF5 Lsc4 Lsc5 Lsc6 FF2 Lsc7 Gx v:FF3 st_lo v:FF4 fo Gx1 st_yg fo1 st_f"


FIRST = "ld_c0 m_FI i_p ld_f ld_l ld_y ld_t i_p5 i_J m_one pi4 pi1 m_xb pi i_Jm pi2 pi3 xl1 pf i_one m_FI1 pf1 pf2 Id i_Bt w15 Im w12 cw1 w13 RH w18 cw3 lw1 v:I128 i_dq w16 R5 w19 E4 v:w4 cw E10 s_MS1 cw2 K v:fw1 w14 m_DD1 w3 w E6 i_JG lw w1 R51 E7 s_Bt E11 v:w7 E3 place w11 v:E8 K1 m_DD s_MS2 dq lw2 w5 E14 i_trt Fl0 v:w8 E15 Go w2 Bw K2 i_NI w17 v:E12 af0 v:w9 w6 v:E5 DD3 v:DD2 s_MS K3 m_FI2 Yl0 E2 vm0 fw v:Gc s_MS3 v:DD5 Bw4 v:K4 v:Bw3 DD6 fwM v:DD7 DD4 tri w10 s_dp Bw6 v:Bw5 fwM1 v:K5 a0 NB s_Idf DD m_FI3 DD1 E E13 v:E1 s_keep ld_c NB1 G3+ vl0 tri1 fi6 Crm+ v:E9 v:K6 Lcv+ v:Gn xl G1+ v:Bw2 v:fi v:G2+ NB2 fi1 Lcv2+ YF0_3 v:fi2 v:own0 v:K7 ownT+ ext1+ tri2 Bw1 low+ fi5 oT+ Lcv1+ fi3 fi8 G+ dA4+ v:fi4 dA2+ fi7 v:YF0_2 dA+ dA3+ YF0_1 Lcv3+ ext+ v:cl1+ ftr2 ftr3 dA1+ th YF0_ c41+ ftr thW Ccv+ v:cl+ c4+ ftr1 A2+ bm+ bm1+ v:A6+ v:bc1+ v:A5+ F1 B5+ bc+ A+ B4+ high+ B1+ A4+ dA5+ dB5+ dB4+ u+ Ccv1+ A1+ B3+ A3+ dB1+ B+ dB3+ bl+ B2+ th1 th2 abs1+ D_+ dB+ abs3+ v:yb+ abs+ dB2+ v:yb1+ abs2+ v:yb2+ D+ m_nf m_c3 D1+ abs5+ abs4+ D2+ D3+ D4+ D5+ pb+"
ROUND = "nod f1 mx pa mp kq u1 kp nf v:jq D_+ X jp n1 cnt oP Zq Ws room new Zp am Wq ls Za send am1 Zc alp Csc am2 W lq Ysc thr fq arM Csc1 l arr F6 ar aw lv eq Fx FF1 v:x1 kl Wx kt Ysc1 FF sl Fx1 Lsc v:x1l Lsc1 Fl x2 FF2 Fg Lsc2 v:Fl1 Lsc3 Wm Lsc4 Lsc5 FF5 v:Flg Wv Lsc6 v:FF3 vm a Wb Lsc7 v:FF4 G1+ Gx v:G+ Gx1 vl xb Yl v:G2+ G3+ ext+ v:own YF1 v:Yl1 ext1+ v:YF ownT+ cl+ v:YF2 YF3 c4+ oT+ v:cl1+ c41+ A+ bm+ v:A1+ dA+ dA5+ st_le A2+ dA2+ v:bc+ v:low+ bm1+ dA4+ B+ dA3+ high+ dA1+ bc1+ A3+ B1+ dB+ A4+ B2+ af dB1+ A5+ Crm+ u+ abs+ B3+ dB2+ abs1+ v:A6+ D+ B4+ dB3+ abs2+ B5+ dB4+ v:yb+ D1+ abs3+ dB5+ D2+ abs4+ v:yb1+ abs5+ D3+ v:yb2+ bl+ D4+ D5+ pb+"
LAST = "pa v:nod mx mp kq nf kp jq X jp Zq Ws oP n1 room Wq new ls Za Ysc send W v:alp lq fq Ysc1 arM F6 l st_yr st_yb ar arr aw lv eq Fx FF1 kl Fx1 kt FF sl v:Fl Lsc Lsc1 Fl1 Lsc2 FF5 Lsc3 Lsc4 Lsc5 FF2 Lsc6 Gx Lsc7 v:FF3 st_lo v:FF4 fo Gx1 st_yg fo1 st_f"


def R(name, a, b, step=1, p0=0, p1=128, ps=1):
    return ("r", name, a, b, step, p0, p1, ps)


def IND(win, off):
    return ("i", win, off)


def isap(x):
    return isinstance(x, tuple)


def ap(T, x):
    if not isap(x):
        return x
    if x[0] == "i":
        return ap(T, x[1]).indirect(ap(T, x[2]))
    cs = slice(x[2], x[3]) if x[4] == 1 else slice(x[2], x[3], x[4])
    ps = slice(x[5], x[6]) if x[7] == 1 else slice(x[5], x[6], x[7])
    return T[x[1]][ps, cs]


def build():
    ops = []
    rnd = [-1]
    used = {}

    def add(eng, calls, rd, wr, name, kind="c", group=None):
        r2 = []
        w2 = []
        for x in rd:
            if isap(x):
                r2 += [x[1], x[2]] if x[0] == "i" else [x]
        for x in wr:
            if x[0] == "i":
                w2.append(x[1])
                r2.append(x[2])
            else:
                w2.append(x)
        k = used.get((rnd[0], name), 0)
        used[(rnd[0], name)] = k + 1
        ops.append({"eng": eng, "calls": calls, "rd": r2, "wr": w2, "kind": kind, "name": name + (str(k) if k else ""), "t": rnd[0], "group": group})

    def cp(out, a, name):
        add("v", [("tensor_copy", (out, a), {})], [a], [out], name)

    def tt(out, a, b, op, name):
        add("v", [("tensor_tensor", (out, a, b, op), {})], [a, b], [out], name)

    def ts(out, a, s1, o1, s2, o2, name):
        args = (out, a, s1, None, o1) if o2 is None else (out, a, s1, s2, o1, o2)
        add("v", [("tensor_scalar", args, {})], [a, s1, s2], [out], name)

    def scan(out, d0, d1, first, o0, o1, name):
        add("v", [("tensor_tensor_scan", (out, d0, d1, first, o0, o1), {})], [d0, d1], [out], name)

    def ms(out, val, name):
        add("v", [("memset", (out, val), {})], [], [out], name)

    def act(out, a, name, f=AF.Identity, bias=0.0, scale=1.0):
        add("a", [("activation", (out, a, f), {"bias": bias, "scale": scale})], [a, bias, scale], [out], name)
        if f == AF.Identity:
            if scale == 1.0 and bias == 0.0:
                ops[-1]["alt"] = [("tensor_copy", (out, a), {})]
            else:
                ops[-1]["alt"] = [("tensor_scalar", (out, a, scale, bias, OP.mult, OP.add), {})]

    def mm(items, name, group=None):
        add("p", [("matmul", x, {}) for x in items], [x[1] for x in items] + [x[2] for x in items], [x[0] for x in items], name, group=group)

    def acc(out, pairs, name):
        mm([(out, l, r, j == 0, j == len(pairs) - 1) for j, (l, r) in enumerate(pairs)], name)

    def iota(out, pat, base, cm, name):
        kw = {} if SCRATCH[out[1]][2] == "int32" else {"allow_small_or_imprecise_dtypes": True}
        add("g", [("iota", (out, pat, base, cm), kw)], [], [out], name)

    def sel(out, a, pat, op, fill, base, cm, name):
        add("g", [("affine_select", (out, a, pat, op, fill, base, cm), {})], [a], [out], name)

    def gcopy(out, a, name):
        sel(out, a, [[0, out[3] - out[2]]], OP.is_ge, 0.0, 0, 0, name)

    def dma(q, out, a, name, after=()):
        add(q, [("dma_start", (out, a), {})], ([a] if a[1] in SCRATCH else []) + list(after), [out] if out[1] in SCRATCH else [], name, kind="d")

    def col(k):
        return R("col", k, k + 1)

    def rh(k):
        return R("RH", k, k + 1)

    def X(name):
        return R(name, 0, 128)
    Id, one = X("Id"), X("one")

    def shift(w, r):
        return R("Bw", 144 * w + 15 - r, 144 * w + 143 - r)

    def rows(out, w, src, a, b, name, first=None):
        acc(out, ([] if first is None else [(Id, first)]) + [(shift(w, r), R(src, a + r, b, 16)) for r in range(16)], name)

    dma("s", R("Ci", 0, 128), R("cl", 0, 128), "ld_c0")
    dma("a", R("fwi", 0, 120), R("fw0", 0, 120), "ld_f")
    dma("s", R("Li", 0, 2048), R("lk", 0, 2048), "ld_l")
    dma("a", R("Y", BS, YW), R("y0", 0, W0), "ld_y")
    dma("a", R("thi", 0, 128, 1, 0, 8), R("th", 0, 128, 1, 0, 8), "ld_t")
    dma("s", R("Ci", 128, 1024), R("cl", 128, 1024), "ld_c", [R("Li", 0, 2048)])
    iota(R("pi", 0, 1), [[0, 1]], 0, 1, "i_p")
    iota(R("pi", 6, 7), [[0, 1]], 11, 1, "i_p5")
    iota(R("J", 0, 152), [[1, 152]], 0, 0, "i_J")
    iota(X("JG"), [[1, 8], [0, 16]], 0, 0, "i_JG")
    iota(X("Jm"), [[1, 16], [16, 8]], 0, 0, "i_Jm")
    iota(X("onf"), [[0, 128]], 1, 0, "i_one")
    iota(X("trt"), [[0, 8], [1, 16]], 0, 0, "i_trt")
    iota(X("NI"), [[0, 4], [1, 32]], 1, 0, "i_NI")
    iota(X("dq"), [[0, 128]], -2, 0, "i_dq")
    sel(X("dp"), X("onf"), [[0, 8], [-1, 16]], OP.is_gt, -1.0, 15, 0, "s_dp")
    sel(X("keep"), X("onf"), [[0, 8], [1, 16]], OP.is_gt, 0.0, 0, 0, "s_keep")
    sel(X("Idf"), X("onf"), [[1, 128]], OP.is_equal, 0.0, 0, -1, "s_Idf")
    iota(R("Bt", 0, 144), [[0, 144]], -int(KEY), 0, "i_Bt")
    sel(R("Bt", 0, 144), R("Bt", 0, 144), [[1, 144]], OP.is_equal, 0.0, -15, -16, "s_Bt")
    for j in range(4):
        sel(R("MS", 128 * j, 128 * j + 128), X("onf"), [[32, 4], [1000, 2], [1, 16]], OP.is_equal, 0.0, 16 * (j // 2) - 1000 * (j % 2), -1, "s_MS")
    ms(one, 1.0, "m_one")
    for h in range(0, WA, 608):
        ms(R("FI", h, h + 608), 0.0, "m_FI")
    for h in range(0, 2048 if PACK else 4096, 1024):
        ms(R("DD", h, h + 1024), 0.0, "m_DD")
    ms(R("xb", 0, 8), -19.0, "m_xb")
    ms(R("nf", 8, 9), 7.5 / 16, "m_nf")
    ms(X("c3"), 393216.0, "m_c3")
    ts(R("pi", 1, 2), R("pi", 0, 1), 15, OP.bitwise_and, None, None, "pi")
    ts(R("pi", 2, 3), R("pi", 0, 1), 4, OP.arith_shift_right, None, None, "pi")
    ts(R("pi", 3, 4), R("pi", 6, 7), 15, OP.bitwise_and, None, None, "pi")
    ts(R("pi", 4, 5), R("pi", 0, 1), 1, OP.bitwise_and, None, None, "pi")
    ts(R("pi", 5, 6), R("pi", 0, 1), 7, OP.bitwise_and, None, None, "pi")
    cp(R("pf", 0, 6), R("pi", 0, 6), "pf")
    pP, pR, pG, pO, p8, p5, pW = [R("pf", k, k + 1) for k in (0, 1, 2, 4, 5, 6, 7)]
    act(p5, pG, "pf", bias=R("pf", 3, 4), scale=16.0)
    act(pW, pG, "pf", bias=15.0, scale=16.0)
    ts(Id, X("J"), pP, OP.is_equal, None, None, "Id")
    ts(X("R5"), X("J"), p5, OP.is_equal, 4096.0 if PACK else 1.0, OP.mult, "R5")
    if PACK:
        tt(X("R5"), X("R5"), Id, OP.add, "R5")
    ts(R("RH", 0, 16), R("J", 0, 16), pR, OP.is_equal, None, None, "RH")
    ts(X("Go"), X("JG"), pG, OP.is_equal, None, None, "Go")
    ts(R("Bw", 0, 144), R("J", 0, 144), pW, OP.is_equal, None, None, "Bw")
    ts(X("Im"), X("Jm"), pP, OP.is_equal, None, None, "Im")
    for j, m in enumerate(("R5",) if PACK else ("Id", "R5")):
        for h in range(8):
            act(R("DD", 2048 * j + 256 * h, 2048 * j + 256 * h + 256, 17), R(m, 16 * h, 16 * h + 16), "DD")
    for k in range(16):
        act(R("E", k, 2048, 16), X("Im"), "E")
    act(R("K", 0, 16), R("RH", 0, 16), "K")
    for k in range(4, 11):
        act(R("K", 2 ** k, 2 ** (k + 1)), R("K", 0, 2 ** k), "K")
    act(col(0), rh(1), "w", bias=rh(0), scale=128.0)
    act(col(1), rh(3), "w", bias=col(0), scale=-2432.0)
    act(col(2), rh(2), "w", bias=col(1), scale=-2432.0)
    act(col(3), rh(2), "w", bias=rh(4))
    act(col(4), rh(3), "w", bias=rh(5))
    act(col(5), col(4), "w", scale=-19.0, bias=col(3))
    act(col(6), col(5), "w", scale=128.0)
    act(col(7), rh(3), "w", bias=rh(4))
    act(col(18), rh(2), "w", bias=rh(6), scale=-8.0)
    act(col(8), col(7), "w", bias=col(18))
    act(col(9), col(7), "w", bias=rh(5))
    act(col(10), rh(6), "w", scale=-4096.0)
    act(col(11), pR, "w", bias=2048.0)
    act(col(12), pR, "w", scale=-128.0, bias=KEY)
    act(col(17), pR, "w", scale=256.0, bias=2.0 ** 23 - 2018)
    act(col(13), pO, "w", scale=128.0)
    act(R("col", 20, 24), R("J", 15, 19), "w", scale=col(13))
    act(col(14), pR, "w", scale=8.0)
    act(col(15), pR, "w", scale=0.125)
    act(col(16), p8, "w", scale=15.875, bias=col(15))
    for w, c in ((1, col(0)), (2, col(1)), (3, col(2)), (4, col(6)), (5, col(3)), (6, KEY)):
        act(R("Bw", 144 * w, 144 * w + 144), R("Bw", 0, 144), "Bw", scale=c)
    act(X("Gn"), X("Go"), "Gn", scale=col(10))
    act(X("Gc"), X("Go"), "Gc", scale=-KEY)
    act(X("I128"), Id, "I128", scale=128.0)
    ts(X("eq"), X("trt"), pR, OP.is_gt, -8192.0, OP.mult, "tri")
    ts(X("kl"), X("trt"), pR, OP.is_equal, 4096.0, OP.mult, "tri")
    tt(X("tri"), X("eq"), X("kl"), OP.add, "tri")
    ts(X("place"), X("J"), -1.0, OP.mult, col(12), OP.add, "place")
    act(R("dq", 15, 128, 16), R("J", 0, 8), "dq", bias=col(17), scale=32.0)
    act(R("lwf", 0, 8), R("J", 0, 8), "lw", bias=col(16), scale=2.0)
    act(R("lwf", 8, 16), R("J", 0, 8), "lw", bias=pR, scale=16.0)
    act(R("lw", 0, 16), R("lwf", 0, 16), "lw")
    cp(R("vm", 0, 8), R("lwf", 0, 8), "vm0")
    ts(R("vl", 0, 8), R("lwf", 8, 16), 512.0, OP.add, None, None, "vl0")
    ts(R("xl", 0, 8), R("J", 0, 8), col(14), OP.add, None, None, "xl")
    cp(R("xl", 8, 16), R("J", 0, 8), "xl")
    ts(R("cw", 8, 16), R("J", 0, 8), 0.0, OP.mult, None, None, "cw")
    ts(R("cw", 16, 24), R("J", 0, 8), 0.0, OP.mult, -float(OFF), OP.add, "cw")
    ts(R("cw", 24, 32), R("lwf", 8, 16), float(WA - OFF), OP.add, None, None, "cw")
    ts(R("cw", 32, 40), R("J", 0, 8), 0.0, OP.mult, 19.0 - OFF, OP.add, "cw")
    ts(X("NI"), X("NI"), 7, OP.bitwise_and, None, None, "NB")
    ts(X("NB"), X("NI"), rh(2), OP.mult, col(8), OP.add, "NB")
    act(R("NB", 19, 128, 32), R("J", 7, 11), "NB", bias=col(9), scale=rh(2))
    act(X("al"), IND(R("Ci", 0, 128), R("vm", 0, 8)), "a0")
    act(X("af"), R("Ci", 0, 128), "af0")
    act(R("Yl", 0, 120), R("fwi", 0, 120), "Yl0")
    act(R("Fl", 64, 120), R("fwi", 64, 120), "Fl0")
    act(R("thf", 0, 128, 1, 0, 8), R("thi", 0, 128, 1, 0, 8), "th")
    acc(R("P7", 0, 8), [(R("Bt", 15 - r, 143 - r, 1, 0, 8), R("thf", r, 128, 16, 0, 8)) for r in range(16)], "thW")
    act(R("th0", 0, 8), R("P7", 0, 8), "th", bias=-KEY)
    act(R("th0", 8, 16), R("P7", 0, 8), "th", bias=-8.5 * KEY)
    act(R("fwf", 0, 120), R("fwi", 0, 120), "fw")
    act(R("fwf", 120, 152), R("J", 120, 152), "fw", bias=pR, scale=16.0)
    for j in range(2):
        acc(R("P6", j, 152, 2), [(R("MS", 256 * j, 256 * j + 128), R("fwf", 0, 152, 2)), (R("MS", 256 * j + 128, 256 * j + 256), R("fwf", 1, 152, 2))], "fwM")
    V, t1 = R("t4", 0, 152), R("t1", 0, 152)

    def fi(k, a=0, b=WA):
        return R("FI", a + k, b, 16)
    act(t1, R("P6", 0, 152), "fi", bias=24576.0 - 63.5)
    act(V, R("P6", 0, 152), "fi", bias=24576.0)
    act(fi(1), t1, "fi", bias=-192.0, scale=1.0 / 128)
    tt(fi(0), V, t1, OP.subtract, "fi")
    for k in (2, 5):
        ts(fi(k, 0, W0), R("t4", 0, 120), 24576.0 + 1024, OP.is_ge, None, None, "fi")
    ms(fi(3, W0), 1.0, "fi")
    ts(fi(4, 0, W0), fi(1, 0, W0), 8.0, OP.min, None, None, "fi")
    act(fi(4, W0), fi(1, W0), "fi")
    for h in range(0, WA, 608):
        add("v", [("transpose", (R("F0", h, h + 608), R("FI", h, h + 608)), {})], [R("FI", h, h + 608)], [R("F0", h, h + 608)], "ftr")
    gcopy(R("F1", W0, WA), R("F0", W0, WA), "F1")
    for a in range(0, W0, 480):
        act(R("YF", a, a + 480), IND(R("Y", BS, YW), R("Yl", a // 16, a // 16 + 30)), "YF0_", scale=0.5)
    act(X("own"), R("Y", BS, BS + 128), "own0")

    for t in range(RO):
        last = t == RO - 1
        rnd[0] = t
        cur, nxt = ("F0", "F1") if t % 2 == 0 else ("F1", "F0")
        Wt = W0 + S * t
        Wn = Wt + S
        Lw = R("Li", 0, 2048) if t == 0 else R("L", 0, 2048)
        YFw = R("YF", 0, Wt)
        Fw = R(cur, 0, WD)
        own, af = X("own"), X("af")
        vl = R("vl", 8 * t, 8 * t + 8)
        for a in range(0, 2048, 512):
            act(R("G", a, a + 512), IND(Lw, R("al", a // 16, a // 16 + 32)), "G", bias=-float(OFF))
        for h in range(2):
            pb = "P%d" % (4 + h)
            hb = R(pb, 0, 64)
            if PACK:
                acc(hb, [(R("DD", k, 2048, 16), R("G", 1024 * h + k, 1024 * h + 1024, 16)) for k in range(16)], "ext")
                act(R("bc", 128 * h, 128 * h + 64), hb, "cl", bias=float(OFF), scale=1.0 / 4096)
                ts(R("c4", 64 * h, 64 * h + 64), hb, RND / 8, OP.add, -RND / 8, OP.add, "c4")
                tt(R("bm", 64 * h, 64 * h + 64), hb, R("c4", 64 * h, 64 * h + 64), OP.subtract, "bm")
                act(R("bc", 128 * h + 64, 128 * h + 128), R("bm", 64 * h, 64 * h + 64), "bc", bias=float(OFF))
            else:
                for j in range(2):
                    acc(R(pb, 64 * j, 64 * j + 64), [(R("DD", 2048 * j + k, 2048 * j + 2048, 16), R("G", 1024 * h + k, 1024 * h + 1024, 16)) for k in range(16)], "ext")
                act(R("bc", 128 * h, 128 * h + 128), R(pb, 0, 128), "bc", bias=float(OFF))
                act(R("bm", 64 * h, 64 * h + 64), hb, "bm")
        act(X("bl"), IND(X("bm"), R("xl", 0, 8)), "bl")
        if t == 0:
            for h in range(0, 2048, 512):
                gcopy(R("L", h, h + 512), R("Li", h, h + 512), "Lcv")
            for h in range(0, 1024, 512):
                gcopy(R("C", 512 + h, 1024 + h), R("Ci", h, h + 512), "Ccv")
        if not last:
            gcopy(R("C", S * t, S * t + S), af, "Crm")
        acc(R("P0", 0, 128), [(own, Id)], "ownT")
        act(X("oT"), R("P0", 0, 128), "oT", scale=-1.0)
        mm([(X("P7"), Id, X("place"), True, False)], "D_", "D")
        for (a, b, pb) in PIECES:
            mm([(R(pb, 0, b - a), X("oT"), R("E", a, b), True, False)], "dA", pb)
        for (a, b, pb) in PIECES:
            o = 64 * (a // 1024)
            for (c, d) in ((a, b),) if a else ((0, 256), (256, 512)):
                act(R("A", c, d), IND(YFw, R("bc", o + c // 16, o + d // 16)), "A", bias=1023.75)
            tt(R("B", a, b), IND(YFw, R("bc", o + 64 + a // 16, o + 64 + b // 16)), R("A", a, b), OP.add, "B")
            mm([(R(pb, 0, b - a), Id, R("B", a, b), False, True)], "dB", pb)
            act(R("ab", a, b), R(pb, 0, b - a), "abs", AF.Abs, -1024.0)
            mm([(X("P7"), shift(6, r), R("ab", 128 * r, 128 * r + 128), False, r == 15) for r in range(a // 128, b // 128)], "D", "D")
        for (a, b) in YBP:
            act(R("yb", a, b), R("B", a, b), "yb", bias=-1024.0)
        act(X("low"), own, "low", bias=-1.0)
        acc(R("P5", 256, 384), [(Id, own), (Id, one)], "high")
        if not last:
            acc(R("P5", 0, 128), [(X("Go"), own), (X("Idf"), af)], "u")
            act(X("f1"), R("P5", 0, 128), "f1", bias=1022.5 - t - 393216.0, scale=-1.0)
            acc(R("P5", 128, 256), [(X("Go"), own), (Id, X("f1")), (Id, X("c3"))] + [(Id, one)] * (t + 1), "u")
            acc(R("P5", 384, 512), [(Id, X("bl"))], "pb")
        acc(R("P5", 0, 128), [(X("Idf"), af)], "pa")
        jq, jp = R("jl", 0, 8), R("jl", 8, 16)
        scan(R("mx", 0, 128), X("P7"), X("dq"), BIG, OP.min, OP.add, "mx")
        ts(R("kj", 0, 8), R("mx", 15, 128, 16), 2047, OP.bitwise_and, None, None, "kq")
        act(jq, R("kj", 0, 8), "jq")
        scan(R("mx", 128, 256), X("P7"), X("dp"), 0.0, OP.max, OP.mult, "mp")
        ts(R("kj", 8, 16), R("mx", 143, 256, 16), 2047, OP.bitwise_and, None, None, "kp")
        act(jp, R("kj", 8, 16), "jp")
        tt(R("nf", 0, 8), R("mx", 143, 256, 16), R("thr" if t else "th0", 0, 8), OP.is_ge, "nf")
        tt(R("X", 0, 8), R("nf", 0, 8), R("xb", 8 * t, 8 * t + 8), OP.mult, "X")
        if not last:
            acc(R("P6", 448, 449), [(X("Gc"), R("nf", c, c + 1)) for c in range(9)], "cnt")
            act(R("am", 0, 1), R("P6", 448, 449), "am", bias=RND)
            act(R("am", 1, 2), R("am", 0, 1), "am", bias=-RND)
            act(R("am", 2, 3), R("P6", 448, 449), "am", bias=R("am", 1, 2), scale=-1.0)
            act(R("thr", 0, 8), R("th0", 8, 16), "thr", bias=R("am", 2, 3))
        nw = R("new", S * t, S * t + S)
        tt(X("n1"), IND(R("yb", 0, 2048), jq), X("low"), OP.max, "n1")
        tt(nw, X("n1"), R("P5", 256, 384), OP.min, "new")
        gh = GA if t % 2 == 0 else GB
        add("g", [("send", (nw, gh, t), {})], [nw], [R("@%d" % t, 0, 1)], "send", kind="s")
        add("x", [("arr", (t,), {})], [R("@%d" % t, 0, 1)], [R("Y", gh, gh + 896)], "arr", kind="x")
        act(R("Y", RM + S * t, RM + S * t + S), IND(R("yb", 0, 2048), jp), "room")
        for h in range(0, 8, SC):
            cp(IND(R("Y", RM, GB), R("vl", 8 * t + h, 8 * t + h + SC)), R("new", S * t + 16 * h, S * t + 16 * (h + SC)), "Ysc")
        Kw = R("K", 0, 2048)
        tt(R("Z", 0, 128), IND(Kw, jq), X("bl"), OP.mult, "Zq")
        rows(R("P2", 0, 8), 0, "Z", 0, 128, "Wq")
        act(R("l1", 0, 8), R("P2", 0, 8), "lq", bias=float(OFF))
        act(X("oP"), IND(Kw, jp), "oP")
        if not last:
            tt(R("Z", 128, 256), R("P5", 384, 512), X("oP"), OP.mult, "Zp")
        tt(R("Z", 256, 384), R("P5", 0, 128), X("oP"), OP.mult, "Za")
        mm([(R("P3", 24, 40), Id, R("cw", 24, 40), True, False), (R("P3", 24, 32), X("I128"), R("X", 0, 8), False, False),
            (R("P3", 32, 40), Id, R("X", 0, 8), False, True)], "Ws")
        act(R("l1", 24, 40), R("P3", 24, 40), "ls", bias=float(OFF))
        rows(R("P0", 8, 24), 0, "Z", 128, 384, "W", R("cw", 8, 24))
        act(R("l1", 8, 24), R("P0", 8, 24), "l", bias=float(OFF))
        bq, bp, aP, vs, vb = [R("l1", 8 * k, 8 * k + 8) for k in range(5)]
        act(X("fq"), IND(Fw, bq), "fq")
        cp(IND(Fw, vs), X("fq"), "F6")
        act(X("alp"), IND(R("NB", 32 * t, 32 * t + 32), vb), "alp")
        if not last:
            act(X("x1"), IND(Fw, bp), "x1")
            rows(R("P2", 0, 8), 1, "x1", 0, 128, "Wx")
            act(R("x1l", 0, 8), R("P2", 0, 8), "x1l")
            tt(X("x2"), IND(Fw, R("x1l", 0, 8)), X("alp"), OP.mult, "x2")
            acc(R("P2", 8, 16), [(Id, R("lw", 0, 8))] + [(shift(4, r), R("x2", 16 * (r % 8) + r // 8, 16 * (r % 8) + 16, 2)) for r in range(16)], "Wm")
            act(R("vm", 0, 8), R("P2", 8, 16), "vm", bias=512.0)
            tt(X("Zc"), R("P5", 128, 256), X("oP"), OP.mult, "Zc")
            for h in range(0, 8, SC):
                tt(IND(R("C", 0, 1536), R("vl", 8 * t + h, 8 * t + h + SC)), R("Zc", 16 * h, 16 * (h + SC)), R("af", 16 * h, 16 * (h + SC)), OP.add, "Csc")
            act(X("al"), IND(R("C", 0, 1536), R("vm", 0, 8)), "a")
        for j, (a, e) in enumerate(((0, 1024), (W0, Wt))):
            if e > a:
                rows(R("P%d" % (3 + j), 0, (e - a) // 16), 1, cur, a, e, "Fx")
                act(R("Fl", a // 16, e // 16), R("P%d" % (3 + j), 0, (e - a) // 16), "Fl")
        acc(R("P1", 0, 128), [(Id, X("tri")), (X("Go"), R("Z", 256, 384)), (X("Gn"), X("alp"))], "arM")
        act(X("ar"), R("P1", 0, 128), "ar", scale=1.0 / 4096)
        act(R("aw", 0, 8), aP, "aw", scale=1.0 / 4096)
        act(X("nod"), X("J"), "nod", bias=col(20 + t), scale=pO)
        tt(X("eq"), IND(R("aw", 0, 8), R("xl", 8, 16)), X("ar"), OP.is_equal, "eq")
        scan(X("kl"), X("keep"), X("eq"), 0.0, OP.mult, OP.max, "kl")
        tt(R("kt", 0, 8), R("kl", 15, 128, 16), R("aw", 0, 8), OP.add, "kt")
        ts(R("sl", 0, 16, 2), R("kt", 0, 8), 4096.0, OP.mult, col(11), OP.min, "sl")
        act(X("lv"), IND(R("L", 0, 2048), aP), "lv")
        for c in range(7, -1, -1):
            tt(IND(R("L", 0, 2064), R("sl", 2 * c, 2 * c + 1)), R("lv", 16 * c, 16 * c + 16), R("nod", 16 * c, 16 * c + 16), OP.max, "Lsc")
        if t == 0:
            dma("s", R("lo", 0, 2048, 1, 0, 128, 2), R("L", 0, 2048, 1, 0, 128, 2), "st_le")
        if last:
            dma("s", R("lo", 0, 2048, 1, 1, 128, 2), R("L", 0, 2048, 1, 1, 128, 2), "st_lo")
            dma("s", R("yo", 0, 1024), R("Y", BS, GB), "st_yb")
            dma("s", R("yo", W0, WA), R("Y", RM, BS), "st_yr")
            dma("s", R("yo", 1024, W0), R("Y", GB, YW), "st_yg")
        else:
            vn = R("vl", 8 * t + 8, 8 * t + 16)
            rows(R("P0", 64, 72), 4, "x2", 0, 128, "Wv", R("lw", 8, 16))
            rows(R("P0", 72, 80), 5, "x2", 0, 128, "Wb")
            act(vn, R("P0", 64, 72), "vl", bias=512.0)
            act(R("xb", 8 * t + 8, 8 * t + 16), R("P0", 72, 80), "xb", bias=-19.0)
            act(af, IND(R("C", 0, 1536), vn), "af")
            act(own, IND(R("Y", RM, GB), vn), "own")
        for (a, b) in FFP + ((W0, Wt),):
            if b > a:
                act(R(nxt, a, b), IND(Fw, R("Fl", a // 16, b // 16)), "FF")
        if not last:
            rows(R("P1", 384, 440), 1, nxt, 1024, W0, "Fg")
            act(R("Fl", 64, 120), R("P1", 384, 440), "Flg")
        win = R("Y", GA, GB) if t % 2 == 0 else R("Y", RM, YW)
        for j, (a, e) in enumerate(((1024, Wn), (0, 1024))):
            pb = ("P6", "P3")[j]
            n = (e - a) // 16
            rows(R(pb, 0, n), 1 if last else 3 - t % 2, nxt, a, e, "Gx")
            if last:
                act(R("fof", a // 16, e // 16), R(pb, 0, n), "fo")
            else:
                act(R("Yl", a // 16, e // 16), R(pb, 0, n), "Yl", bias=1408.0 if t % 2 == 0 else 512.0)
                for (c, d) in ((a, a + 512), (a + 512, e)):
                    act(R("YF", c, d), IND(win, R("Yl", c // 16, d // 16)), "YF", scale=0.5)
        if last:
            dma("a", R("fo", 0, 152), R("fof", 0, 152), "st_f")
    return ops


def meet(x, y, same):
    if x[1][0] == "P" and not same:
        return True
    return x[2] < y[3] and y[2] < x[3] and x[5] < y[6] and y[5] < x[6] and (x[4] != y[4] or (x[2] - y[2]) % x[4] == 0)


def links(ops):
    hist = {}
    for i, o in enumerate(ops):
        pre = set()
        o["raw"] = set()
        for w0, xs in ((False, o["rd"]), (True, o["wr"])):
            for x in xs:
                for (j, y, w) in hist.get(x[1], []):
                    same = ops[j]["eng"] == "p" and o["eng"] == "p"
                    if (w or w0 or (x[1][0] == "P" and not same)) and meet(x, y, same):
                        pre.add(j)
                        if w or o["kind"] != "c" or ops[j]["kind"] != "c":
                            o["raw"].add(j)
        if o["group"]:
            pre |= set([j for j in range(i) if ops[j]["group"] == o["group"] and ops[j]["t"] == o["t"]][-1:])
        o["soft"] = [j for j in pre if o["group"] and ops[j]["group"] == o["group"] and ops[j]["t"] == o["t"]]
        o["pre"] = sorted(pre)
        for w0, xs in ((False, o["rd"]), (True, o["wr"])):
            for x in xs:
                h = hist.get(x[1], [])
                if x[1][0] == "P" and o["eng"] != "p":
                    h = [z for z in h if z[0] == i]
                elif w0 and x[4] == 1 and x[7] == 1 and x[1][0] != "P":
                    h = [z for z in h if z[0] == i or not (x[2] <= z[1][2] and z[1][3] <= x[3] and x[5] <= z[1][5] and z[1][6] <= x[6])]
                hist[x[1]] = h + [(i, x, w0)]


def plan(first=None, mid=None, end=None):
    ops = build()
    links(ops)
    at = {(o["t"], o["name"]): i for i, o in enumerate(ops)}
    want = []
    for t, names in ((-1, first or FIRST), (0, mid or ROUND), (1, mid or ROUND), (2, mid or ROUND), (3, end or LAST)):
        for w in names.split():
            e, nm = w.split(":") if ":" in w else (None, w)
            i = at.get((t + 1, nm[:-1]) if nm[-1] == "+" else (t, nm))
            if i is not None:
                want.append(i)
                if e == "v" and "alt" in ops[i]:
                    ops[i]["eng"] = "v"
                    ops[i]["calls"] = ops[i]["alt"]
    order = []
    done = set()
    for i0 in want + list(range(len(ops))):
        stack = [i0]
        while stack:
            i = stack[-1]
            miss = [j for j in ops[i]["pre"] if j not in done]
            if miss:
                stack.append(miss[0])
            else:
                stack.pop()
                if i not in done:
                    done.add(i)
                    order.append(i)
    return ops, order


PLAN = []


def helpers(T, topo, r):
    core = T.cores[r]
    far = [k for k in range(N) if topo.chip(T.cores[k]) != topo.chip(core)]
    aides = [c for c in topo.cores_of(core) if topo.die(c) == topo.die(core) and T.rank_of(c) is None][:HELP]
    m = len(far) // (len(aides) + 1)
    return aides, [far[m * j:m * j + m] for j in range(len(aides) + 1)]


def dst(topo, c):
    return DstId(rid=topo.addr(c)[0], pnc=topo.addr(c)[1])


def rank_program(g, core, T, topo):
    rank = T.rank_of(core)
    if rank is None:
        for r in range(N):
            aides, shares = helpers(T, topo, r)
            if core in aides:
                grp = shares[1 + aides.index(core)]
                eng = topo.engines(core, T.cores[grp[0]])
                for t in range(RO):
                    gh = GA if t % 2 == 0 else GB
                    g.wait_ge(T.sem["hop%d" % t], len(topo.engines(T.cores[r], core)))
                    at = [gh + S * ((r - k - 1) % N) for k in grp]
                    g.remote_dma_fused([RemoteDMATransfer(dst_ids=[dst(topo, T.cores[k]) for k in grp],
                                                          dma_engine_mask=sum(1 << k for k in eng), remote_sem=T.sem["arr%d" % t],
                                                          srcs=[T.new[:, S * t:S * t + S]], dsts=[T.Y[:, a:a + S] for a in at])], local_sem=T.sem.sent)
                g.wait_ge(T.sem.sent, RO * len(eng))
        return
    aides, shares = helpers(T, topo, rank)
    mine = shares[0]
    if not PLAN:
        PLAN.append(plan())
    ops, order = PLAN[0]
    q = {"v": g.vector, "a": g.scalar, "p": g.tensor, "g": g, "s": g.sync}
    csem = {"v": "sv", "a": "sa", "p": "sp", "g": "sg"}
    peers = [r for r in range(N) if r != rank]
    far = [r for r in peers if topo.chip(T.cores[r]) != topo.chip(core)]
    near = [r for r in peers if r not in far]
    fe = [e for e in topo.engines(core, T.cores[far[0]]) if all(e in topo.engines(core, T.cores[r]) for r in far)]
    ne = [e for e in topo.engines(core, T.cores[near[0]]) if e not in fe]
    arrive = len(far) * len(fe) + len(near) * len(ne)
    done = {}
    total = {}
    seen = {}
    nd = [0]

    def wait(e, s, v):
        if seen.get((e, s), 0) < v:
            q[e].wait_ge(T.sem[s], v)
            seen[(e, s)] = v

    for i in order:
        o = ops[i]
        e = o["eng"]
        if o["kind"] == "x":
            t = o["calls"][0][1][0]
            done[i] = ("arr%d" % t, arrive)
            total["arr%d" % t] = arrive
            continue
        need = {}
        for j in o["pre"]:
            if j not in o["soft"] and (j in o["raw"] or ops[j]["eng"] != e):
                s, v = done[j]
                need[s] = max(need.get(s, 0), v)
        for s in sorted(need):
            wait(e, s, need[s])
        if o["kind"] == "s":
            src, gh, t = o["calls"][0][1]
            he = topo.engines(core, aides[0])
            g.remote_dma_fused([RemoteDMATransfer(dst_ids=[dst(topo, h) for h in aides], dma_engine_mask=sum(1 << k for k in he),
                                                  remote_sem=T.sem["hop%d" % t], srcs=[ap(T, src)], dsts=[ap(T, src) for h in aides])], local_sem=T.sem.sent)
            trs = []
            for grp, eng in ((mine, fe), (near, ne)):
                at = [gh + S * ((rank - r - 1) % N) for r in grp]
                trs.append(RemoteDMATransfer(dst_ids=[dst(topo, T.cores[r]) for r in grp], dma_engine_mask=sum(1 << k for k in eng),
                                             remote_sem=T.sem["arr%d" % t], srcs=[ap(T, src)], dsts=[T.Y[:, a:a + S] for a in at]))
            g.remote_dma_fused(trs, local_sem=T.sem.sent)
            total["sent"] = total.get("sent", 0) + len(he) + len(fe) + len(ne)
            done[i] = ("sent", total["sent"])
        elif o["kind"] == "d":
            s = "d%d" % nd[0]
            nd[0] += 1
            out, src = o["calls"][0][1]
            q[e].dma_start(ap(T, out), ap(T, src)).then_inc(T.sem[s], 16)
            total[s] = 16
            done[i] = (s, 16)
        else:
            s = csem[e]
            for (nm, args, kw) in o["calls"]:
                a = [ap(T, x) for x in args]
                k = {u: ap(T, x) for u, x in kw.items()}
                if nm == "matmul":
                    ins = g.tensor.matmul(*a)
                elif nm == "activation":
                    ins = g.scalar.activation(*a, **k)
                elif nm == "iota":
                    ins = g.iota(*a, **k)
                elif nm == "affine_select":
                    ins = g.affine_select(*a)
                elif nm == "tensor_copy":
                    ins = g.vector.tensor_copy(*a)
                elif nm == "tensor_tensor":
                    ins = g.vector.tensor_tensor(*a)
                elif nm == "tensor_scalar":
                    ins = g.vector.tensor_scalar(*a)
                elif nm == "tensor_tensor_scan":
                    ins = g.vector.tensor_tensor_scan(*a)
                elif nm == "memset":
                    ins = g.vector.memset(*a)
                else:
                    ins = g.vector.transpose(*a)
                ins.then_inc(T.sem[s], 1)
                total[s] = total.get(s, 0) + 1
            done[i] = (s, total[s])
    for s in sorted(total):
        wait("g", s, total[s])
